import numpy as np, ml_dtypes
CORES = [2,3,42,43,82,83,122,123]
N = 8
import mx_ref
BF = ml_dtypes.bfloat16
def gcols(t, e):
    v = np.concatenate([t.reshape(8, 16, -1, 4), np.zeros((8, 16, 1, 4), BF)], axis=2)
    return np.ascontiguousarray(np.stack([v[g][:, e[g]] for g in range(8)])).reshape(128, -1)
def tile(rs):
    return np.stack(rs, axis=2).reshape(128, -1).astype(BF)
def cut(t, i, w=512):
    return t[:, w * i:w * i + w]
def pick(q, e):
    c = np.concatenate([q[0].reshape(128, -1, 4), np.zeros((128, 1, 4), np.uint8)], axis=1); s = np.concatenate([q[1], np.ones((16, 1), np.uint8)], axis=1)
    return (np.ascontiguousarray(c[:, e].reshape(128, -1)), np.ascontiguousarray(s[:, e]))
def join(*qs):
    return (np.concatenate([q[0] for q in qs], axis=1), np.concatenate([q[1] for q in qs], axis=1))
def put(q, e, v):
    c, s = q[0].reshape(128, -1, 4).copy(), q[1].copy(); c[:, e] = v[0].reshape(128, -1, 4); s[:, e] = v[1]
    return (c.reshape(128, -1), s)
def pk(c, s):
    return (np.ascontiguousarray(c), mx_ref.live(s))
def emit(q):
    return q[0], q[1]
def packed(v, rng):
    q = [mx_ref.quantize(np.ascontiguousarray(v[r])) for r in range(N)]
    return np.stack([a for a, b in q]), np.stack([mx_ref.plane(b, rng) for a, b in q])
def values_of_codes():
    e, c = np.zeros((128, 128, 4), np.float32), np.zeros((128, 2, 4), np.uint8)
    e[np.arange(128), np.arange(128), 0] = 1
    c[:127, :, 0] = np.arange(256).reshape(2, 128).T[:127]
    return mx_ref.matmul(mx_ref.quantize(e.reshape(128, 512).astype(BF)), (c.reshape(128, 8), np.full((16, 2), 127, np.uint8))).T.reshape(-1).astype(np.float64)
CODE_VALUE, SCALE_VALUE = values_of_codes(), 2.0 ** (np.arange(256) - 127.0)
def decode(q):
    return (CODE_VALUE[q[0]].reshape(16, 8, -1, 4) * SCALE_VALUE[q[1]][:, None, :, None] + 0.0).reshape(128, -1).astype(np.float32)
def f(rng, *shape):
    return mx_ref.flush((rng.standard_normal(shape, dtype=np.float32) * np.exp2(rng.integers(-2, 3, shape[:-1] + (1,)))).astype(BF))
def wide(rng, *shape, cols=0):
    v = rng.standard_normal(shape, dtype=np.float32) * np.exp2(rng.integers(-12, 13, shape)).astype(np.float32)
    if cols: v *= np.repeat(np.exp2(rng.integers(-cols, cols + 1, shape[:-2] + (1, shape[-1] // 4))) * (rng.random(shape[:-2] + (1, shape[-1] // 4)) > 0.0625), 4, axis=-1).astype(np.float32)
    return mx_ref.flush(v.astype(BF))
C, T, R = 512, 64, 2
def match(o):
    m, stack, closes = np.full(C, -1), [], []
    for j in range(C):
        if o[j]:
            stack.append(j)
        elif stack:
            i = stack.pop()
            m[i], m[j] = j, i
        else:
            closes.append(j)
    return m, np.array(stack[::-1], int)[:T], np.array(closes, int)[:T]
def big(v, k):
    v = v.astype(np.float32) * np.float32(k)
    v[np.abs(v) < np.float32(2.0 ** -16)] = 0
    return v.astype(BF)
def same(v):
    return np.stack([v] * N)
def weights(rng, h=-1):
    w = big(f(rng, 128, 2048), 0.25)
    if h >= 0:
        w = w.reshape(128, 4, 128, 4)
        w[:, :, 16 * h:16 * h + 8] = 0
        p = np.arange(16 * h, 16 * h + 8)
        for b in range(2): w[p + 8, b, p, b] = 16
        w = w.reshape(128, 2048)
    c, s = packed(same(w), rng)
    return {"wc": c, "ws": s}
def numbers_of(rng):
    return {"x": big(f(rng, N, 128, 4 * C), 1), "u": same(np.array(f(rng, 128, 512))), "v": np.array(f(rng, N, 128, 512))}
def plant(rng, h, first, then, size=np.ones(8), less=(False, False)):
    d = {**numbers_of(rng), **weights(rng, h)}
    x = d["x"].reshape(N, 128, C, 4)
    x[:, 16 * h:16 * h + 16] = 0
    for t, s in enumerate((first, then)):
        p = 16 * h + 8 * t
        x[:, p:p + 8, :, 0] = (np.where(less[t], -1.25 * s, s) + 0.0).astype(np.float32).astype(BF)
        x[:, p:p + 8, :, 1] = np.roll(np.where(less[t], 1.125 * s, 0.0), 1, axis=1).astype(np.float32).astype(BF)
    d["x"] = x.reshape(N, 128, 4 * C)
    for g in range(8):
        d["u"][:, :, 64 * g:64 * g + 4] = 0
        d["u"][:, 16 * h + g, 64 * g] = float(size[g])
        d["u"][:, 16 * h + (g + 1) % 8, 64 * g + 1] = 1.125 * float(size[g])
    return d
def half(rng, n, b):
    v = rng.permutation(np.repeat([1.0, -1.0], [n + b, n]))
    if n + b == 0: return v
    return np.roll(v, -1 - int(np.argmin(np.cumsum(v))))
def word(rng, a, b):
    n = (C - a - b) // 2
    m = int(rng.integers(0, n + 1))
    return np.concatenate([-half(rng, m, a)[::-1], half(rng, n - m, b)])
def brackets(rng, a, b):
    return np.stack([np.stack([word(rng, int(a[r, g]), int(b[r, g])) for g in range(8)]) for r in range(N)])
def setup_inputs(rng):
    return {**numbers_of(rng), **weights(rng)}
def setup_inputs_zeros(rng):
    h = int(rng.integers(0, 8))
    size = np.exp2(rng.integers(-30, 1, (N, 1, C)))
    first, then = [rng.choice([-1.0, -1.0, 0.0, 1.0], (N, 8, C)) for t in range(2)]
    first[:, h] = rng.integers(0, 2, (N, C))
    less = rng.random((2, N, 8, C)) < 0.5
    return plant(rng, h, first * size, then * size, np.exp2(rng.permutation(np.repeat([-30.0, -12.0, 12.0], [4, 2, 2]))), less)
def counts(rng):
    e = rng.permutation(8) % 2 == 0
    a, b = [np.where(e, rng.choice([0, T, T + 2, 2 * T], (N, 8)), rng.choice([T - 1, T + 1], (N, 8))) for i in range(2)]
    g = np.arange(8)
    i = rng.integers(0, N - 1, 8)
    j = (i + 1) % (N - 1)
    b[i, g] = np.where(e, T, T + 1)
    a[i + 1, g] = np.where(e, T, T + 1)
    b[j, g] = np.where(e, 2 * T, T - 1)
    a[j + 1, g] = np.where(e, 2 * T, T + 1)
    return a, b
def setup_inputs_cap(rng):
    h = int(rng.integers(0, 8))
    first, then = brackets(rng, *counts(rng)), brackets(rng, *counts(rng))
    first[:, h] = 1
    return plant(rng, h, first, then)
def setup_inputs_nest(rng):
    h = int(rng.integers(0, 8))
    n = np.arange(C)
    s = np.stack([np.ones(C), -np.ones(C), np.where(n < C // 2, 1.0, -1.0), np.where(n < C // 2, -1.0, 1.0), 1.0 - 2 * (n % 2), 2.0 * (n % 2) - 1,
                  np.where(n < 7 * C // 8, 1.0, -1.0), np.where(n < C - 1, 1.0, -1.0)] + [np.where((n >= c) & (n < (c + C) // 2), 1.0, -1.0) for c in (3 * C // 4, C - 4, C - 2)])
    o = []
    for t in range(2):
        k = np.zeros((N, 8), int)
        lead = rng.permutation(8) % 3 if N < 8 else np.zeros(8, int)
        deep = rng.permutation(np.repeat([8, 9, 10], [4, 2, 2]))
        for g in range(8):
            pairs = [[0, 1], [2, 3], [7, int(rng.integers(4, 6))]]
            l = int(lead[g])
            e = pairs[l] + [6, int(deep[g])] + pairs[(l + 1) % 3] + pairs[(l + 2) % 3]
            k[(int(rng.integers(0, N - 1)) + np.arange(N)) % N, g] = np.resize(e, N)
        o.append(s[k])
    o[0][:, h] = 1
    return plant(rng, h, *o)
def setup_inputs_turns(rng):
    h = int(rng.integers(0, 8))
    e = rng.permutation(8) % 2 == 0
    a, b = [rng.choice([T, 2 * T], (N, 8)) for i in range(2)]
    first, then = brackets(rng, np.where(e, a, 0), np.where(e, b, 0)), brackets(rng, np.where(e, 0, a), np.where(e, 0, b))
    first[:, h] = 1
    return plant(rng, h, first, then)
def setup_inputs_spread(rng):
    d = setup_inputs(rng)
    d["x"] = big(wide(rng, N, 128, 4 * C, cols=6), 1)
    return d
def check_inputs(d):
    b = []
    for k in ("x", "u", "v"):
        a = np.abs(d[k].astype(np.float32))
        if not (np.isfinite(a).all() and ((a == 0) | (a >= 2.0 ** -30) & (a <= 2.0 ** 30)).all()): b.append("a value of " + k)
    if (d["u"].astype(np.float32) != d["u"][:1].astype(np.float32)).any(): b.append("u differs between ranks")
    if (d["wc"] != d["wc"][:1]).any(): b.append("wc differs between ranks")
    s = [mx_ref.live(p) for p in d["ws"]]
    if any((p != s[0]).any() for p in s): b.append("ws differs between ranks")
    c = d["wc"] & 127
    if (c == 127).any(): b.append("a code of wc")
    zero, low, high = [emit(mx_ref.quantize(np.full((128, 16), k).astype(BF)))[1].astype(int) for k in (0.0, 2.0 ** -30, 2.0 ** 30)]
    full = (c.reshape(N, 16, 8, 512, 4) != 0).any(axis=(2, 4))
    l = np.stack(s).astype(int)
    if (((l < np.min(low)) | (l > np.max(high))) & (full | (l != zero[0, 0]))).any(): b.append("a scale of ws")
    return b
def reference(x, u, v, wc, ws):
    w = pk(wc[0], ws[0])
    w = [pick(w, np.arange(128 * b, 128 * b + 128)) for b in range(4)]
    qu = mx_ref.quantize(np.ascontiguousarray(u[0]))
    a = [mx_ref.quantize(np.ascontiguousarray(x[r])) for r in range(N)]
    none = np.zeros((128, 4 * T), BF)
    for t in range(R):
        p, get, mo, mc = [], [], [], []
        for r in range(N):
            s = mx_ref.matmul(qu, a[r])[::16]
            p.append(tile([mx_ref.matmul(w[b], a[r]) * np.float32(0.0625) for b in range(4)]))
            e, o, c = np.full((8, C), -1), np.full((8, T), -1), np.full((8, T), -1)
            for g in range(8):
                e[g], opens, closes = match(s[g] >= 0)
                o[g, :len(opens)] = opens
                c[g, :len(closes)] = closes
                e[g, closes] = C + np.arange(len(closes))
                e[g, opens] = C + T + np.arange(len(opens))
            get.append(e)
            mo.append(mx_ref.quantize(gcols(p[r], o)))
            mc.append(mx_ref.quantize(gcols(p[r], c)))
        d = decode(join(*mo, *mc)).astype(BF)
        for r in range(N):
            left = cut(d, r - 1, 4 * T) if r > 0 else none
            right = cut(d, N + r + 1, 4 * T) if r < N - 1 else none
            z = gcols(np.concatenate([p[r], left, right], axis=1), get[r])
            a[r] = mx_ref.quantize((p[r].astype(np.float32) + z.astype(np.float32)).astype(BF))
    y, oc, osc = np.zeros((N, 128, C), np.float32), np.zeros((N, 128, 4 * C), np.uint8), np.zeros((N, 16, C), np.uint8)
    for r in range(N):
        y[r] = mx_ref.matmul(mx_ref.quantize(np.ascontiguousarray(v[r])), a[r])
        oc[r], osc[r] = emit(a[r])
    return {"y": y, "oc": oc, "osc": osc}

@@ -1,0 +1,399 @@
+import math
+from concourse.bass import DstId, RemoteDMATransfer
+from concourse.mybir import dt, AluOpType, AxisListType, ActivationFunctionType
+
+C, TM, R = 512, 64, 2
+P0 = 16
+D0 = P0 + C
+PL = D0 + 4 * TM
+ZV = -(256.0 + P0)
+S = 1280
+BASE = S // 2 + 16
+CC = 10 * S + BASE
+CO = 12 * S - S // 2 + BASE
+TAB = CO + S // 2
+BETA = 1.0 / 32
+BIG = 1024.0
+HOLD, FREE = 1280.0, 2064.0
+PARTS = (((0, 256), (256, C)), ((0, 384), (384, C)), ((0, 384), (384, C)))
+F4, U8 = "float8_e4m3fn_x4", "uint8"
+
+
+def _sb(n, t):
+    return ("sbuf", [128, n], t)
+
+
+SCRATCH = {
+    "xt": _sb(4 * C, "bfloat16"), "ut": _sb(512, "bfloat16"), "vt": _sb(512, "bfloat16"),
+    "uq": _sb(128, F4), "us": _sb(128, U8), "uq2": _sb(128, F4), "us2": _sb(128, U8),
+    "vq": _sb(128, F4), "vs": _sb(128, U8), "wq": _sb(512, F4), "wsc": _sb(512, U8),
+    "et": _sb(2048, "bfloat16"), "eq": _sb(512, F4), "es": _sb(512, U8),
+    "zt": _sb(512, "bfloat16"), "zq": _sb(128, F4), "zs": _sb(128, U8), "ones": _sb(512, "bfloat16"),
+    "ui": _sb(8, "int32"), "ul": _sb(8, "uint16"),
+    "i80": _sb(80, "int32"), "i80b": _sb(80, "int32"), "e80": _sb(80, "float32"),
+    "pi": _sb(8, "int32"), "cst": _sb(32, "float32"), "p16": _sb(64, "float32"), "w64": _sb(128, "float32"),
+    "jf": _sb(C, "float32"), "jh": _sb(C, "float32"), "jr": _sb(C, "float32"), "flo": _sb(C, "float16"),
+    "jw": _sb(64, "int32"), "jm": _sb(64, "int32"), "gi": _sb(9 * 64, "int32"), "prm": _sb(4, "uint16"),
+    "c2": _sb(2 * C, "float16"),
+    "wrp": _sb(C, "float16"), "val": _sb(C, "bfloat16"), "tab": _sb(TAB, "bfloat16"),
+    "sg": _sb(C, "bfloat16"), "y2": _sb(2 * C, "float16"), "t2": _sb(2 * C, "float16"), "r2": _sb(2 * C, "float16"),
+    "k": _sb(32 * 20, "float32"), "pm": _sb(64, "float32"), "key": _sb(128, "float32"), "kt": _sb(96, "float32"),
+    "ow": _sb(64, "uint16"), "lst": _sb(32, "uint16"), "lst2": _sb(32, "uint16"), "ml": _sb(8, "uint16"),
+    "mw": _sb(128, "float16"), "gp": _sb(C, "bfloat16"), "gw": _sb(C, "float16"),
+    "pw": _sb(4 * PL, "bfloat16"), "pc": _sb(4 * C, "bfloat16"), "x0": _sb(2 * PL, "bfloat16"),
+    "mt": _sb(512, "bfloat16"), "xn": _sb(4 * C, "bfloat16"), "ysb": _sb(C, "float32"),
+    "pss": ("psum", [128, 1024], "float32"), "psp": ("psum", [128, 2048], "float32"), "psy": ("psum", [128, 1024], "float32"),
+}
+for _t in range(R + 1):
+    SCRATCH["aq%d" % _t] = _sb(C, F4)
+    SCRATCH["as%d" % _t] = _sb(C, U8)
+for _t in range(R):
+    for _n in ("m", "l"):
+        SCRATCH["%sq%d" % (_n, _t)] = _sb(128, F4)
+        SCRATCH["%ss%d" % (_n, _t)] = _sb(128, U8)
+
+NDMA = 24
+SEMAPHORES = ["v", "a", "t", "p", "sent"] + ["arr%d" % _t for _t in range(R)] + ["d%d" % _i for _i in range(NDMA)]
+
+
+def rank_program(g, core, T, topo):
+    rank = T.rank_of(core)
+    if rank is None:
+        return
+    A, AF = AluOpType, ActivationFunctionType
+    n_ranks = len(T.cores)
+    Q = {"v": g.vector, "a": g.scalar, "t": g.tensor, "p": g, "s": g.sync}
+    count = {"v": 0, "a": 0, "t": 0, "p": 0}
+    seen = {q: {} for q in Q}
+    wrote, readers = {}, {}
+    ndma = [0]
+
+    def wait(q, sem, n):
+        if seen[q].get(sem, 0) < n:
+            Q[q].wait_ge(T.sem[sem], n)
+            seen[q][sem] = n
+
+    def order(q, r, w):
+        need = {}
+        for name in r:
+            if name in wrote:
+                s, n = wrote[name]
+                need[s] = max(need.get(s, 0), n)
+        for name in w:
+            for s, n in readers.get(name, []) + ([wrote[name]] if name in wrote else []):
+                need[s] = max(need.get(s, 0), n)
+        for s, n in need.items():
+            wait(q, s, n)
+
+    def note(tok, r, w):
+        for name in r:
+            readers.setdefault(name, []).append(tok)
+        for name in w:
+            wrote[name] = tok
+            readers[name] = []
+
+    def op(q, r, w, name, *args, **kw):
+        order(q, r, w)
+        e = Q[q]
+        calls = {
+            "ts": lambda: e.tensor_scalar(*args), "tt": lambda: e.tensor_tensor(*args), "cp": lambda: e.tensor_copy(*args),
+            "ms": lambda: e.memset(*args), "sc": lambda: e.tensor_tensor_scan(*args), "tr": lambda: e.transpose(*args),
+            "rd": lambda: e.tensor_reduce(*args), "qz": lambda: e.quantize_mx(*args), "ac": lambda: e.activation(*args, **kw),
+            "mm": lambda: e.matmul_mx(*args), "io": lambda: e.iota(*args, **kw), "as": lambda: e.affine_select(*args),
+        }
+        count[q] += 1
+        calls[name]().then_inc(T.sem[q], 1)
+        note((q, count[q]), r, w)
+
+    def dma(q, r, w, out, in_):
+        order(q, r, w)
+        s = "d%d" % ndma[0]
+        ndma[0] += 1
+        Q[q].dma_start(out, in_).then_inc(T.sem[s], 16)
+        note((s, 16), r, w)
+
+    def V(r, w, name, *args):
+        op("v", r, w, name, *args)
+
+    def lin(r, w, out, in_, scale, bias):
+        op("a", r, w, "ac", out, in_, AF.Identity, bias=bias, scale=scale)
+
+    def iota(w, *args):
+        op("p", [], w, "io", *args, allow_small_or_imprecise_dtypes=True)
+
+    def bytes_of(view):
+        return view.bitcast(dt.uint8)
+
+    nb = []
+    if rank > 0:
+        nb.append((T.cores[rank - 1], 0, TM))
+    if rank < n_ranks - 1:
+        nb.append((T.cores[rank + 1], TM, 0))
+    edge = len(nb) < 2
+
+    col = lambda i: T.cst[:, i:i + 1]
+    K = lambda i: T.k[:, 32 * i:32 * i + 32]
+    M1, PW, C1, MG, OFF, INI, CV, I32, I16, X0, X1, X2, X3, X4, X5, PA, PB, PC, PD = range(19)
+    JH, J16 = 18, 19
+
+    dma("s", [], ["ut"], T.ut[:], T.u[:])
+    for h, (c0, c1) in enumerate(PARTS[0]):
+        dma("as"[h], [], ["xt%d" % h], T.xt[:, 4 * c0:4 * c1], T.x[:, 4 * c0:4 * c1])
+    dma("s", [], ["wq"], bytes_of(T.wq[:]), T.wc[:])
+    dma("s", [], ["wsc"], T.wsc[:], T.ws[:])
+    dma("s", [], ["vt"], T.vt[:], T.v[:])
+
+    op("p", [], ["i80"], "io", T.i80[:], [[1, 80]], 128, -1)
+    op("p", [], ["pi"], "io", T.pi[:, 0:1], [[0, 1]], 0, 1)
+    iota(["jf"], T.jf[:], [[1, C]], 0, 0)
+    op("p", [], ["jwa"], "io", T.jw[:, 0:32], [[32, 16], [0, 2]], 0, 0)
+    op("p", [], ["ui"], "io", T.ui[:], [[16, 8]], 0, 0)
+    if edge:
+        iota(["zt"], T.zt[:], [[0, 512]], 0, 0)
+    iota(["val"], T.val[:], [[1, C]], -256, 0)
+    for i, (c1, v0) in enumerate(((CC - S // 2, 256), (CO + S // 2, 256 + 2 * TM))):
+        iota(["tabv%d" % (2 * i)], T.tab[:, c1 - C:c1 - TM], [[0, C - TM]], int(ZV), 0)
+        iota(["tabv%d" % (2 * i + 1)], T.tab[:, c1 - TM:c1], [[-2, TM]], v0 + 2 * (TM - 1), 0)
+    op("p", [], ["jwc"], "io", T.jw[:, 32:64], [[16, 32]], P0, 0)
+    iota(["ones"], T.ones[:], [[0, 512]], 1, 0)
+    for b in range(4):
+        op("p", ["ones"], ["et%d" % b], "as", T.et[:, 512 * b:512 * b + 512], T.ones[:], [[-1, 512]], A.is_equal, 0.0, b, 4)
+    V([], ["p2"], "ms", T.p16[:, 0:16], 2.0)
+    V([], ["p0"], "ms", T.p16[:, 16:32], 0.0)
+    op("a", ["p0"], ["pm"], "ac", T.pm[:, 0:16], T.p16[:, 16:32], AF.Exp)
+    V([], ["cx"], "ms", T.c2[:], BIG)
+    V(["p2", "p0"], ["pp"], "sc", T.p16[:, 32:48], T.p16[:, 0:16], T.p16[:, 16:32], 0.5, A.mult, A.add)
+    V(["i80"], ["i80b"], "ts", T.i80b[:], T.i80[:], 15, None, A.bitwise_and)
+    V(["pi"], ["pr"], "ts", T.pi[:, 1:2], T.pi[:, 0:1], 31, None, A.bitwise_and)
+    V(["i80b"], ["e80"], "ts", T.e80[:], T.i80b[:], 0.0, None, A.is_equal)
+    V(["pr"], ["i32"], "cp", col(I32), T.pi[:, 1:2])
+    V(["cx"], ["c9f"], "ms", T.c2[:, 9:C:16], -(0.5 + 10 * BETA))
+    V(["e80", "pp"], ["pe"], "tt", T.p16[:, 48:64], T.p16[:, 32:48], T.e80[:, 0:16], A.mult)
+    V(["cx"], ["c9b"], "ms", T.c2[:, C + 9:2 * C:16], -(0.5 + 11.5 * BETA))
+    V(["pe"], ["pw0"], "rd", col(X0), T.p16[:, 48:64], AxisListType.X, A.add)
+    V(["pi"], ["ph"], "ts", T.pi[:, 2:3], T.pi[:, 0:1], 4, 1, A.logical_shift_right, A.bitwise_and)
+    V(["pw0"], ["pwc"], "ts", col(PW), col(X0), float(C), None, A.min)
+    V(["pi"], ["pa"], "ts", T.pi[:, 3:4], T.pi[:, 0:1], 14, None, A.bitwise_and)
+    V(["pi"], ["pb"], "ts", T.pi[:, 4:5], T.pi[:, 0:1], 1, None, A.bitwise_and)
+    V(["ph"], ["m1"], "cp", col(M1), T.pi[:, 2:3])
+    lin(["pwc"], ["c1"], col(C1), col(PW), -0.25, 0.25)
+    lin(["pwc"], ["mg"], col(MG), col(PW), 1.5 * 2.0 ** 22, 0.0)
+    lin(["jf", "c1"], ["jh"], T.jh[:], T.jf[:], 0.5, col(C1))
+    lin(["e80"], ["off"], col(OFF), T.e80[:, 10:11], -1001.0, 1.0)
+    lin(["jh", "mg"], ["jr"], T.jr[:], T.jh[:], 1.0, col(MG))
+    lin(["e80"], ["ini"], col(INI), T.e80[:, 10:11], 300.0, 0.0)
+    V(["i32", "jwa"], ["j1"], "ts", T.jm[:, 0:32], T.jw[:, 0:32], col(I32), None, A.add)
+    V(["pb", "m1"], ["x1"], "ts", col(X1), T.pi[:, 4:5], col(M1), None, A.not_equal)
+    V(["pa", "m1"], ["x3"], "ts", col(X3), T.pi[:, 3:4], col(M1), None, A.add)
+    V(["j1"], ["j2"], "ts", T.jm[:, 32:64], T.jm[:, 0:32], -1.0, float(C - 1), A.mult, A.add)
+    V(["ui"], ["ul"], "cp", T.ul[:], T.ui[:])
+    V(["ut"], ["uq"], "qz", T.uq[:], T.us[:], T.ut[:])
+    lin(["m1"], ["x2"], col(X2), col(M1), 32.0, 64.0)
+    lin(["m1"], ["x4"], col(X4), col(M1), -32.0, 64.0)
+    lin(["x3"], ["x5"], col(X5), col(X3), 1.0, 32.0)
+    lin(["x1", "x2", "x3"], ["pA"], col(PA), col(X1), col(X2), col(X3))
+    lin(["x1", "x4", "x5"], ["pC"], col(PC), col(X1), col(X4), col(X5))
+    lin(["pA"], ["pB"], col(PB), col(PA), 1.0, 16.0)
+    lin(["pC"], ["pD"], col(PD), col(PC), 1.0, 16.0)
+    lin(["e80"], ["wa"], T.w64[:, 0:64], T.e80[:, 0:64], -HOLD, 0.0)
+    lin(["e80"], ["wb"], T.w64[:, 64:128], T.e80[:, 1:65], FREE, 0.0)
+    lin(["e80"], ["cv"], col(CV), T.e80[:, 0:1], -FREE, HOLD - ZV)
+    for b in range(4):
+        lin(["p0"], ["pz%d" % b], T.pw[:, b * PL:b * PL + P0], T.p16[:, 16:32], 1.0, 0.0)
+    G = lambda u: T.gi[:, 64 * u:64 * u + 64]
+    for u in range(9):
+        V(["j1", "j2"], ["g%d" % u], "ts", G(u), T.jm[:], 1 << u, None, A.bitwise_and)
+        if u == 1:
+            V(["uq", "ul"], ["uq2"], "cp", T.uq2[:].bitcast(dt.uint32), T.uq[:].bitcast(dt.uint32).indirect(T.ul[:]))
+            V(["uq", "ul"], ["us2"], "cp", T.us2[:], T.us[:].indirect(T.ul[:]))
+    V(["jr", "mg", "off"], ["flo"], "ts", T.flo[:], T.jr[:], col(MG), col(OFF), A.subtract, A.add)
+    for u in range(4):
+        V(["g%d" % u, "cx"], ["c%d" % u], "ts", T.c2[:, u:2 * C:16], G(u), -0.5, BETA, A.mult, A.add)
+    for h, (c0, c1) in enumerate(PARTS[0]):
+        V(["xt%d" % h], ["a0h%d" % h], "qz", T.aq0[:, c0:c1], T.as0[:, c0:c1], T.xt[:, 4 * c0:4 * c1])
+    for u in range(4, 8):
+        V(["g%d" % u, "cx"], ["c%d" % u], "ts", T.c2[:, u:2 * C:16], G(u), -0.5, BETA, A.mult, A.add)
+    V(["g8", "cx"], ["c8f"], "ts", T.c2[:, 8:C:16], T.gi[:, 512:544], -0.5, 2 * BETA, A.mult, A.add)
+    V(["g8", "cx"], ["c8b"], "ts", T.c2[:, C + 8:2 * C:16], T.gi[:, 544:576], -0.5, 4 * BETA, A.mult, A.add)
+    cn = ["c%d" % u for u in range(8)] + ["c8f", "c8b", "c9f", "c9b"]
+    V(["j1"], ["jhalf"], "ts", K(JH), T.jm[:, 0:32], 0.5, None, A.add)
+    if edge:
+        V(["zt"], ["zq"], "qz", T.zq[:], T.zs[:], T.zt[:])
+        z0 = TM - nb[0][1]
+        for t in range(R):
+            dma("s", ["zq"], ["zl%d" % t], bytes_of(T["lq%d" % t][:, z0:z0 + TM]), bytes_of(T.zq[:, 0:TM]))
+            dma("s", ["zq"], ["zm%d" % t], T["ls%d" % t][:, z0:z0 + TM], T.zs[:, 0:TM])
+
+    def masks(c):
+        r = T.rank_of(c)
+        ds = [T.cores[i] for i in (r - 1, r + 1) if 0 <= i < n_ranks]
+        used, out = set(), {}
+        width = min(len(topo.engines(a, b)) for a, b in zip(T.cores, T.cores[1:]))
+        for d in sorted(ds, key=lambda d: len(topo.engines(c, d))):
+            free = [e for e in topo.engines(c, d) if e not in used]
+            if len(ds) > 1 and not used:
+                other = [x for x in ds if x != d][0]
+                if not set(topo.engines(c, other)) - set(free):
+                    free = free[:len(free) // 2]
+            free = free[:min(width, 1 << (len(free).bit_length() - 1))]
+            used.update(free)
+            out[d] = free
+        return out
+
+    mine = masks(core)
+    arrive = sum(2 * len(masks(d)[core]) for d, _, _ in nb)
+    sent = [0]
+    plane = lambda b: T.pw[:, b * PL:(b + 1) * PL]
+    bank = lambda b, n: T.psp[:, 512 * b:512 * b + n]
+    pls = lambda b: ["pw%d" % b, "pz%d" % b, "pd%d" % b]
+    ln2 = math.log(2.0)
+    GA = 10
+
+    def scores(t, h):
+        c0, c1 = PARTS[t][h]
+        op("t", ["a%dh%d" % (t, h), "uq2", "us2"], ["pss%d" % h], "mm", T.pss[:, 512 * h:512 * h + c1 - c0], T.uq2[:], T.us2[:],
+           T["aq%d" % t][:, c0:c1], T["as%d" % t][:, c0:c1], True, True)
+
+    def first_copy(b):
+        op("a", [], ["psp%d" % b, "pw%d" % b], "ac", T.pw[:, b * PL + P0:b * PL + D0], bank(b, C), AF.Copy, scale=0.0625)
+
+    def second_copy(b):
+        op("a", ["pw%d" % b], ["pc%d" % b], "ac", T.pc[:, b * C:(b + 1) * C], T.pw[:, b * PL + P0:b * PL + D0], AF.Copy)
+
+    scores(0, 0)
+    scores(0, 1)
+    for t in range(R):
+        aq, asc = T["aq%d" % t], T["as%d" % t]
+        ah = ["a%dh0" % t, "a%dh1" % t]
+        mq, ms_, lq, ls = T["mq%d" % t], T["ms%d" % t], T["lq%d" % t], T["ls%d" % t]
+        for b in range(4):
+            op("t", ah + ["wq", "wsc"], ["psp%d" % b], "mm", bank(b, C),
+               T.wq[:, 128 * b:128 * b + 128], T.wsc[:, 128 * b:128 * b + 128], aq[:], asc[:], True, True)
+        V([], ["tabc"], "ms", T.tab[:, CC - TM:CC], ZV)
+        V([], ["tabo"], "ms", T.tab[:, CO - TM:CO], ZV)
+        for h, (c0, c1) in enumerate(PARTS[t]):
+            V([], ["pss%d" % h, "sg%d" % h], "ts", T.sg[:, c0:c1], T.pss[:, 512 * h:512 * h + c1 - c0], 0.0, 0.5, A.is_ge, A.subtract)
+        sg = ["sg0", "sg1"]
+        for b in range(3):
+            first_copy(b)
+        V(sg + ["flo", "ini"], ["yf"], "sc", T.y2[:, 0:C], T.flo[:], T.sg[:], col(INI), A.max, A.add)
+        V(sg + ["flo", "ini"], ["yb"], "sc", T.y2[:, 2 * C - 1:C - 1:-1], T.flo[:], T.sg[:, ::-1], col(INI), A.max, A.subtract)
+        V(["yf"], ["tf"], "tr", T.t2[:, 0:C], T.y2[:, 0:C])
+        V(["yb"], ["tb"], "tr", T.t2[:, C:2 * C], T.y2[:, C:2 * C])
+        V(["tf"] + cn, ["rf"], "sc", T.r2[:, 0:C - 6], T.t2[:, 0:C - 6], T.c2[:, 0:C - 6], BIG, A.min, A.add)
+        V(["tb"] + cn, ["rb"], "sc", T.r2[:, C:2 * C - 6], T.t2[:, C:2 * C - 6], T.c2[:, C:2 * C - 6], BIG, A.min, A.add)
+        nf, nbk = T.r2[:, 9:C:16], T.r2[:, C + 9:2 * C:16]
+        V(["tf"], ["hf"], "ts", K(0), T.t2[:, 10:C:16], 2.0, -599.75, A.mult, A.add)
+        V(["rf", "rb"], ["n"], "tt", K(3), nf, nbk, A.min)
+        V(["rf", "rb"], ["o"], "tt", K(4), nbk, nf, A.is_lt)
+        op("a", ["n"], ["e2"], "ac", T.pm[:, 32:64], K(3), AF.Exp, scale=-ln2 / BETA)
+        op("a", ["n"], ["pm"], "ac", T.pm[:, 0:32], K(3), AF.Exp, bias=math.log(1.5 * 2.0 ** 24), scale=-ln2 / BETA)
+        lin(["n"], ["b0"], K(6), K(3), -S / BETA, float(BASE))
+        lin(["o"], ["d2"], K(8), K(4), float(S), -S / 2.0)
+        first_copy(3)
+        second_copy(0)
+        second_copy(1)
+        V(["tb"], ["hb"], "ts", K(1), T.t2[:, C + 10:2 * C:16], 2.0, -599.75, A.mult, A.add)
+        V(["hf", "o"], ["l1"], "tt", K(7), K(0), K(4), A.subtract)
+        V(["n"], ["f9"], "ts", K(5), K(3), -11 * BETA, None, A.is_le)
+        V(["hb", "l1"], ["df"], "tt", K(2), K(1), K(7), A.subtract)
+        if t == 0:
+            V(["pA", "pB", "pC", "pD"], ["prm"], "cp", T.prm[:], T.cst[:, PA:PD + 1])
+        V(["df", "f9"], ["gg"], "tt", K(10), K(2), K(5), A.mult)
+        V(["e2", "jhalf"], ["x"], "tt", K(13), K(JH), T.pm[:, 32:64], A.subtract)
+        V(["l1", "gg"], ["l"], "tt", K(9), K(7), K(10), A.add)
+        V(["x", "pm"], ["t2"], "tt", K(14), K(13), T.pm[:, 0:32], A.add)
+        V(["l", "pm"], ["tq"], "tt", K(11), K(9), T.pm[:, 0:32], A.add)
+        V(["l", "b0"], ["lb"], "tt", K(12), K(9), K(6), A.add)
+        V(["tq", "t2"], ["q"], "tt", K(15), K(14), K(11), A.subtract)
+        V(["lb", "d2"], ["lb2"], "tt", K(16), K(12), K(8), A.add)
+        V(["lb", "q"], ["of"], "tt", T.key[:, 0:32], K(12), K(15), A.add)
+        V(["lb2", "q"], ["wf"], "tt", T.key[:, 32:64], K(16), K(15), A.add)
+        V(["of"], ["kt1"], "tr", T.kt[:, 64:96], T.key[:, 0:32])
+        V(["of", "wf"], ["kt0"], "tr", T.kt[:, 0:64], T.key[:, 0:64])
+        if t == 0:
+            V(["wa", "wb"], ["wrp0"], "tt", T.wrp[:, 0:64], T.w64[:, 0:64], T.w64[:, 64:128], A.add)
+        V(["kt0", "kt1"], ["rot"], "tr", T.key[:, 64:128], T.kt[:, 16:80])
+        V(["of", "wf", "rot", "prm"], ["ow"], "cp", T.ow[:], T.key[:].indirect(T.prm[:]))
+        tabs = ["tabc", "tabo"] + ["tabv%d" % i for i in range(4)]
+        V(["ow", "val"], tabs, "cp", T.tab[:].indirect(T.ow[:, 0:32]), T.val[:])
+        op("a", tabs + ["ow"], ["gpa"], "ac", T.gp[:, 0:16 * GA], T.tab[:].indirect(T.ow[:, 32:32 + GA]), AF.Copy)
+        V(tabs + ["wrp0"], ["mw0"], "sc", T.mw[:, 0:TM], T.tab[:, CC - 1:CC - TM - 1:-1], T.wrp[:, 0:TM], FREE, A.min, A.add)
+        V(tabs + ["wrp0"], ["mw1"], "sc", T.mw[:, TM:2 * TM], T.tab[:, CO - 1:CO - TM - 1:-1], T.wrp[:, 0:TM], FREE, A.min, A.add)
+        V(["mw0", "mw1", "cv"], ["ml"], "ts", T.ml[:], T.mw[:, 15:128:16], col(CV), None, A.add)
+        for b in (2, 3):
+            op("a", ["ml"] + pls(b), ["mt%d" % b], "ac", T.mt[:, b:512:4], plane(b).indirect(T.ml[:]), AF.Copy)
+        for b in (0, 1):
+            V(["ml"] + pls(b), ["mt%d" % b], "cp", T.mt[:, b:512:4], plane(b).indirect(T.ml[:]))
+        V(["mt%d" % b for b in range(4)], ["mq%d" % t], "qz", mq[:], ms_[:], T.mt[:])
+        order("p", ["mq%d" % t], [])
+        for src, dst, cast in ((mq, lq, bytes_of), (ms_, ls, lambda v: v)):
+            trs = []
+            for d, c0, c1 in nb:
+                rid, pid, _ = topo.addr(d)
+                trs.append(RemoteDMATransfer(dst_ids=[DstId(rid=rid, pnc=pid)], dma_engine_mask=sum(1 << e for e in mine[d]),
+                                             remote_sem=T.sem["arr%d" % t], src=cast(src[:, c0:c0 + TM]), dst=cast(dst[:, c1:c1 + TM])))
+                sent[0] += len(mine[d])
+            g.remote_dma_fused(trs, local_sem=T.sem.sent)
+        op("a", tabs + ["ow"], ["gpb"], "ac", T.gp[:, 16 * GA:C], T.tab[:].indirect(T.ow[:, 32 + GA:64]), AF.Copy)
+        second_copy(2)
+        second_copy(3)
+        if t == 0:
+            for i in range(3):
+                w = 64 << i
+                V(["wrp%d" % i], ["wrp%d" % (i + 1)], "cp", T.wrp[:, w:2 * w], T.wrp[:, 0:w])
+                if i < 2:
+                    V([], ["pd%d" % i], "ms", T.pw[:, i * PL + D0:(i + 1) * PL], 0.0)
+            V(["pi"], ["p15"], "ts", T.pi[:, 5:6], T.pi[:, 0:1], 15, None, A.bitwise_and)
+        else:
+            V(["vt"], ["vq"], "qz", T.vq[:], T.vs[:], T.vt[:])
+        V(["gpa", "gpb", "wrp3"], ["gw"], "sc", T.gw[:], T.gp[:], T.wrp[:], FREE, A.min, A.add)
+        if t == 0:
+            V(["p15"], ["i16"], "cp", col(I16), T.pi[:, 5:6])
+        V(["gw", "cv"], ["lst"], "ts", T.lst[:], T.gw[:, 15:C:16], col(CV), None, A.add)
+        V(["gw", "cv"], ["lc"], "ts", K(0), T.gw[:, 15:C:16], col(CV), None, A.add)
+        V(["gw", "cv"], ["lf"], "ts", K(1), T.gw[:, 15:C:16], col(CV), float(D0), A.add, A.is_ge)
+        if t == 0:
+            V(["i16", "jwc"], ["j16"], "ts", K(J16), T.jw[:, 32:64], col(I16), None, A.add)
+        V(["lst", "pc0"] + pls(0), ["x00"], "tt", T.x0[:, P0:D0], plane(0).indirect(T.lst[:]), T.pc[:, 0:C], A.add)
+        V(["lc", "lf"], ["lg"], "tt", K(2), K(0), K(1), A.mult)
+        if t == 0:
+            V(["et%d" % b for b in range(4)], ["eq"], "qz", T.eq[:], T.es[:], T.et[:])
+        V(["lg", "j16"], ["lh"], "tt", K(5), K(2), K(J16), A.max)
+        V(["lst", "pc1"] + pls(1), ["x01"], "tt", T.x0[:, PL + P0:PL + D0], plane(1).indirect(T.lst[:]), T.pc[:, C:2 * C], A.add)
+        V(["lh"], ["lst2"], "cp", T.lst2[:], K(5))
+        order("t", ["eq", "zl%d" % t, "zm%d" % t], [])
+        wait("t", "arr%d" % t, arrive)
+        for b in (2, 0, 3, 1):
+            op("t", ["eq"], ["psp%d" % b], "mm", bank(b, 128),
+               T.eq[:, 128 * b:128 * b + 128], T.es[:, 128 * b:128 * b + 128], lq[:], ls[:], True, True)
+        for b in (2, 3):
+            op("a", [], ["psp%d" % b, "pd%d" % b], "ac", T.pw[:, b * PL + D0:(b + 1) * PL:2], bank(b, 128), AF.Copy)
+        for b in (0, 1):
+            V(["mt%d" % b], ["psp%d" % b, "fx%d" % b], "tt", T.x0[:, b * PL + D0:(b + 1) * PL:2], T.mt[:, b:512:4], bank(b, 128), A.add)
+        nq, ns = T["aq%d" % (t + 1)], T["as%d" % (t + 1)]
+        for h, (c0, c1) in enumerate(PARTS[t + 1]):
+            for b in (0, 1):
+                op("a", ["lst2", "x0%d" % b, "fx%d" % b], ["xn%d_%d" % (h, b)], "ac", T.xn[:, 4 * c0 + b:4 * c1:4],
+                   T.x0[:, b * PL:(b + 1) * PL].indirect(T.lst2[:, c0 // 16:c1 // 16]), AF.Copy)
+        for h, (c0, c1) in enumerate(PARTS[t + 1]):
+            for b in (2, 3):
+                V(["lst", "pc%d" % b] + pls(b), ["xn%d_%d" % (h, b)], "tt", T.xn[:, 4 * c0 + b:4 * c1:4],
+                  plane(b).indirect(T.lst[:, c0 // 16:c1 // 16]), T.pc[:, b * C + c0:b * C + c1], A.add)
+            names = ["a%dh%d" % (t + 1, h)]
+            V(["xn%d_%d" % (h, b) for b in range(4)], names, "qz", nq[:, c0:c1], ns[:, c0:c1], T.xn[:, 4 * c0:4 * c1])
+            if t < R - 1:
+                scores(t + 1, h)
+            else:
+                dma("s", names, [], T.oc[:, 4 * c0:4 * c1], bytes_of(nq[:, c0:c1]))
+                op("t", names + ["vq"], ["psy%d" % h], "mm", T.psy[:, 512 * h:512 * h + c1 - c0], T.vq[:], T.vs[:], nq[:, c0:c1], ns[:, c0:c1], True, True)
+                op("a", [], ["psy%d" % h, "y%d" % h], "ac", T.ysb[:, c0:c1], T.psy[:, 512 * h:512 * h + c1 - c0], AF.Copy)
+                dma("a", ["y%d" % h], [], T.y[:, c0:c1], T.ysb[:, c0:c1])
+    last = ["a%dh0" % R, "a%dh1" % R]
+    for k in range(4):
+        dma("s", last, [], T.osc[4 * k:4 * k + 4, :], T["as%d" % R][32 * k:32 * k + 4, :])
+    for i in range(ndma[0]):
+        g.sync.wait_ge(T.sem["d%d" % i], 16)
+    for q in count:
+        g.sync.wait_ge(T.sem[q], count[q])
+    g.wait_ge(T.sem.sent, sent[0])

@@ -12,8 +12,9 @@ BASE = S // 2 + 16
 CC = 10 * S + BASE
 CO = 12 * S - S // 2 + BASE
 TAB = CO + S // 2
-BETA = 1.0 / 32
-BIG = 1024.0
+BETA = 1.0 / 16
+BIG = 2048.0
+TINY = 2.0 ** -120
 HOLD, FREE = 1280.0, 2064.0
 PARTS = (((0, 256), (256, C)), ((0, 384), (384, C)), ((0, 384), (384, C)))
 F4, U8 = "float8_e4m3fn_x4", "uint8"
@@ -31,7 +32,7 @@ SCRATCH = {
     "zt": _sb(512, "bfloat16"), "zq": _sb(128, F4), "zs": _sb(128, U8), "ones": _sb(512, "bfloat16"),
     "ui": _sb(8, "int32"), "ul": _sb(8, "uint16"),
     "i80": _sb(80, "int32"), "i80b": _sb(80, "int32"), "e80": _sb(80, "float32"),
-    "pi": _sb(8, "int32"), "cst": _sb(32, "float32"), "p16": _sb(64, "float32"), "w64": _sb(128, "float32"),
+    "pi": _sb(8, "int32"), "cst": _sb(32, "float32"), "w64": _sb(128, "float32"),
     "jf": _sb(C, "float32"), "jh": _sb(C, "float32"), "jr": _sb(C, "float32"), "flo": _sb(C, "float16"),
     "jw": _sb(64, "int32"), "jm": _sb(64, "int32"), "gi": _sb(9 * 64, "int32"), "prm": _sb(4, "uint16"),
     "c2": _sb(2 * C, "float16"),
@@ -98,7 +99,7 @@ def rank_program(g, core, T, topo):
         calls = {
             "ts": lambda: e.tensor_scalar(*args), "tt": lambda: e.tensor_tensor(*args), "cp": lambda: e.tensor_copy(*args),
             "ms": lambda: e.memset(*args), "sc": lambda: e.tensor_tensor_scan(*args), "tr": lambda: e.transpose(*args),
-            "rd": lambda: e.tensor_reduce(*args), "qz": lambda: e.quantize_mx(*args), "ac": lambda: e.activation(*args, **kw),
+            "qz": lambda: e.quantize_mx(*args), "ac": lambda: e.activation(*args, **kw),
             "mm": lambda: e.matmul_mx(*args), "io": lambda: e.iota(*args, **kw), "as": lambda: e.affine_select(*args),
         }
         count[q] += 1
@@ -135,6 +136,7 @@ def rank_program(g, core, T, topo):
     K = lambda i: T.k[:, 32 * i:32 * i + 32]
     M1, PW, C1, MG, OFF, INI, CV, I32, I16, X0, X1, X2, X3, X4, X5, PA, PB, PC, PD = range(19)
     JH, J16 = 18, 19
+    ln2 = math.log(2.0)
 
     dma("s", [], ["ut"], T.ut[:], T.u[:])
     for h, (c0, c1) in enumerate(PARTS[0]):
@@ -143,80 +145,90 @@ def rank_program(g, core, T, topo):
     dma("s", [], ["wsc"], T.wsc[:], T.ws[:])
     dma("s", [], ["vt"], T.vt[:], T.v[:])
 
-    op("p", [], ["i80"], "io", T.i80[:], [[1, 80]], 128, -1)
+    def clear_lists():
+        iota(["tabc"], T.tab[:, CC - TM:CC], [[0, TM]], int(ZV), 0)
+        iota(["tabo"], T.tab[:, CO - TM:CO], [[0, TM]], int(ZV), 0)
+
     op("p", [], ["pi"], "io", T.pi[:, 0:1], [[0, 1]], 0, 1)
-    iota(["jf"], T.jf[:], [[1, C]], 0, 0)
     op("p", [], ["jwa"], "io", T.jw[:, 0:32], [[32, 16], [0, 2]], 0, 0)
+    op("p", [], ["i80"], "io", T.i80[:], [[1, 80]], 128, -1)
+    iota(["jf"], T.jf[:], [[1, C]], 0, 0)
     op("p", [], ["ui"], "io", T.ui[:], [[16, 8]], 0, 0)
     if edge:
         iota(["zt"], T.zt[:], [[0, 512]], 0, 0)
     iota(["val"], T.val[:], [[1, C]], -256, 0)
-    for i, (c1, v0) in enumerate(((CC - S // 2, 256), (CO + S // 2, 256 + 2 * TM))):
-        iota(["tabv%d" % (2 * i)], T.tab[:, c1 - C:c1 - TM], [[0, C - TM]], int(ZV), 0)
+    fixed = ((CC - S // 2, 256), (CO + S // 2, 256 + 2 * TM))
+    for i, (c1, v0) in enumerate(fixed):
         iota(["tabv%d" % (2 * i + 1)], T.tab[:, c1 - TM:c1], [[-2, TM]], v0 + 2 * (TM - 1), 0)
+    clear_lists()
     op("p", [], ["jwc"], "io", T.jw[:, 32:64], [[16, 32]], P0, 0)
     iota(["ones"], T.ones[:], [[0, 512]], 1, 0)
     for b in range(4):
         op("p", ["ones"], ["et%d" % b], "as", T.et[:, 512 * b:512 * b + 512], T.ones[:], [[-1, 512]], A.is_equal, 0.0, b, 4)
-    V([], ["p2"], "ms", T.p16[:, 0:16], 2.0)
-    V([], ["p0"], "ms", T.p16[:, 16:32], 0.0)
-    op("a", ["p0"], ["pm"], "ac", T.pm[:, 0:16], T.p16[:, 16:32], AF.Exp)
-    V([], ["cx"], "ms", T.c2[:], BIG)
-    V(["p2", "p0"], ["pp"], "sc", T.p16[:, 32:48], T.p16[:, 0:16], T.p16[:, 16:32], 0.5, A.mult, A.add)
-    V(["i80"], ["i80b"], "ts", T.i80b[:], T.i80[:], 15, None, A.bitwise_and)
+    V([], ["c9f"], "ms", T.c2[:, 9:C:16], -(1.0 + 10 * BETA))
+    V([], ["c9b"], "ms", T.c2[:, C + 9:2 * C:16], -(1.0 + 11.5 * BETA))
+    V(["pi"], ["p15"], "ts", T.pi[:, 5:6], T.pi[:, 0:1], 15, None, A.bitwise_and)
     V(["pi"], ["pr"], "ts", T.pi[:, 1:2], T.pi[:, 0:1], 31, None, A.bitwise_and)
-    V(["i80b"], ["e80"], "ts", T.e80[:], T.i80b[:], 0.0, None, A.is_equal)
+    V(["p15"], ["p9"], "ts", col(X0), T.pi[:, 5:6], 9.0, None, A.min)
+    op("a", ["p9"], ["pwc"], "ac", col(PW), col(X0), AF.Exp, scale=ln2)
     V(["pr"], ["i32"], "cp", col(I32), T.pi[:, 1:2])
-    V(["cx"], ["c9f"], "ms", T.c2[:, 9:C:16], -(0.5 + 10 * BETA))
-    V(["e80", "pp"], ["pe"], "tt", T.p16[:, 48:64], T.p16[:, 32:48], T.e80[:, 0:16], A.mult)
-    V(["cx"], ["c9b"], "ms", T.c2[:, C + 9:2 * C:16], -(0.5 + 11.5 * BETA))
-    V(["pe"], ["pw0"], "rd", col(X0), T.p16[:, 48:64], AxisListType.X, A.add)
+    V(["p15"], ["i16"], "cp", col(I16), T.pi[:, 5:6])
+    V(["i32", "jwa"], ["j1"], "ts", T.jm[:, 0:32], T.jw[:, 0:32], col(I32), None, A.add)
     V(["pi"], ["ph"], "ts", T.pi[:, 2:3], T.pi[:, 0:1], 4, 1, A.logical_shift_right, A.bitwise_and)
-    V(["pw0"], ["pwc"], "ts", col(PW), col(X0), float(C), None, A.min)
+    V(["j1"], ["j2"], "ts", T.jm[:, 32:64], T.jm[:, 0:32], -1.0, float(C - 1), A.mult, A.add)
     V(["pi"], ["pa"], "ts", T.pi[:, 3:4], T.pi[:, 0:1], 14, None, A.bitwise_and)
     V(["pi"], ["pb"], "ts", T.pi[:, 4:5], T.pi[:, 0:1], 1, None, A.bitwise_and)
     V(["ph"], ["m1"], "cp", col(M1), T.pi[:, 2:3])
-    lin(["pwc"], ["c1"], col(C1), col(PW), -0.25, 0.25)
-    lin(["pwc"], ["mg"], col(MG), col(PW), 1.5 * 2.0 ** 22, 0.0)
-    lin(["jf", "c1"], ["jh"], T.jh[:], T.jf[:], 0.5, col(C1))
-    lin(["e80"], ["off"], col(OFF), T.e80[:, 10:11], -1001.0, 1.0)
-    lin(["jh", "mg"], ["jr"], T.jr[:], T.jh[:], 1.0, col(MG))
-    lin(["e80"], ["ini"], col(INI), T.e80[:, 10:11], 300.0, 0.0)
-    V(["i32", "jwa"], ["j1"], "ts", T.jm[:, 0:32], T.jw[:, 0:32], col(I32), None, A.add)
+    V(["i80"], ["i80b"], "ts", T.i80b[:], T.i80[:], 15, None, A.bitwise_and)
     V(["pb", "m1"], ["x1"], "ts", col(X1), T.pi[:, 4:5], col(M1), None, A.not_equal)
+    V(["i80b"], ["e80"], "ts", T.e80[:], T.i80b[:], 0.0, None, A.is_equal)
     V(["pa", "m1"], ["x3"], "ts", col(X3), T.pi[:, 3:4], col(M1), None, A.add)
-    V(["j1"], ["j2"], "ts", T.jm[:, 32:64], T.jm[:, 0:32], -1.0, float(C - 1), A.mult, A.add)
-    V(["ui"], ["ul"], "cp", T.ul[:], T.ui[:])
-    V(["ut"], ["uq"], "qz", T.uq[:], T.us[:], T.ut[:])
+    lin(["pwc"], ["c1"], col(C1), col(PW), -0.5, 0.5)
+    lin(["pwc"], ["mg"], col(MG), col(PW), 1.5 * 2.0 ** 23, 0.0)
+    lin(["e80"], ["off"], col(OFF), T.e80[:, 10:11], -2002.0, 2.0)
+    lin(["jf", "c1"], ["jh"], T.jh[:], T.jf[:], 1.0, col(C1))
     lin(["m1"], ["x2"], col(X2), col(M1), 32.0, 64.0)
-    lin(["m1"], ["x4"], col(X4), col(M1), -32.0, 64.0)
-    lin(["x3"], ["x5"], col(X5), col(X3), 1.0, 32.0)
-    lin(["x1", "x2", "x3"], ["pA"], col(PA), col(X1), col(X2), col(X3))
-    lin(["x1", "x4", "x5"], ["pC"], col(PC), col(X1), col(X4), col(X5))
-    lin(["pA"], ["pB"], col(PB), col(PA), 1.0, 16.0)
-    lin(["pC"], ["pD"], col(PD), col(PC), 1.0, 16.0)
-    lin(["e80"], ["wa"], T.w64[:, 0:64], T.e80[:, 0:64], -HOLD, 0.0)
-    lin(["e80"], ["wb"], T.w64[:, 64:128], T.e80[:, 1:65], FREE, 0.0)
-    lin(["e80"], ["cv"], col(CV), T.e80[:, 0:1], -FREE, HOLD - ZV)
-    for b in range(4):
-        lin(["p0"], ["pz%d" % b], T.pw[:, b * PL:b * PL + P0], T.p16[:, 16:32], 1.0, 0.0)
+    lin(["jh", "mg"], ["jr"], T.jr[:], T.jh[:], 1.0, col(MG))
     G = lambda u: T.gi[:, 64 * u:64 * u + 64]
     for u in range(9):
         V(["j1", "j2"], ["g%d" % u], "ts", G(u), T.jm[:], 1 << u, None, A.bitwise_and)
-        if u == 1:
-            V(["uq", "ul"], ["uq2"], "cp", T.uq2[:].bitcast(dt.uint32), T.uq[:].bitcast(dt.uint32).indirect(T.ul[:]))
-            V(["uq", "ul"], ["us2"], "cp", T.us2[:], T.us[:].indirect(T.ul[:]))
-    V(["jr", "mg", "off"], ["flo"], "ts", T.flo[:], T.jr[:], col(MG), col(OFF), A.subtract, A.add)
-    for u in range(4):
-        V(["g%d" % u, "cx"], ["c%d" % u], "ts", T.c2[:, u:2 * C:16], G(u), -0.5, BETA, A.mult, A.add)
+    for u in range(8):
+        V(["g%d" % u], ["c%d" % u], "ts", T.c2[:, u:2 * C:16], G(u), -1.0, BETA, A.mult, A.add)
+    V(["g8"], ["c8f"], "ts", T.c2[:, 8:C:16], T.gi[:, 512:544], -1.0, 2 * BETA, A.mult, A.add)
+    V(["g8"], ["c8b"], "ts", T.c2[:, C + 8:2 * C:16], T.gi[:, 544:576], -1.0, 4 * BETA, A.mult, A.add)
+    V(["ui"], ["ul"], "cp", T.ul[:], T.ui[:])
+    V(["ut"], ["uq"], "qz", T.uq[:], T.us[:], T.ut[:])
+    for u in range(10, 13):
+        V([], ["c%d" % u], "ms", T.c2[:, u:2 * C:16], BIG)
+    V(["uq", "ul"], ["uq2"], "cp", T.uq2[:].bitcast(dt.uint32), T.uq[:].bitcast(dt.uint32).indirect(T.ul[:]))
+    op("a", ["uq", "ul"], ["us2"], "ac", T.us2[:], T.us[:].indirect(T.ul[:]), AF.Copy)
     for h, (c0, c1) in enumerate(PARTS[0]):
         V(["xt%d" % h], ["a0h%d" % h], "qz", T.aq0[:, c0:c1], T.as0[:, c0:c1], T.xt[:, 4 * c0:4 * c1])
-    for u in range(4, 8):
-        V(["g%d" % u, "cx"], ["c%d" % u], "ts", T.c2[:, u:2 * C:16], G(u), -0.5, BETA, A.mult, A.add)
-    V(["g8", "cx"], ["c8f"], "ts", T.c2[:, 8:C:16], T.gi[:, 512:544], -0.5, 2 * BETA, A.mult, A.add)
-    V(["g8", "cx"], ["c8b"], "ts", T.c2[:, C + 8:2 * C:16], T.gi[:, 544:576], -0.5, 4 * BETA, A.mult, A.add)
-    cn = ["c%d" % u for u in range(8)] + ["c8f", "c8b", "c9f", "c9b"]
+    V(["jr", "mg", "off"], ["flo"], "ts", T.flo[:], T.jr[:], col(MG), col(OFF), A.subtract, A.add)
+    for u in range(13, 16):
+        V([], ["c%d" % u], "ms", T.c2[:, u:2 * C:16], BIG)
+    cn = ["c%d" % u for u in range(8)] + ["c8f", "c8b", "c9f", "c9b"] + ["c%d" % u for u in range(10, 16)]
     V(["j1"], ["jhalf"], "ts", K(JH), T.jm[:, 0:32], 0.5, None, A.add)
+
+    def late_constants():
+        lin(["m1"], ["x4"], col(X4), col(M1), -32.0, 64.0)
+        lin(["x3"], ["x5"], col(X5), col(X3), 1.0, 32.0)
+        lin(["x1", "x2", "x3"], ["pA"], col(PA), col(X1), col(X2), col(X3))
+        lin(["x1", "x4", "x5"], ["pC"], col(PC), col(X1), col(X4), col(X5))
+        lin(["e80"], ["cv"], col(CV), T.e80[:, 0:1], -FREE, HOLD - ZV)
+        lin(["pA"], ["pB"], col(PB), col(PA), 1.0, 16.0)
+        lin(["pC"], ["pD"], col(PD), col(PC), 1.0, 16.0)
+        lin(["e80"], ["wa"], T.w64[:, 0:64], T.e80[:, 0:64], -HOLD, 0.0)
+        lin(["e80"], ["wb"], T.w64[:, 64:128], T.e80[:, 1:65], FREE, 0.0)
+        for i, (c1, v0) in enumerate(fixed):
+            lin(["jf"], ["tabv%d" % (2 * i)], T.tab[:, c1 - C:c1 - TM], T.jf[:, 0:C - TM], 0.0, ZV)
+
+    def zero_columns():
+        for b in range(4):
+            lin(["jf"], ["pz%d" % b], T.pw[:, b * PL:b * PL + P0], T.jf[:, 0:P0], 0.0, 0.0)
+        for b in range(2):
+            lin(["jf"], ["pd%d" % b], T.pw[:, b * PL + D0:(b + 1) * PL:2], T.jf[:, 0:2 * TM], 0.0, 0.0)
+
     if edge:
         V(["zt"], ["zq"], "qz", T.zq[:], T.zs[:], T.zt[:])
         z0 = TM - nb[0][1]
@@ -246,7 +258,6 @@ def rank_program(g, core, T, topo):
     plane = lambda b: T.pw[:, b * PL:(b + 1) * PL]
     bank = lambda b, n: T.psp[:, 512 * b:512 * b + n]
     pls = lambda b: ["pw%d" % b, "pz%d" % b, "pd%d" % b]
-    ln2 = math.log(2.0)
     GA = 10
 
     def scores(t, h):
@@ -269,57 +280,67 @@ def rank_program(g, core, T, topo):
         for b in range(4):
             op("t", ah + ["wq", "wsc"], ["psp%d" % b], "mm", bank(b, C),
                T.wq[:, 128 * b:128 * b + 128], T.wsc[:, 128 * b:128 * b + 128], aq[:], asc[:], True, True)
-        V([], ["tabc"], "ms", T.tab[:, CC - TM:CC], ZV)
-        V([], ["tabo"], "ms", T.tab[:, CO - TM:CO], ZV)
         for h, (c0, c1) in enumerate(PARTS[t]):
-            V([], ["pss%d" % h, "sg%d" % h], "ts", T.sg[:, c0:c1], T.pss[:, 512 * h:512 * h + c1 - c0], 0.0, 0.5, A.is_ge, A.subtract)
+            op("a", [], ["pss%d" % h, "sg%d" % h], "ac", T.sg[:, c0:c1], T.pss[:, 512 * h:512 * h + c1 - c0], AF.Sign, bias=TINY)
         sg = ["sg0", "sg1"]
-        for b in range(3):
+        early = 3 if t else 0
+        if t == 0:
+            late_constants()
+        for b in range(early):
             first_copy(b)
-        V(sg + ["flo", "ini"], ["yf"], "sc", T.y2[:, 0:C], T.flo[:], T.sg[:], col(INI), A.max, A.add)
-        V(sg + ["flo", "ini"], ["yb"], "sc", T.y2[:, 2 * C - 1:C - 1:-1], T.flo[:], T.sg[:, ::-1], col(INI), A.max, A.subtract)
+        V(sg + ["flo"], ["yf"], "sc", T.y2[:, 0:C], T.flo[:], T.sg[:], 0.5, A.max, A.add)
+        V(sg + ["flo"], ["yb"], "sc", T.y2[:, 2 * C - 1:C - 1:-1], T.flo[:], T.sg[:, ::-1], 0.5, A.max, A.subtract)
         V(["yf"], ["tf"], "tr", T.t2[:, 0:C], T.y2[:, 0:C])
         V(["yb"], ["tb"], "tr", T.t2[:, C:2 * C], T.y2[:, C:2 * C])
         V(["tf"] + cn, ["rf"], "sc", T.r2[:, 0:C - 6], T.t2[:, 0:C - 6], T.c2[:, 0:C - 6], BIG, A.min, A.add)
         V(["tb"] + cn, ["rb"], "sc", T.r2[:, C:2 * C - 6], T.t2[:, C:2 * C - 6], T.c2[:, C:2 * C - 6], BIG, A.min, A.add)
         nf, nbk = T.r2[:, 9:C:16], T.r2[:, C + 9:2 * C:16]
-        V(["tf"], ["hf"], "ts", K(0), T.t2[:, 10:C:16], 2.0, -599.75, A.mult, A.add)
         V(["rf", "rb"], ["n"], "tt", K(3), nf, nbk, A.min)
         V(["rf", "rb"], ["o"], "tt", K(4), nbk, nf, A.is_lt)
         op("a", ["n"], ["e2"], "ac", T.pm[:, 32:64], K(3), AF.Exp, scale=-ln2 / BETA)
         op("a", ["n"], ["pm"], "ac", T.pm[:, 0:32], K(3), AF.Exp, bias=math.log(1.5 * 2.0 ** 24), scale=-ln2 / BETA)
-        lin(["n"], ["b0"], K(6), K(3), -S / BETA, float(BASE))
+        op("a", ["n"], ["f9"], "ac", K(5), K(3), AF.Relu, bias=-10.5, scale=-1.0 / BETA)
+        lin(["n"], ["b0"], K(6), K(3), -S / BETA, BASE - 0.25)
         lin(["o"], ["d2"], K(8), K(4), float(S), -S / 2.0)
-        first_copy(3)
-        second_copy(0)
-        second_copy(1)
-        V(["tb"], ["hb"], "ts", K(1), T.t2[:, C + 10:2 * C:16], 2.0, -599.75, A.mult, A.add)
-        V(["hf", "o"], ["l1"], "tt", K(7), K(0), K(4), A.subtract)
-        V(["n"], ["f9"], "ts", K(5), K(3), -11 * BETA, None, A.is_le)
-        V(["hb", "l1"], ["df"], "tt", K(2), K(1), K(7), A.subtract)
+        for b in range(early, 4):
+            first_copy(b)
+        if t == 0:
+            zero_columns()
+        for b in range(4 if t else 1):
+            second_copy(b)
+        V(["tf", "o"], ["l1"], "tt", K(7), T.t2[:, 10:C:16], K(4), A.subtract)
         if t == 0:
             V(["pA", "pB", "pC", "pD"], ["prm"], "cp", T.prm[:], T.cst[:, PA:PD + 1])
-        V(["df", "f9"], ["gg"], "tt", K(10), K(2), K(5), A.mult)
+        V(["tb", "l1"], ["df"], "tt", K(2), T.t2[:, C + 10:2 * C:16], K(7), A.subtract)
         V(["e2", "jhalf"], ["x"], "tt", K(13), K(JH), T.pm[:, 32:64], A.subtract)
-        V(["l1", "gg"], ["l"], "tt", K(9), K(7), K(10), A.add)
+        V(["l1", "pm"], ["tq"], "tt", K(11), K(7), T.pm[:, 0:32], A.add)
         V(["x", "pm"], ["t2"], "tt", K(14), K(13), T.pm[:, 0:32], A.add)
-        V(["l", "pm"], ["tq"], "tt", K(11), K(9), T.pm[:, 0:32], A.add)
-        V(["l", "b0"], ["lb"], "tt", K(12), K(9), K(6), A.add)
+        V(["df", "f9"], ["gg"], "tt", K(10), K(2), K(5), A.mult)
+        V(["l1", "b0"], ["lb"], "tt", K(12), K(7), K(6), A.add)
         V(["tq", "t2"], ["q"], "tt", K(15), K(14), K(11), A.subtract)
-        V(["lb", "d2"], ["lb2"], "tt", K(16), K(12), K(8), A.add)
-        V(["lb", "q"], ["of"], "tt", T.key[:, 0:32], K(12), K(15), A.add)
-        V(["lb2", "q"], ["wf"], "tt", T.key[:, 32:64], K(16), K(15), A.add)
+        V(["lb", "gg"], ["l"], "tt", K(9), K(12), K(10), A.add)
+        V(["q", "d2"], ["q2"], "tt", K(16), K(15), K(8), A.add)
+        V(["l", "q"], ["of"], "tt", T.key[:, 0:32], K(9), K(15), A.add)
+        V(["l", "q2"], ["wf"], "tt", T.key[:, 32:64], K(9), K(16), A.add)
         V(["of"], ["kt1"], "tr", T.kt[:, 64:96], T.key[:, 0:32])
         V(["of", "wf"], ["kt0"], "tr", T.kt[:, 0:64], T.key[:, 0:64])
         if t == 0:
             V(["wa", "wb"], ["wrp0"], "tt", T.wrp[:, 0:64], T.w64[:, 0:64], T.w64[:, 64:128], A.add)
         V(["kt0", "kt1"], ["rot"], "tr", T.key[:, 64:128], T.kt[:, 16:80])
+        if t == 0:
+            V(["wrp0"], ["wrp1"], "cp", T.wrp[:, 64:128], T.wrp[:, 0:64])
         V(["of", "wf", "rot", "prm"], ["ow"], "cp", T.ow[:], T.key[:].indirect(T.prm[:]))
+        if t == 0:
+            V(["wrp1"], ["wrp2"], "cp", T.wrp[:, 128:256], T.wrp[:, 0:128])
         tabs = ["tabc", "tabo"] + ["tabv%d" % i for i in range(4)]
         V(["ow", "val"], tabs, "cp", T.tab[:].indirect(T.ow[:, 0:32]), T.val[:])
+        if t == 0:
+            V(["i16", "jwc"], ["j16"], "ts", K(J16), T.jw[:, 32:64], col(I16), None, A.add)
         op("a", tabs + ["ow"], ["gpa"], "ac", T.gp[:, 0:16 * GA], T.tab[:].indirect(T.ow[:, 32:32 + GA]), AF.Copy)
         V(tabs + ["wrp0"], ["mw0"], "sc", T.mw[:, 0:TM], T.tab[:, CC - 1:CC - TM - 1:-1], T.wrp[:, 0:TM], FREE, A.min, A.add)
         V(tabs + ["wrp0"], ["mw1"], "sc", T.mw[:, TM:2 * TM], T.tab[:, CO - 1:CO - TM - 1:-1], T.wrp[:, 0:TM], FREE, A.min, A.add)
+        if t == 0:
+            V(["wrp2"], ["wrp3"], "cp", T.wrp[:, 256:512], T.wrp[:, 0:256])
         V(["mw0", "mw1", "cv"], ["ml"], "ts", T.ml[:], T.mw[:, 15:128:16], col(CV), None, A.add)
         for b in (2, 3):
             op("a", ["ml"] + pls(b), ["mt%d" % b], "ac", T.mt[:, b:512:4], plane(b).indirect(T.ml[:]), AF.Copy)
@@ -336,32 +357,21 @@ def rank_program(g, core, T, topo):
                 sent[0] += len(mine[d])
             g.remote_dma_fused(trs, local_sem=T.sem.sent)
         op("a", tabs + ["ow"], ["gpb"], "ac", T.gp[:, 16 * GA:C], T.tab[:].indirect(T.ow[:, 32 + GA:64]), AF.Copy)
-        second_copy(2)
-        second_copy(3)
         if t == 0:
-            for i in range(3):
-                w = 64 << i
-                V(["wrp%d" % i], ["wrp%d" % (i + 1)], "cp", T.wrp[:, w:2 * w], T.wrp[:, 0:w])
-                if i < 2:
-                    V([], ["pd%d" % i], "ms", T.pw[:, i * PL + D0:(i + 1) * PL], 0.0)
-            V(["pi"], ["p15"], "ts", T.pi[:, 5:6], T.pi[:, 0:1], 15, None, A.bitwise_and)
+            clear_lists()
+            for b in (1, 2, 3):
+                second_copy(b)
+            V(["et%d" % b for b in range(4)], ["eq"], "qz", T.eq[:], T.es[:], T.et[:])
         else:
             V(["vt"], ["vq"], "qz", T.vq[:], T.vs[:], T.vt[:])
         V(["gpa", "gpb", "wrp3"], ["gw"], "sc", T.gw[:], T.gp[:], T.wrp[:], FREE, A.min, A.add)
-        if t == 0:
-            V(["p15"], ["i16"], "cp", col(I16), T.pi[:, 5:6])
         V(["gw", "cv"], ["lst"], "ts", T.lst[:], T.gw[:, 15:C:16], col(CV), None, A.add)
         V(["gw", "cv"], ["lc"], "ts", K(0), T.gw[:, 15:C:16], col(CV), None, A.add)
         V(["gw", "cv"], ["lf"], "ts", K(1), T.gw[:, 15:C:16], col(CV), float(D0), A.add, A.is_ge)
-        if t == 0:
-            V(["i16", "jwc"], ["j16"], "ts", K(J16), T.jw[:, 32:64], col(I16), None, A.add)
         V(["lst", "pc0"] + pls(0), ["x00"], "tt", T.x0[:, P0:D0], plane(0).indirect(T.lst[:]), T.pc[:, 0:C], A.add)
         V(["lc", "lf"], ["lg"], "tt", K(2), K(0), K(1), A.mult)
-        if t == 0:
-            V(["et%d" % b for b in range(4)], ["eq"], "qz", T.eq[:], T.es[:], T.et[:])
-        V(["lg", "j16"], ["lh"], "tt", K(5), K(2), K(J16), A.max)
         V(["lst", "pc1"] + pls(1), ["x01"], "tt", T.x0[:, PL + P0:PL + D0], plane(1).indirect(T.lst[:]), T.pc[:, C:2 * C], A.add)
-        V(["lh"], ["lst2"], "cp", T.lst2[:], K(5))
+        V(["lg", "j16"], ["lh"], "tt", K(17), K(2), K(J16), A.max)
         order("t", ["eq", "zl%d" % t, "zm%d" % t], [])
         wait("t", "arr%d" % t, arrive)
         for b in (2, 0, 3, 1):
@@ -369,6 +379,7 @@ def rank_program(g, core, T, topo):
                T.eq[:, 128 * b:128 * b + 128], T.es[:, 128 * b:128 * b + 128], lq[:], ls[:], True, True)
         for b in (2, 3):
             op("a", [], ["psp%d" % b, "pd%d" % b], "ac", T.pw[:, b * PL + D0:(b + 1) * PL:2], bank(b, 128), AF.Copy)
+        V(["lh"], ["lst2"], "cp", T.lst2[:], K(17))
         for b in (0, 1):
             V(["mt%d" % b], ["psp%d" % b, "fx%d" % b], "tt", T.x0[:, b * PL + D0:(b + 1) * PL:2], T.mt[:, b:512:4], bank(b, 128), A.add)
         nq, ns = T["aq%d" % (t + 1)], T["as%d" % (t + 1)]
@@ -387,11 +398,13 @@ def rank_program(g, core, T, topo):
             else:
                 dma("s", names, [], T.oc[:, 4 * c0:4 * c1], bytes_of(nq[:, c0:c1]))
                 op("t", names + ["vq"], ["psy%d" % h], "mm", T.psy[:, 512 * h:512 * h + c1 - c0], T.vq[:], T.vs[:], nq[:, c0:c1], ns[:, c0:c1], True, True)
-                op("a", [], ["psy%d" % h, "y%d" % h], "ac", T.ysb[:, c0:c1], T.psy[:, 512 * h:512 * h + c1 - c0], AF.Copy)
+                if h == 0:
+                    op("a", [], ["psy0", "y0"], "ac", T.ysb[:, c0:c1], T.psy[:, 0:c1 - c0], AF.Copy)
+                else:
+                    V([], ["psy1", "y1"], "cp", T.ysb[:, c0:c1], T.psy[:, 512:512 + c1 - c0])
+                    for k in range(4):
+                        dma("saas"[k], ["a%dh0" % R, "a%dh1" % R], [], T.osc[4 * k:4 * k + 4, :], T["as%d" % R][32 * k:32 * k + 4, :])
                 dma("a", ["y%d" % h], [], T.y[:, c0:c1], T.ysb[:, c0:c1])
-    last = ["a%dh0" % R, "a%dh1" % R]
-    for k in range(4):
-        dma("s", last, [], T.osc[4 * k:4 * k + 4, :], T["as%d" % R][32 * k:32 * k + 4, :])
     for i in range(ndma[0]):
         g.sync.wait_ge(T.sem["d%d" % i], 16)
     for q in count:

@@ -1,22 +1,25 @@
-import math
 from concourse.bass import DstId, RemoteDMATransfer
 from concourse.mybir import dt, AluOpType, AxisListType, ActivationFunctionType
 
 C, TM, R = 512, 64, 2
 P0 = 16
-D0 = P0 + C
-PL = D0 + 4 * TM
 ZV = -(256.0 + P0)
-S = 1280
-BASE = S // 2 + 16
-CC = 10 * S + BASE
-CO = 12 * S - S // 2 + BASE
-TAB = CO + S // 2
-BETA = 1.0 / 16
-BIG = 2048.0
+AV = 512
+D0 = AV + 256 + P0
+PL = D0 + 8 * TM
+X0 = 2 * AV - 494
+XL = 1552
+S, DP = 3072, 1536
+CC = 28928
+LK = DP - 1
+TAB = CC + LK + TM + 1
+BETA = 2.0 ** -15
+H0 = -1000.0
+BIG = 3000
 TINY = 2.0 ** -120
-HOLD, FREE = 1280.0, 2064.0
+HOLD, FREE = 1296.0, 2592.0
 PARTS = (((0, 256), (256, C)), ((0, 384), (384, C)), ((0, 384), (384, C)))
+GA, GB = 8, 22
 F4, U8 = "float8_e4m3fn_x4", "uint8"
 
 
@@ -28,20 +31,18 @@ SCRATCH = {
     "xt": _sb(4 * C, "bfloat16"), "ut": _sb(512, "bfloat16"), "vt": _sb(512, "bfloat16"),
     "uq": _sb(128, F4), "us": _sb(128, U8), "uq2": _sb(128, F4), "us2": _sb(128, U8),
     "vq": _sb(128, F4), "vs": _sb(128, U8), "wq": _sb(512, F4), "wsc": _sb(512, U8),
-    "et": _sb(2048, "bfloat16"), "eq": _sb(512, F4), "es": _sb(512, U8),
-    "zt": _sb(512, "bfloat16"), "zq": _sb(128, F4), "zs": _sb(128, U8), "ones": _sb(512, "bfloat16"),
+    "et": _sb(1056, "bfloat16"), "eq": _sb(512, F4), "es": _sb(512, U8),
+    "zt": _sb(512, "bfloat16"), "zq": _sb(128, F4), "zs": _sb(128, U8), "ones": _sb(516, "bfloat16"),
     "ui": _sb(8, "int32"), "ul": _sb(8, "uint16"),
-    "i80": _sb(80, "int32"), "i80b": _sb(80, "int32"), "e80": _sb(80, "float32"),
-    "pi": _sb(8, "int32"), "cst": _sb(32, "float32"), "w64": _sb(128, "float32"),
-    "jf": _sb(C, "float32"), "jh": _sb(C, "float32"), "jr": _sb(C, "float32"), "flo": _sb(C, "float16"),
-    "jw": _sb(64, "int32"), "jm": _sb(64, "int32"), "gi": _sb(9 * 64, "int32"), "prm": _sb(4, "uint16"),
-    "c2": _sb(2 * C, "float16"),
-    "wrp": _sb(C, "float16"), "val": _sb(C, "bfloat16"), "tab": _sb(TAB, "bfloat16"),
-    "sg": _sb(C, "bfloat16"), "y2": _sb(2 * C, "float16"), "t2": _sb(2 * C, "float16"), "r2": _sb(2 * C, "float16"),
-    "k": _sb(32 * 20, "float32"), "pm": _sb(64, "float32"), "key": _sb(128, "float32"), "kt": _sb(96, "float32"),
+    "pi": _sb(16, "int32"), "cst": _sb(48, "float32"), "w64": _sb(144, "float32"),
+    "jf": _sb(256, "float32"), "jh": _sb(256, "float32"), "jr": _sb(256, "float32"), "flo": _sb(C, "float16"),
+    "prm": _sb(4, "uint16"), "c2": _sb(2 * C, "float32"),
+    "wrp": _sb(C, "bfloat16"), "wrm": _sb(128, "bfloat16"), "val0": _sb(C, "bfloat16"), "val": _sb(C, "bfloat16"), "tab": _sb(TAB, "bfloat16"),
+    "sg": _sb(C, "bfloat16"), "y2": _sb(2 * C, "float16"), "t2": _sb(2 * C, "float16"), "r2": _sb(2 * C, "float32"),
+    "k": _sb(32 * 14, "float32"), "key": _sb(128, "float32"), "kt": _sb(64, "float32"),
     "ow": _sb(64, "uint16"), "lst": _sb(32, "uint16"), "lst2": _sb(32, "uint16"), "ml": _sb(8, "uint16"),
     "mw": _sb(128, "float16"), "gp": _sb(C, "bfloat16"), "gw": _sb(C, "float16"),
-    "pw": _sb(4 * PL, "bfloat16"), "pc": _sb(4 * C, "bfloat16"), "x0": _sb(2 * PL, "bfloat16"),
+    "pw": _sb(4 * PL, "bfloat16"), "pc": _sb(4 * C, "bfloat16"), "x0": _sb(2 * XL, "bfloat16"),
     "mt": _sb(512, "bfloat16"), "xn": _sb(4 * C, "bfloat16"), "ysb": _sb(C, "float32"),
     "pss": ("psum", [128, 1024], "float32"), "psp": ("psum", [128, 2048], "float32"), "psy": ("psum", [128, 1024], "float32"),
 }
@@ -53,7 +54,7 @@ for _t in range(R):
         SCRATCH["%sq%d" % (_n, _t)] = _sb(128, F4)
         SCRATCH["%ss%d" % (_n, _t)] = _sb(128, U8)
 
-NDMA = 24
+NDMA = 32
 SEMAPHORES = ["v", "a", "t", "p", "sent"] + ["arr%d" % _t for _t in range(R)] + ["d%d" % _i for _i in range(NDMA)]
 
 
@@ -99,7 +100,7 @@ def rank_program(g, core, T, topo):
         calls = {
             "ts": lambda: e.tensor_scalar(*args), "tt": lambda: e.tensor_tensor(*args), "cp": lambda: e.tensor_copy(*args),
             "ms": lambda: e.memset(*args), "sc": lambda: e.tensor_tensor_scan(*args), "tr": lambda: e.transpose(*args),
-            "qz": lambda: e.quantize_mx(*args), "ac": lambda: e.activation(*args, **kw),
+            "qz": lambda: e.quantize_mx(*args), "ac": lambda: e.activation(*args, **kw), "rd": lambda: e.tensor_reduce(*args),
             "mm": lambda: e.matmul_mx(*args), "io": lambda: e.iota(*args, **kw), "as": lambda: e.affine_select(*args),
         }
         count[q] += 1
@@ -116,8 +117,11 @@ def rank_program(g, core, T, topo):
     def V(r, w, name, *args):
         op("v", r, w, name, *args)
 
+    def act(r, w, out, in_, f, scale, bias):
+        op("a", r, w, "ac", out, in_, f, bias=bias, scale=scale)
+
     def lin(r, w, out, in_, scale, bias):
-        op("a", r, w, "ac", out, in_, AF.Identity, bias=bias, scale=scale)
+        act(r, w, out, in_, AF.Identity, scale, bias)
 
     def iota(w, *args):
         op("p", [], w, "io", *args, allow_small_or_imprecise_dtypes=True)
@@ -127,16 +131,18 @@ def rank_program(g, core, T, topo):
 
     nb = []
     if rank > 0:
-        nb.append((T.cores[rank - 1], 0, TM))
+        nb.append((T.cores[rank - 1], 0))
     if rank < n_ranks - 1:
-        nb.append((T.cores[rank + 1], TM, 0))
+        nb.append((T.cores[rank + 1], TM))
     edge = len(nb) < 2
 
     col = lambda i: T.cst[:, i:i + 1]
     K = lambda i: T.k[:, 32 * i:32 * i + 32]
-    M1, PW, C1, MG, OFF, INI, CV, I32, I16, X0, X1, X2, X3, X4, X5, PA, PB, PC, PD = range(19)
-    JH, J16 = 18, 19
-    ln2 = math.log(2.0)
+    XX, AA, EE, EV, E9, PW, C1, MG, OA, OB, OC, OD, OFF, INC, YP, YQ, Y0, M1, X1, X2, X3, PA, PB, PC, PD, YX, YA = range(5, 32)
+    KF, KB, JW, JF, J16, JC, L2, L3 = 0, 1, 2, 3, 4, 5, 6, 7
+    KG = lambda u: K(8 + u - 5)
+    slot = lambda d, pos: T.c2[:, d * C + pos:(d + 1) * C:16]
+    up, dn = 1.0 + 2 * BETA, 1.0 - 2 * BETA
 
     dma("s", [], ["ut"], T.ut[:], T.u[:])
     for h, (c0, c1) in enumerate(PARTS[0]):
@@ -146,95 +152,108 @@ def rank_program(g, core, T, topo):
     dma("s", [], ["vt"], T.vt[:], T.v[:])
 
     def clear_lists():
-        iota(["tabc"], T.tab[:, CC - TM:CC], [[0, TM]], int(ZV), 0)
-        iota(["tabo"], T.tab[:, CO - TM:CO], [[0, TM]], int(ZV), 0)
+        iota(["tabc"], T.tab[:, CC - TM:CC + TM], [[0, 2 * TM]], int(ZV), 0)
 
-    op("p", [], ["pi"], "io", T.pi[:, 0:1], [[0, 1]], 0, 1)
-    op("p", [], ["jwa"], "io", T.jw[:, 0:32], [[32, 16], [0, 2]], 0, 0)
-    op("p", [], ["i80"], "io", T.i80[:], [[1, 80]], 128, -1)
-    iota(["jf"], T.jf[:], [[1, C]], 0, 0)
+    op("p", [], ["pi"], "io", T.pi[:, 0:2], [[12, 2]], 0, 1)
+    iota(["jf"], T.jf[:], [[1, 256]], 0, 0)
     op("p", [], ["ui"], "io", T.ui[:], [[16, 8]], 0, 0)
+    iota(["jw"], K(JW), [[32, 16], [0, 2]], 0, 0)
+    iota(["val0a"], T.val0[:, 0:256], [[32, 16], [1, 16]], -256, 0)
+    iota(["val0b"], T.val0[:, 256:C], [[32, 16], [-1, 16]], 31 - 256, 0)
+    for u in range(5, 9):
+        pat = [[0, 1 << (8 - u)], [1 << u, 2], [0, 2 << (u - 5)]]
+        iota(["kg%d" % u], KG(u), pat[1:] if u == 8 else pat, 0, 0)
+    iota(["s0"], T.c2[:, 0:2 * C:16], [[0, 64]], BIG, 0)
+    iota(["s15"], T.c2[:, 15:2 * C:16], [[0, 64]], 0, 0)
+    iota(["tabv1"], T.tab[:, CC - LK - TM:CC - LK], [[-4, TM]], AV + 4 * (2 * TM - 1), 0)
+    iota(["tabv3"], T.tab[:, CC + LK:CC + LK + TM], [[-4, TM]], AV + 4 * (TM - 1), 0)
+    clear_lists()
+    iota(["jc"], K(JC), [[16, 32]], P0, 0)
     if edge:
         iota(["zt"], T.zt[:], [[0, 512]], 0, 0)
-    iota(["val"], T.val[:], [[1, C]], -256, 0)
-    fixed = ((CC - S // 2, 256), (CO + S // 2, 256 + 2 * TM))
-    for i, (c1, v0) in enumerate(fixed):
-        iota(["tabv%d" % (2 * i + 1)], T.tab[:, c1 - TM:c1], [[-2, TM]], v0 + 2 * (TM - 1), 0)
-    clear_lists()
-    op("p", [], ["jwc"], "io", T.jw[:, 32:64], [[16, 32]], P0, 0)
-    iota(["ones"], T.ones[:], [[0, 512]], 1, 0)
-    for b in range(4):
-        op("p", ["ones"], ["et%d" % b], "as", T.et[:, 512 * b:512 * b + 512], T.ones[:], [[-1, 512]], A.is_equal, 0.0, b, 4)
-    V([], ["c9f"], "ms", T.c2[:, 9:C:16], -(1.0 + 10 * BETA))
-    V([], ["c9b"], "ms", T.c2[:, C + 9:2 * C:16], -(1.0 + 11.5 * BETA))
-    V(["pi"], ["p15"], "ts", T.pi[:, 5:6], T.pi[:, 0:1], 15, None, A.bitwise_and)
-    V(["pi"], ["pr"], "ts", T.pi[:, 1:2], T.pi[:, 0:1], 31, None, A.bitwise_and)
-    V(["p15"], ["p9"], "ts", col(X0), T.pi[:, 5:6], 9.0, None, A.min)
-    op("a", ["p9"], ["pwc"], "ac", col(PW), col(X0), AF.Exp, scale=ln2)
-    V(["pr"], ["i32"], "cp", col(I32), T.pi[:, 1:2])
-    V(["p15"], ["i16"], "cp", col(I16), T.pi[:, 5:6])
-    V(["i32", "jwa"], ["j1"], "ts", T.jm[:, 0:32], T.jw[:, 0:32], col(I32), None, A.add)
-    V(["pi"], ["ph"], "ts", T.pi[:, 2:3], T.pi[:, 0:1], 4, 1, A.logical_shift_right, A.bitwise_and)
-    V(["j1"], ["j2"], "ts", T.jm[:, 32:64], T.jm[:, 0:32], -1.0, float(C - 1), A.mult, A.add)
-    V(["pi"], ["pa"], "ts", T.pi[:, 3:4], T.pi[:, 0:1], 14, None, A.bitwise_and)
-    V(["pi"], ["pb"], "ts", T.pi[:, 4:5], T.pi[:, 0:1], 1, None, A.bitwise_and)
-    V(["ph"], ["m1"], "cp", col(M1), T.pi[:, 2:3])
-    V(["i80"], ["i80b"], "ts", T.i80b[:], T.i80[:], 15, None, A.bitwise_and)
-    V(["pb", "m1"], ["x1"], "ts", col(X1), T.pi[:, 4:5], col(M1), None, A.not_equal)
-    V(["i80b"], ["e80"], "ts", T.e80[:], T.i80b[:], 0.0, None, A.is_equal)
-    V(["pa", "m1"], ["x3"], "ts", col(X3), T.pi[:, 3:4], col(M1), None, A.add)
+
+    V([], ["kf"], "ms", K(KF), -up)
+    V([], ["kb"], "ms", K(KB), dn)
+    V([], ["s14f"], "ms", slot(0, 14), BETA * LK)
+    V(["pi"], ["pe"], "ts", T.pi[:, 9:10], T.pi[:, 1:2], 15, None, A.bitwise_and)
+    V(["pi"], ["px"], "ts", T.pi[:, 7:8], T.pi[:, 0:1], 15, None, A.bitwise_and)
+    V(["pe"], ["e9"], "ts", col(E9), T.pi[:, 9:10], 9.0, None, A.min)
+    for u, m in ((2, 1), (3, 2), (4, 4), (5, 8), (6, 16), (8, 31), (10, 14)):
+        V(["pi"], ["pb%d" % u], "ts", T.pi[:, u:u + 1], T.pi[:, 0:1], m, None, A.bitwise_and)
+    V(["jf", "e9"], ["tw"], "ts", T.cst[:, 32:41], T.jf[:, 0:9], col(E9), 1.0, A.is_lt, A.add)
+    V(["pe", "px"] + ["pb%d" % u for u in (2, 3, 4, 5, 6, 8, 10)], ["cf"], "cp", T.cst[:, 0:9], T.pi[:, 2:11])
+    V(["tw"], ["pwc"], "rd", col(PW), T.cst[:, 32:41], AxisListType.X, A.mult)
+    V(["e9"], ["oa"], "ts", col(OA), col(E9), 9.0, -1256.0, A.not_equal, A.mult)
+    V(["cf"], ["ob"], "ts", col(OB), col(XX), 0.0, -3000.0, A.is_equal, A.mult)
+    V(["cf"], ["oc"], "ts", col(OC), col(XX), 1.0, -1000.0, A.is_equal, A.mult)
+    V(["e9"], ["inc"], "ts", col(INC), col(E9), 9.0, 256.0, A.not_equal, A.mult)
+    V(["oa", "ob", "oc"], ["od"], "ts", col(OD), col(OA), col(OB), col(OC), A.add, A.add)
+    V(["cf", "jw"], ["jj"], "ts", K(JF), K(JW), col(AA), None, A.add)
+    V(["ui"], ["ul"], "cp", T.ul[:], T.ui[:])
+    V([], ["s14b"], "ms", slot(1, 14), -BETA * LK)
+    V([], ["s1f"], "ms", slot(0, 1), 0.0)
+    V([], ["s2f"], "ms", slot(0, 2), 0.0)
+    V([], ["pz"], "ms", T.pw[:, 0:4 * PL:PL], 0.0)
+    V([], ["tabv2"], "ms", T.tab[:, CC + LK + TM:CC + LK + TM + 1], ZV)
+    V([], ["ones"], "ms", T.ones[:], 1.0)
+    for i in range(2):
+        op("p", ["ones"], ["et%d" % i], "as", T.et[:, 528 * i:528 * i + 516], T.ones[:], [[-1, 516]], A.is_equal, 0.0, 2 + i, 4)
     lin(["pwc"], ["c1"], col(C1), col(PW), -0.5, 0.5)
     lin(["pwc"], ["mg"], col(MG), col(PW), 1.5 * 2.0 ** 23, 0.0)
-    lin(["e80"], ["off"], col(OFF), T.e80[:, 10:11], -2002.0, 2.0)
     lin(["jf", "c1"], ["jh"], T.jh[:], T.jf[:], 1.0, col(C1))
-    lin(["m1"], ["x2"], col(X2), col(M1), 32.0, 64.0)
+    lin(["od"], ["off"], col(OFF), col(OD), 1.0, 1000.0)
     lin(["jh", "mg"], ["jr"], T.jr[:], T.jh[:], 1.0, col(MG))
-    G = lambda u: T.gi[:, 64 * u:64 * u + 64]
-    for u in range(9):
-        V(["j1", "j2"], ["g%d" % u], "ts", G(u), T.jm[:], 1 << u, None, A.bitwise_and)
-    for u in range(8):
-        V(["g%d" % u], ["c%d" % u], "ts", T.c2[:, u:2 * C:16], G(u), -1.0, BETA, A.mult, A.add)
-    V(["g8"], ["c8f"], "ts", T.c2[:, 8:C:16], T.gi[:, 512:544], -1.0, 2 * BETA, A.mult, A.add)
-    V(["g8"], ["c8b"], "ts", T.c2[:, C + 8:2 * C:16], T.gi[:, 544:576], -1.0, 4 * BETA, A.mult, A.add)
-    V(["ui"], ["ul"], "cp", T.ul[:], T.ui[:])
+    for u in range(5):
+        lin(["cf", "kf"], ["sf%d" % u], slot(0, 4 + u), K(KF), col(u), BETA * S)
+        lin(["cf", "kb"], ["sb%d" % u], slot(1, 4 + u), K(KB), col(u), BETA * S - dn * (1 << u))
+
+    def high_steps():
+        for u in range(5, 9):
+            last = u == 8
+            lin(["kg%d" % u], ["sf%d" % u], slot(0, 4 + u), KG(u), -up, 257.0 - BETA * (8 * S + DP) if last else BETA * S)
+            lin(["kg%d" % u], ["sb%d" % u], slot(1, 4 + u), KG(u), dn,
+                (257.0 - BETA * (8 * S + 1024) if last else BETA * S) - dn * (1 << u))
+
+    cn = [["s0", "s15", "s1f", "s2f", "s3f", "s14f", "d13f"] + ["sf%d" % u for u in range(9)],
+          ["s0", "s15", "s3b", "s14b", "d13b", "d1b", "d2b"] + ["sb%d" % u for u in range(9)]]
     V(["ut"], ["uq"], "qz", T.uq[:], T.us[:], T.ut[:])
-    for u in range(10, 13):
-        V([], ["c%d" % u], "ms", T.c2[:, u:2 * C:16], BIG)
+    V(["jr", "mg", "off"], ["floa"], "ts", T.flo[:, 0:256], T.jr[:], col(MG), col(OFF), A.subtract, A.add)
     V(["uq", "ul"], ["uq2"], "cp", T.uq2[:].bitcast(dt.uint32), T.uq[:].bitcast(dt.uint32).indirect(T.ul[:]))
     op("a", ["uq", "ul"], ["us2"], "ac", T.us2[:], T.us[:].indirect(T.ul[:]), AF.Copy)
+    lin(["jj"], ["s3f"], slot(0, 3), K(JF), up, -256.0 - BETA * (CC - DP))
+    lin(["jj"], ["s3b"], slot(1, 3), K(JF), -dn, 511 * dn - 256.0 - BETA * (CC - 1025))
+    lin(["cf"], ["m1"], col(M1), col(4), 1.0 / 16, 0.0)
+    lin(["cf"], ["n2"], col(Y0), col(4), -2.0, 0.0)
+    act(["cf"], ["ya"], col(YA), col(AA), AF.Abs, 1.0, -15.5)
+    lin(["cf"], ["yx"], col(YX), col(XX), -1.0, 0.0)
     for h, (c0, c1) in enumerate(PARTS[0]):
         V(["xt%d" % h], ["a0h%d" % h], "qz", T.aq0[:, c0:c1], T.as0[:, c0:c1], T.xt[:, 4 * c0:4 * c1])
-    V(["jr", "mg", "off"], ["flo"], "ts", T.flo[:], T.jr[:], col(MG), col(OFF), A.subtract, A.add)
-    for u in range(13, 16):
-        V([], ["c%d" % u], "ms", T.c2[:, u:2 * C:16], BIG)
-    cn = ["c%d" % u for u in range(8)] + ["c8f", "c8b", "c9f", "c9b"] + ["c%d" % u for u in range(10, 16)]
-    V(["j1"], ["jhalf"], "ts", K(JH), T.jm[:, 0:32], 0.5, None, A.add)
+    V(["floa", "inc"], ["flob"], "ts", T.flo[:, 256:C], T.flo[:, 0:256], col(INC), None, A.add)
+    V([], ["tabv0"], "ms", T.tab[:, CC - LK - C:CC - LK - TM], ZV)
+    V(["val0a", "cf"], ["vala"], "ts", T.val[:, 0:256], T.val0[:, 0:256], col(4), None, A.add)
+    V(["val0b", "cf"], ["valb"], "ts", T.val[:, 256:C], T.val0[:, 256:C], col(4), None, A.subtract)
 
     def late_constants():
-        lin(["m1"], ["x4"], col(X4), col(M1), -32.0, 64.0)
-        lin(["x3"], ["x5"], col(X5), col(X3), 1.0, 32.0)
-        lin(["x1", "x2", "x3"], ["pA"], col(PA), col(X1), col(X2), col(X3))
-        lin(["x1", "x4", "x5"], ["pC"], col(PC), col(X1), col(X4), col(X5))
-        lin(["e80"], ["cv"], col(CV), T.e80[:, 0:1], -FREE, HOLD - ZV)
-        lin(["pA"], ["pB"], col(PB), col(PA), 1.0, 16.0)
-        lin(["pC"], ["pD"], col(PD), col(PC), 1.0, 16.0)
-        lin(["e80"], ["wa"], T.w64[:, 0:64], T.e80[:, 0:64], -HOLD, 0.0)
-        lin(["e80"], ["wb"], T.w64[:, 64:128], T.e80[:, 1:65], FREE, 0.0)
-        for i, (c1, v0) in enumerate(fixed):
-            lin(["jf"], ["tabv%d" % (2 * i)], T.tab[:, c1 - C:c1 - TM], T.jf[:, 0:C - TM], 0.0, ZV)
+        lin(["cf", "m1"], ["pA"], col(PA), col(XX), 2.0, col(M1))
+        lin(["cf", "m1"], ["x2"], col(X2), col(EV), 1.0, col(M1))
+        act(["cf", "n2"], ["x1"], col(X1), col(0), AF.Abs, 32.0, col(Y0))
+        lin(["ya"], ["yp"], col(YP), col(YA), 1.0, -15.5)
+        lin(["ya"], ["yq"], col(YQ), col(YA), -1.0, 0.5)
 
-    def zero_columns():
-        for b in range(4):
-            lin(["jf"], ["pz%d" % b], T.pw[:, b * PL:b * PL + P0], T.jf[:, 0:P0], 0.0, 0.0)
-        for b in range(2):
-            lin(["jf"], ["pd%d" % b], T.pw[:, b * PL + D0:(b + 1) * PL:2], T.jf[:, 0:2 * TM], 0.0, 0.0)
+    def later_constants():
+        lin(["x1", "x2"], ["x3"], col(X3), col(X1), 1.0, col(X2))
+        lin(["pA"], ["pB"], col(PB), col(PA), 1.0, 96.0)
+        for i, y in enumerate((YP, YQ, YX)):
+            act(["jf", "yp", "yq", "yx"], ["wd%d" % i], T.w64[:, 96 + 16 * i:112 + 16 * i], T.jf[:, 0:16], AF.Abs, 1.0, col(y))
+        lin(["x3"], ["pC"], col(PC), col(X3), 1.0, 32.0)
+        lin(["x3"], ["pD"], col(PD), col(X3), 1.0, 48.0)
+        act(["wd0", "wd1", "wd2"], ["wa"], T.w64[:, 0:48], T.w64[:, 96:144], AF.Relu, -HOLD, HOLD)
+        for i in range(3):
+            act(["wd%d" % i], ["wb%d" % i], T.w64[:, 48 + 16 * i:63 + 16 * i], T.w64[:, 97 + 16 * i:112 + 16 * i], AF.Relu, -FREE, FREE)
 
-    if edge:
-        V(["zt"], ["zq"], "qz", T.zq[:], T.zs[:], T.zt[:])
-        z0 = TM - nb[0][1]
-        for t in range(R):
-            dma("s", ["zq"], ["zl%d" % t], bytes_of(T["lq%d" % t][:, z0:z0 + TM]), bytes_of(T.zq[:, 0:TM]))
-            dma("s", ["zq"], ["zm%d" % t], T["ls%d" % t][:, z0:z0 + TM], T.zs[:, 0:TM])
+    def spread(name, buf, n0, i):
+        n0 = n0 << i
+        op("a", ["%s%d" % (name, i)], ["%s%d" % (name, i + 1)], "ac", buf[:, n0:2 * n0], buf[:, 0:n0], AF.Copy)
 
     def masks(c):
         r = T.rank_of(c)
@@ -253,23 +272,20 @@ def rank_program(g, core, T, topo):
         return out
 
     mine = masks(core)
-    arrive = sum(2 * len(masks(d)[core]) for d, _, _ in nb)
+    arrive = sum(2 * len(masks(d)[core]) for d, _ in nb)
     sent = [0]
     plane = lambda b: T.pw[:, b * PL:(b + 1) * PL]
     bank = lambda b, n: T.psp[:, 512 * b:512 * b + n]
-    pls = lambda b: ["pw%d" % b, "pz%d" % b, "pd%d" % b]
-    GA = 10
+    pls = lambda b: ["pw%d" % b, "pz", "pd%d" % b]
 
     def scores(t, h):
         c0, c1 = PARTS[t][h]
         op("t", ["a%dh%d" % (t, h), "uq2", "us2"], ["pss%d" % h], "mm", T.pss[:, 512 * h:512 * h + c1 - c0], T.uq2[:], T.us2[:],
            T["aq%d" % t][:, c0:c1], T["as%d" % t][:, c0:c1], True, True)
 
-    def first_copy(b):
-        op("a", [], ["psp%d" % b, "pw%d" % b], "ac", T.pw[:, b * PL + P0:b * PL + D0], bank(b, C), AF.Copy, scale=0.0625)
-
-    def second_copy(b):
-        op("a", ["pw%d" % b], ["pc%d" % b], "ac", T.pc[:, b * C:(b + 1) * C], T.pw[:, b * PL + P0:b * PL + D0], AF.Copy)
+    def p_copy(b):
+        op("a", [], ["psp%d" % b, "pw%d" % b], "ac", T.pw[:, b * PL + P0:b * PL + P0 + C], bank(b, C), AF.Copy, scale=0.0625)
+        dma("s", ["pw%d" % b], ["pc%d" % b], T.pc[:, b * C:(b + 1) * C], T.pw[:, b * PL + P0:b * PL + P0 + C])
 
     scores(0, 0)
     scores(0, 1)
@@ -282,66 +298,57 @@ def rank_program(g, core, T, topo):
                T.wq[:, 128 * b:128 * b + 128], T.wsc[:, 128 * b:128 * b + 128], aq[:], asc[:], True, True)
         for h, (c0, c1) in enumerate(PARTS[t]):
             op("a", [], ["pss%d" % h, "sg%d" % h], "ac", T.sg[:, c0:c1], T.pss[:, 512 * h:512 * h + c1 - c0], AF.Sign, bias=TINY)
-        sg = ["sg0", "sg1"]
-        early = 3 if t else 0
+        sg = ["sg0", "sg1", "floa", "flob"]
         if t == 0:
+            high_steps()
             late_constants()
-        for b in range(early):
-            first_copy(b)
-        V(sg + ["flo"], ["yf"], "sc", T.y2[:, 0:C], T.flo[:], T.sg[:], 0.5, A.max, A.add)
-        V(sg + ["flo"], ["yb"], "sc", T.y2[:, 2 * C - 1:C - 1:-1], T.flo[:], T.sg[:, ::-1], 0.5, A.max, A.subtract)
+        else:
+            p_copy(0)
+        V(sg, ["yf"], "sc", T.y2[:, 0:C], T.flo[:], T.sg[:], H0, A.max, A.add)
+        V(sg, ["yb"], "sc", T.y2[:, 2 * C - 1:C - 1:-1], T.flo[:], T.sg[:, ::-1], H0, A.max, A.subtract)
         V(["yf"], ["tf"], "tr", T.t2[:, 0:C], T.y2[:, 0:C])
         V(["yb"], ["tb"], "tr", T.t2[:, C:2 * C], T.y2[:, C:2 * C])
-        V(["tf"] + cn, ["rf"], "sc", T.r2[:, 0:C - 6], T.t2[:, 0:C - 6], T.c2[:, 0:C - 6], BIG, A.min, A.add)
-        V(["tb"] + cn, ["rb"], "sc", T.r2[:, C:2 * C - 6], T.t2[:, C:2 * C - 6], T.c2[:, C:2 * C - 6], BIG, A.min, A.add)
-        nf, nbk = T.r2[:, 9:C:16], T.r2[:, C + 9:2 * C:16]
-        V(["rf", "rb"], ["n"], "tt", K(3), nf, nbk, A.min)
-        V(["rf", "rb"], ["o"], "tt", K(4), nbk, nf, A.is_lt)
-        op("a", ["n"], ["e2"], "ac", T.pm[:, 32:64], K(3), AF.Exp, scale=-ln2 / BETA)
-        op("a", ["n"], ["pm"], "ac", T.pm[:, 0:32], K(3), AF.Exp, bias=math.log(1.5 * 2.0 ** 24), scale=-ln2 / BETA)
-        op("a", ["n"], ["f9"], "ac", K(5), K(3), AF.Relu, bias=-10.5, scale=-1.0 / BETA)
-        lin(["n"], ["b0"], K(6), K(3), -S / BETA, BASE - 0.25)
-        lin(["o"], ["d2"], K(8), K(4), float(S), -S / 2.0)
-        for b in range(early, 4):
-            first_copy(b)
+        hf, hb = T.t2[:, 0:C:16], T.t2[:, C:2 * C:16]
+        lin(["tf"], ["d13f"], slot(0, 13), hf, -BETA, BETA * H0)
+        lin(["tf"], ["d13b"], slot(1, 13), hf, -BETA, BETA * H0)
+        lin(["tf"], ["d2b"], slot(1, 2), hf, BETA, -BETA * H0)
+        lin(["tb"], ["d1b"], slot(1, 1), hb, BETA, -BETA * H0)
         if t == 0:
-            zero_columns()
-        for b in range(4 if t else 1):
-            second_copy(b)
-        V(["tf", "o"], ["l1"], "tt", K(7), T.t2[:, 10:C:16], K(4), A.subtract)
+            later_constants()
+            p_copy(0)
+        else:
+            for b in range(1, 4):
+                p_copy(b)
+        V(["tf"] + cn[0], ["rf"], "sc", T.r2[:, 0:C - 1], T.t2[:, 0:C - 1], T.c2[:, 0:C - 1], float(BIG), A.min, A.add)
+        V(["tb"] + cn[1], ["rb"], "sc", T.r2[:, C:2 * C - 1], T.t2[:, C:2 * C - 1], T.c2[:, C:2 * C - 1], float(BIG), A.min, A.add)
+        for i in range(2):
+            V(["rf", "rb"], ["key%d" % i], "tt", T.key[:, 32 * i:32 * i + 32], T.r2[:, 13 + i:C:16], T.r2[:, C + 13 + i:2 * C:16], A.min)
+        if t == 0:
+            V([], ["wc"], "ms", T.w64[:, 63:96:16], FREE)
+        V(["key0", "key1"], ["kt"], "tr", T.kt[:], T.key[:, 0:64])
         if t == 0:
             V(["pA", "pB", "pC", "pD"], ["prm"], "cp", T.prm[:], T.cst[:, PA:PD + 1])
-        V(["tb", "l1"], ["df"], "tt", K(2), T.t2[:, C + 10:2 * C:16], K(7), A.subtract)
-        V(["e2", "jhalf"], ["x"], "tt", K(13), K(JH), T.pm[:, 32:64], A.subtract)
-        V(["l1", "pm"], ["tq"], "tt", K(11), K(7), T.pm[:, 0:32], A.add)
-        V(["x", "pm"], ["t2"], "tt", K(14), K(13), T.pm[:, 0:32], A.add)
-        V(["df", "f9"], ["gg"], "tt", K(10), K(2), K(5), A.mult)
-        V(["l1", "b0"], ["lb"], "tt", K(12), K(7), K(6), A.add)
-        V(["tq", "t2"], ["q"], "tt", K(15), K(14), K(11), A.subtract)
-        V(["lb", "gg"], ["l"], "tt", K(9), K(12), K(10), A.add)
-        V(["q", "d2"], ["q2"], "tt", K(16), K(15), K(8), A.add)
-        V(["l", "q"], ["of"], "tt", T.key[:, 0:32], K(9), K(15), A.add)
-        V(["l", "q2"], ["wf"], "tt", T.key[:, 32:64], K(9), K(16), A.add)
-        V(["of"], ["kt1"], "tr", T.kt[:, 64:96], T.key[:, 0:32])
-        V(["of", "wf"], ["kt0"], "tr", T.kt[:, 0:64], T.key[:, 0:64])
+            V(["wa", "wb2", "wc"], ["wrm0"], "tt", T.wrm[:, 0:16], T.w64[:, 80:96], T.w64[:, 32:48], A.subtract)
+        V(["kt"], ["rot"], "tr", T.key[:, 64:128], T.kt[:, ::-1])
         if t == 0:
-            V(["wa", "wb"], ["wrp0"], "tt", T.wrp[:, 0:64], T.w64[:, 0:64], T.w64[:, 64:128], A.add)
-        V(["kt0", "kt1"], ["rot"], "tr", T.key[:, 64:128], T.kt[:, 16:80])
+            V(["wa", "wb0", "wb1", "wc"], ["wrp0"], "tt", T.wrp[:, 0:32], T.w64[:, 48:80], T.w64[:, 0:32], A.subtract)
+        V(["key0", "key1", "rot", "prm"], ["ow"], "ts", T.ow[:], T.key[:].indirect(T.prm[:]), -1.0 / BETA, float(CC + LK + TM), A.mult, A.min)
+        tabs = ["tabc"] + ["tabv%d" % i for i in range(4)]
         if t == 0:
-            V(["wrp0"], ["wrp1"], "cp", T.wrp[:, 64:128], T.wrp[:, 0:64])
-        V(["of", "wf", "rot", "prm"], ["ow"], "cp", T.ow[:], T.key[:].indirect(T.prm[:]))
+            V([], ["pd0"], "ms", T.pw[:, D0:PL:4], 0.0)
+            for b in range(1, 4):
+                p_copy(b)
+                spread("wrm", T.wrm, 16, b - 1)
+                spread("wrp", T.wrp, 32, b - 1)
+            spread("wrp", T.wrp, 32, 3)
+        V(["ow", "vala", "valb"], tabs, "cp", T.tab[:].indirect(T.ow[:, 0:32]), T.val[:])
         if t == 0:
-            V(["wrp1"], ["wrp2"], "cp", T.wrp[:, 128:256], T.wrp[:, 0:128])
-        tabs = ["tabc", "tabo"] + ["tabv%d" % i for i in range(4)]
-        V(["ow", "val"], tabs, "cp", T.tab[:].indirect(T.ow[:, 0:32]), T.val[:])
-        if t == 0:
-            V(["i16", "jwc"], ["j16"], "ts", K(J16), T.jw[:, 32:64], col(I16), None, A.add)
+            V([], ["pd1"], "ms", T.pw[:, PL + D0:2 * PL:4], 0.0)
         op("a", tabs + ["ow"], ["gpa"], "ac", T.gp[:, 0:16 * GA], T.tab[:].indirect(T.ow[:, 32:32 + GA]), AF.Copy)
-        V(tabs + ["wrp0"], ["mw0"], "sc", T.mw[:, 0:TM], T.tab[:, CC - 1:CC - TM - 1:-1], T.wrp[:, 0:TM], FREE, A.min, A.add)
-        V(tabs + ["wrp0"], ["mw1"], "sc", T.mw[:, TM:2 * TM], T.tab[:, CO - 1:CO - TM - 1:-1], T.wrp[:, 0:TM], FREE, A.min, A.add)
+        V(tabs + ["wrm3"], ["mw"], "sc", T.mw[:], T.tab[:, CC - TM:CC + TM], T.wrm[:], FREE, A.min, A.add)
         if t == 0:
-            V(["wrp2"], ["wrp3"], "cp", T.wrp[:, 256:512], T.wrp[:, 0:256])
-        V(["mw0", "mw1", "cv"], ["ml"], "ts", T.ml[:], T.mw[:, 15:128:16], col(CV), None, A.add)
+            V(["cf", "jc"], ["j16"], "ts", K(J16), K(JC), col(XX), None, A.add)
+        V(["mw"], ["ml"], "ts", T.ml[:], T.mw[:, 15:128:16], HOLD - FREE - ZV, None, A.add)
         for b in (2, 3):
             op("a", ["ml"] + pls(b), ["mt%d" % b], "ac", T.mt[:, b:512:4], plane(b).indirect(T.ml[:]), AF.Copy)
         for b in (0, 1):
@@ -350,43 +357,48 @@ def rank_program(g, core, T, topo):
         order("p", ["mq%d" % t], [])
         for src, dst, cast in ((mq, lq, bytes_of), (ms_, ls, lambda v: v)):
             trs = []
-            for d, c0, c1 in nb:
+            for d, c0 in nb:
                 rid, pid, _ = topo.addr(d)
                 trs.append(RemoteDMATransfer(dst_ids=[DstId(rid=rid, pnc=pid)], dma_engine_mask=sum(1 << e for e in mine[d]),
-                                             remote_sem=T.sem["arr%d" % t], src=cast(src[:, c0:c0 + TM]), dst=cast(dst[:, c1:c1 + TM])))
+                                             remote_sem=T.sem["arr%d" % t], src=cast(src[:, c0:c0 + TM]), dst=cast(dst[:, c0:c0 + TM])))
                 sent[0] += len(mine[d])
             g.remote_dma_fused(trs, local_sem=T.sem.sent)
-        op("a", tabs + ["ow"], ["gpb"], "ac", T.gp[:, 16 * GA:C], T.tab[:].indirect(T.ow[:, 32 + GA:64]), AF.Copy)
+        op("a", tabs + ["ow"], ["gpb"], "ac", T.gp[:, 16 * GA:16 * GB], T.tab[:].indirect(T.ow[:, 32 + GA:32 + GB]), AF.Copy)
+        V(tabs + ["ow"], ["gpc"], "cp", T.gp[:, 16 * GB:C], T.tab[:].indirect(T.ow[:, 32 + GB:64]))
         if t == 0:
             clear_lists()
-            for b in (1, 2, 3):
-                second_copy(b)
-            V(["et%d" % b for b in range(4)], ["eq"], "qz", T.eq[:], T.es[:], T.et[:])
-        else:
-            V(["vt"], ["vq"], "qz", T.vq[:], T.vs[:], T.vt[:])
-        V(["gpa", "gpb", "wrp3"], ["gw"], "sc", T.gw[:], T.gp[:], T.wrp[:], FREE, A.min, A.add)
-        V(["gw", "cv"], ["lst"], "ts", T.lst[:], T.gw[:, 15:C:16], col(CV), None, A.add)
-        V(["gw", "cv"], ["lc"], "ts", K(0), T.gw[:, 15:C:16], col(CV), None, A.add)
-        V(["gw", "cv"], ["lf"], "ts", K(1), T.gw[:, 15:C:16], col(CV), float(D0), A.add, A.is_ge)
-        V(["lst", "pc0"] + pls(0), ["x00"], "tt", T.x0[:, P0:D0], plane(0).indirect(T.lst[:]), T.pc[:, 0:C], A.add)
-        V(["lc", "lf"], ["lg"], "tt", K(2), K(0), K(1), A.mult)
-        V(["lst", "pc1"] + pls(1), ["x01"], "tt", T.x0[:, PL + P0:PL + D0], plane(1).indirect(T.lst[:]), T.pc[:, C:2 * C], A.add)
-        V(["lg", "j16"], ["lh"], "tt", K(17), K(2), K(J16), A.max)
-        order("t", ["eq", "zl%d" % t, "zm%d" % t], [])
+            if edge:
+                V(["zt"], ["zq"], "qz", T.zq[:], T.zs[:], T.zt[:])
+                z0 = nb[0][1]
+                for i in range(R):
+                    dma("s", ["zq"], ["zl%d" % i], bytes_of(T["lq%d" % i][:, z0:z0 + TM]), bytes_of(T.zq[:, 0:TM]))
+                    dma("s", ["zq"], ["zm%d" % i], T["ls%d" % i][:, z0:z0 + TM], T.zs[:, 0:TM])
+        V(["gpa", "gpb", "gpc", "wrp4"], ["gw"], "sc", T.gw[:], T.gp[:], T.wrp[:], FREE, A.min, A.add)
+        V(["gw"], ["lst"], "ts", T.lst[:], T.gw[:, 15:C:16], HOLD - FREE - ZV, None, A.add)
+        V(["gw"], ["l2"], "ts", K(L2), T.gw[:, 15:C:16], 2.0, 2 * (HOLD - FREE) + X0 - 2 * AV, A.mult, A.add)
+        V(["lst", "pc0"] + pls(0), ["x00"], "tt", T.x0[:, P0:P0 + C], plane(0).indirect(T.lst[:]), T.pc[:, 0:C], A.add)
+        V(["l2", "j16"], ["l3"], "tt", K(L3), K(L2), K(J16), A.max)
+        V(["lst", "pc1"] + pls(1), ["x01"], "tt", T.x0[:, XL + P0:XL + P0 + C], plane(1).indirect(T.lst[:]), T.pc[:, C:2 * C], A.add)
+        V(["l3"], ["lst2"], "cp", T.lst2[:], K(L3))
+        if t == 0:
+            for b in (2, 0, 3, 1):
+                e0 = 528 * (b % 2) + 2 - b // 2 * 2
+                V(["et%d" % (b % 2)], ["eq%d" % b], "qz", T.eq[:, 128 * b:128 * b + 128], T.es[:, 128 * b:128 * b + 128], T.et[:, e0:e0 + 512])
+        order("t", ["zl%d" % t, "zm%d" % t], [])
         wait("t", "arr%d" % t, arrive)
         for b in (2, 0, 3, 1):
-            op("t", ["eq"], ["psp%d" % b], "mm", bank(b, 128),
+            op("t", ["eq%d" % b], ["psp%d" % b], "mm", bank(b, 128),
                T.eq[:, 128 * b:128 * b + 128], T.es[:, 128 * b:128 * b + 128], lq[:], ls[:], True, True)
         for b in (2, 3):
-            op("a", [], ["psp%d" % b, "pd%d" % b], "ac", T.pw[:, b * PL + D0:(b + 1) * PL:2], bank(b, 128), AF.Copy)
-        V(["lh"], ["lst2"], "cp", T.lst2[:], K(17))
+            op("a", [], ["psp%d" % b, "pd%d" % b], "ac", T.pw[:, b * PL + D0:(b + 1) * PL:4], bank(b, 128), AF.Copy)
         for b in (0, 1):
-            V(["mt%d" % b], ["psp%d" % b, "fx%d" % b], "tt", T.x0[:, b * PL + D0:(b + 1) * PL:2], T.mt[:, b:512:4], bank(b, 128), A.add)
+            V(["mt%d" % b], ["psp%d" % b, "fx%d" % b], "tt", T.x0[:, b * XL + X0:b * XL + X0 + 8 * 127 + 1:8],
+              T.mt[:, 508 + b::-4], bank(b, 128), A.add)
         nq, ns = T["aq%d" % (t + 1)], T["as%d" % (t + 1)]
         for h, (c0, c1) in enumerate(PARTS[t + 1]):
             for b in (0, 1):
                 op("a", ["lst2", "x0%d" % b, "fx%d" % b], ["xn%d_%d" % (h, b)], "ac", T.xn[:, 4 * c0 + b:4 * c1:4],
-                   T.x0[:, b * PL:(b + 1) * PL].indirect(T.lst2[:, c0 // 16:c1 // 16]), AF.Copy)
+                   T.x0[:, b * XL:(b + 1) * XL].indirect(T.lst2[:, c0 // 16:c1 // 16]), AF.Copy)
         for h, (c0, c1) in enumerate(PARTS[t + 1]):
             for b in (2, 3):
                 V(["lst", "pc%d" % b] + pls(b), ["xn%d_%d" % (h, b)], "tt", T.xn[:, 4 * c0 + b:4 * c1:4],
@@ -395,6 +407,8 @@ def rank_program(g, core, T, topo):
             V(["xn%d_%d" % (h, b) for b in range(4)], names, "qz", nq[:, c0:c1], ns[:, c0:c1], T.xn[:, 4 * c0:4 * c1])
             if t < R - 1:
                 scores(t + 1, h)
+                if h == 1:
+                    V(["vt"], ["vq"], "qz", T.vq[:], T.vs[:], T.vt[:])
             else:
                 dma("s", names, [], T.oc[:, 4 * c0:4 * c1], bytes_of(nq[:, c0:c1]))
                 op("t", names + ["vq"], ["psy%d" % h], "mm", T.psy[:, 512 * h:512 * h + c1 - c0], T.vq[:], T.vs[:], nq[:, c0:c1], ns[:, c0:c1], True, True)

@@ -15,11 +15,12 @@ LK = DP - 1
 TAB = CC + LK + TM + 1
 BETA = 2.0 ** -15
 H0 = -1000.0
-BIG = 3000
+BIG = 3000.0
 TINY = 2.0 ** -120
 HOLD, FREE = 1296.0, 2592.0
-PARTS = (((0, 256), (256, C)), ((0, 384), (384, C)), ((0, 384), (384, C)))
-GA, GB = 8, 22
+PARTS = (((0, 256), (256, 384), (384, C)), ((0, 320), (320, C)), ((0, 256), (256, 384), (384, C)))
+GA, GB, GC, GD, GE = 8, 22, 24, 26, 28
+MV = 16
 F4, U8 = "float8_e4m3fn_x4", "uint8"
 
 
@@ -31,20 +32,19 @@ SCRATCH = {
     "xt": _sb(4 * C, "bfloat16"), "ut": _sb(512, "bfloat16"), "vt": _sb(512, "bfloat16"),
     "uq": _sb(128, F4), "us": _sb(128, U8), "uq2": _sb(128, F4), "us2": _sb(128, U8),
     "vq": _sb(128, F4), "vs": _sb(128, U8), "wq": _sb(512, F4), "wsc": _sb(512, U8),
-    "et": _sb(1056, "bfloat16"), "eq": _sb(512, F4), "es": _sb(512, U8),
-    "zt": _sb(512, "bfloat16"), "zq": _sb(128, F4), "zs": _sb(128, U8), "ones": _sb(516, "bfloat16"),
-    "ui": _sb(8, "int32"), "ul": _sb(8, "uint16"),
-    "pi": _sb(16, "int32"), "cst": _sb(48, "float32"), "w64": _sb(144, "float32"),
+    "et": _sb(1056, "bfloat16"), "eq": _sb(512, F4), "es": _sb(512, U8), "ones": _sb(516, "bfloat16"),
+    "jp": _sb(32, "float32"), "wd": _sb(64, "float32"), "wa": _sb(64, "bfloat16"), "wb": _sb(64, "bfloat16"),
+    "ui": _sb(8, "int32"), "ul": _sb(8, "uint16"), "pi": _sb(16, "int32"), "cst": _sb(48, "float32"),
     "jf": _sb(256, "float32"), "jh": _sb(256, "float32"), "jr": _sb(256, "float32"), "flo": _sb(C, "float16"),
     "prm": _sb(4, "uint16"), "c2": _sb(2 * C, "float32"),
     "wrp": _sb(C, "bfloat16"), "wrm": _sb(128, "bfloat16"), "val0": _sb(C, "bfloat16"), "val": _sb(C, "bfloat16"), "tab": _sb(TAB, "bfloat16"),
     "sg": _sb(C, "bfloat16"), "y2": _sb(2 * C, "float16"), "t2": _sb(2 * C, "float16"), "r2": _sb(2 * C, "float32"),
     "k": _sb(32 * 14, "float32"), "key": _sb(128, "float32"), "kt": _sb(64, "float32"),
-    "ow": _sb(64, "uint16"), "lst": _sb(32, "uint16"), "lst2": _sb(32, "uint16"), "ml": _sb(8, "uint16"),
+    "ow": _sb(32, "uint16"), "ow1": _sb(32, "uint16"), "lst": _sb(32, "uint16"), "lst2": _sb(32, "uint16"), "ml": _sb(32, "uint16"),
     "mw": _sb(128, "float16"), "gp": _sb(C, "bfloat16"), "gw": _sb(C, "float16"),
     "pw": _sb(4 * PL, "bfloat16"), "pc": _sb(4 * C, "bfloat16"), "x0": _sb(2 * XL, "bfloat16"),
     "mt": _sb(512, "bfloat16"), "xn": _sb(4 * C, "bfloat16"), "ysb": _sb(C, "float32"),
-    "pss": ("psum", [128, 1024], "float32"), "psp": ("psum", [128, 2048], "float32"), "psy": ("psum", [128, 1024], "float32"),
+    "pss": ("psum", [128, 1024], "float32"), "psp": ("psum", [128, 2048], "float32"), "psy": ("psum", [128, 512], "float32"),
 }
 for _t in range(R + 1):
     SCRATCH["aq%d" % _t] = _sb(C, F4)
@@ -54,7 +54,7 @@ for _t in range(R):
         SCRATCH["%sq%d" % (_n, _t)] = _sb(128, F4)
         SCRATCH["%ss%d" % (_n, _t)] = _sb(128, U8)
 
-NDMA = 32
+NDMA = 36
 SEMAPHORES = ["v", "a", "t", "p", "sent"] + ["arr%d" % _t for _t in range(R)] + ["d%d" % _i for _i in range(NDMA)]
 
 
@@ -138,7 +138,8 @@ def rank_program(g, core, T, topo):
 
     col = lambda i: T.cst[:, i:i + 1]
     K = lambda i: T.k[:, 32 * i:32 * i + 32]
-    XX, AA, EE, EV, E9, PW, C1, MG, OA, OB, OC, OD, OFF, INC, YP, YQ, Y0, M1, X1, X2, X3, PA, PB, PC, PD, YX, YA = range(5, 32)
+    XX, AA, EE, EV, QA, QB, E9, PW, C1, MG, OA, OB, OC, OD, OFF, INC, Y0, M1, X1, X2, MN, PA, PB, PC, PD, INI, YA = range(5, 32)
+    QC = 42
     KF, KB, JW, JF, J16, JC, L2, L3 = 0, 1, 2, 3, 4, 5, 6, 7
     KG = lambda u: K(8 + u - 5)
     slot = lambda d, pos: T.c2[:, d * C + pos:(d + 1) * C:16]
@@ -146,8 +147,8 @@ def rank_program(g, core, T, topo):
 
     dma("s", [], ["ut"], T.ut[:], T.u[:])
     for h, (c0, c1) in enumerate(PARTS[0]):
-        dma("as"[h], [], ["xt%d" % h], T.xt[:, 4 * c0:4 * c1], T.x[:, 4 * c0:4 * c1])
-    dma("s", [], ["wq"], bytes_of(T.wq[:]), T.wc[:])
+        dma("asa"[h], [], ["xt%d" % h], T.xt[:, 4 * c0:4 * c1], T.x[:, 4 * c0:4 * c1])
+    dma("s", ["xt0", "xt1", "xt2"], ["wq"], bytes_of(T.wq[:]), T.wc[:])
     dma("s", [], ["wsc"], T.wsc[:], T.ws[:])
     dma("s", [], ["vt"], T.vt[:], T.v[:])
 
@@ -159,29 +160,28 @@ def rank_program(g, core, T, topo):
     op("p", [], ["ui"], "io", T.ui[:], [[16, 8]], 0, 0)
     iota(["jw"], K(JW), [[32, 16], [0, 2]], 0, 0)
     iota(["val0a"], T.val0[:, 0:256], [[32, 16], [1, 16]], -256, 0)
-    iota(["val0b"], T.val0[:, 256:C], [[32, 16], [-1, 16]], 31 - 256, 0)
     for u in range(5, 9):
         pat = [[0, 1 << (8 - u)], [1 << u, 2], [0, 2 << (u - 5)]]
         iota(["kg%d" % u], KG(u), pat[1:] if u == 8 else pat, 0, 0)
-    iota(["s0"], T.c2[:, 0:2 * C:16], [[0, 64]], BIG, 0)
-    iota(["s15"], T.c2[:, 15:2 * C:16], [[0, 64]], 0, 0)
-    iota(["tabv1"], T.tab[:, CC - LK - TM:CC - LK], [[-4, TM]], AV + 4 * (2 * TM - 1), 0)
-    iota(["tabv3"], T.tab[:, CC + LK:CC + LK + TM], [[-4, TM]], AV + 4 * (TM - 1), 0)
+    iota(["val0b"], T.val0[:, 256:C], [[32, 16], [-1, 16]], 31 - 256, 0)
+    iota(["jpb"], T.jp[:], [[0, 8], [4, 4]], 0, 0)
+    for name, c0, v0, there in (("tabv1", CC - LK - TM, 2 * TM - 1, rank > 0), ("tabv3", CC + LK, TM - 1, rank < n_ranks - 1)):
+        iota([name], T.tab[:, c0:c0 + TM], [[-4 if there else 0, TM]], AV + 4 * v0 if there else int(ZV), 0)
     clear_lists()
+    iota(["tabv0"], T.tab[:, CC - LK - C:CC - LK - TM], [[0, C - TM]], int(ZV), 0)
     iota(["jc"], K(JC), [[16, 32]], P0, 0)
-    if edge:
-        iota(["zt"], T.zt[:], [[0, 512]], 0, 0)
+    for b in range(2):
+        iota(["pd%d" % b], T.pw[:, b * PL + D0:(b + 1) * PL:4], [[0, 2 * TM]], 0, 0)
 
-    V([], ["kf"], "ms", K(KF), -up)
-    V([], ["kb"], "ms", K(KB), dn)
-    V([], ["s14f"], "ms", slot(0, 14), BETA * LK)
+    V([], ["ones"], "ms", T.ones[:], 1.0)
     V(["pi"], ["pe"], "ts", T.pi[:, 9:10], T.pi[:, 1:2], 15, None, A.bitwise_and)
     V(["pi"], ["px"], "ts", T.pi[:, 7:8], T.pi[:, 0:1], 15, None, A.bitwise_and)
     V(["pe"], ["e9"], "ts", col(E9), T.pi[:, 9:10], 9.0, None, A.min)
-    for u, m in ((2, 1), (3, 2), (4, 4), (5, 8), (6, 16), (8, 31), (10, 14)):
+    bits = ((2, 1), (3, 2), (4, 4), (5, 8), (6, 16), (8, 31), (10, 14), (11, 12), (12, 3))
+    for u, m in bits:
         V(["pi"], ["pb%d" % u], "ts", T.pi[:, u:u + 1], T.pi[:, 0:1], m, None, A.bitwise_and)
     V(["jf", "e9"], ["tw"], "ts", T.cst[:, 32:41], T.jf[:, 0:9], col(E9), 1.0, A.is_lt, A.add)
-    V(["pe", "px"] + ["pb%d" % u for u in (2, 3, 4, 5, 6, 8, 10)], ["cf"], "cp", T.cst[:, 0:9], T.pi[:, 2:11])
+    V(["pe", "px"] + ["pb%d" % u for u, _ in bits], ["cf"], "cp", T.cst[:, 0:11], T.pi[:, 2:13])
     V(["tw"], ["pwc"], "rd", col(PW), T.cst[:, 32:41], AxisListType.X, A.mult)
     V(["e9"], ["oa"], "ts", col(OA), col(E9), 9.0, -1256.0, A.not_equal, A.mult)
     V(["cf"], ["ob"], "ts", col(OB), col(XX), 0.0, -3000.0, A.is_equal, A.mult)
@@ -190,70 +190,62 @@ def rank_program(g, core, T, topo):
     V(["oa", "ob", "oc"], ["od"], "ts", col(OD), col(OA), col(OB), col(OC), A.add, A.add)
     V(["cf", "jw"], ["jj"], "ts", K(JF), K(JW), col(AA), None, A.add)
     V(["ui"], ["ul"], "cp", T.ul[:], T.ui[:])
-    V([], ["s14b"], "ms", slot(1, 14), -BETA * LK)
-    V([], ["s1f"], "ms", slot(0, 1), 0.0)
-    V([], ["s2f"], "ms", slot(0, 2), 0.0)
-    V([], ["pz"], "ms", T.pw[:, 0:4 * PL:PL], 0.0)
-    V([], ["tabv2"], "ms", T.tab[:, CC + LK + TM:CC + LK + TM + 1], ZV)
-    V([], ["ones"], "ms", T.ones[:], 1.0)
     for i in range(2):
         op("p", ["ones"], ["et%d" % i], "as", T.et[:, 528 * i:528 * i + 516], T.ones[:], [[-1, 516]], A.is_equal, 0.0, 2 + i, 4)
+    for name, out, n, v in (("kf", K(KF), 32, -up), ("kb", K(KB), 32, dn), ("s14f", slot(0, 14), 32, BETA * LK), ("s14b", slot(1, 14), 32, -BETA * LK),
+                            ("s1f", slot(0, 1), 32, 0.0), ("s2f", slot(0, 2), 32, 0.0), ("pz", T.pw[:, 0:4 * PL:PL], 4, 0.0),
+                            ("tabv2", T.tab[:, TAB - 1:TAB], 1, ZV)):
+        lin(["jf"], [name], out, T.jf[:, 0:n], 0.0, v)
     lin(["pwc"], ["c1"], col(C1), col(PW), -0.5, 0.5)
     lin(["pwc"], ["mg"], col(MG), col(PW), 1.5 * 2.0 ** 23, 0.0)
-    lin(["jf", "c1"], ["jh"], T.jh[:], T.jf[:], 1.0, col(C1))
+    lin(["jf", "c1"], ["jh", "jq"], T.jh[:], T.jf[:], 1.0, col(C1))
     lin(["od"], ["off"], col(OFF), col(OD), 1.0, 1000.0)
-    lin(["jh", "mg"], ["jr"], T.jr[:], T.jh[:], 1.0, col(MG))
-    for u in range(5):
-        lin(["cf", "kf"], ["sf%d" % u], slot(0, 4 + u), K(KF), col(u), BETA * S)
-        lin(["cf", "kb"], ["sb%d" % u], slot(1, 4 + u), K(KB), col(u), BETA * S - dn * (1 << u))
+    lin(["jh", "jq", "mg"], ["jr"], T.jr[:], T.jh[:], 1.0, col(MG))
 
     def high_steps():
         for u in range(5, 9):
-            last = u == 8
-            lin(["kg%d" % u], ["sf%d" % u], slot(0, 4 + u), KG(u), -up, 257.0 - BETA * (8 * S + DP) if last else BETA * S)
+            lin(["kg%d" % u], ["sf%d" % u], slot(0, 4 + u), KG(u), -up, 257.0 - BETA * (8 * S + DP) if u == 8 else BETA * S)
+        for u in range(5):
+            lin(["cf", "kb"], ["sb%d" % u], slot(1, 4 + u), K(KB), col(u), BETA * S - dn * (1 << u))
+        for u in range(5, 9):
             lin(["kg%d" % u], ["sb%d" % u], slot(1, 4 + u), KG(u), dn,
-                (257.0 - BETA * (8 * S + 1024) if last else BETA * S) - dn * (1 << u))
+                (257.0 - BETA * (8 * S + 1024) if u == 8 else BETA * S) - dn * (1 << u))
+        lin(["jj"], ["s3b"], slot(1, 3), K(JF), -dn, 511 * dn - 256.0 - BETA * (CC - 1025))
 
     cn = [["s0", "s15", "s1f", "s2f", "s3f", "s14f", "d13f"] + ["sf%d" % u for u in range(9)],
           ["s0", "s15", "s3b", "s14b", "d13b", "d1b", "d2b"] + ["sb%d" % u for u in range(9)]]
     V(["ut"], ["uq"], "qz", T.uq[:], T.us[:], T.ut[:])
-    V(["jr", "mg", "off"], ["floa"], "ts", T.flo[:, 0:256], T.jr[:], col(MG), col(OFF), A.subtract, A.add)
     V(["uq", "ul"], ["uq2"], "cp", T.uq2[:].bitcast(dt.uint32), T.uq[:].bitcast(dt.uint32).indirect(T.ul[:]))
     op("a", ["uq", "ul"], ["us2"], "ac", T.us2[:], T.us[:].indirect(T.ul[:]), AF.Copy)
+    for u in range(5):
+        lin(["cf", "kf"], ["sf%d" % u], slot(0, 4 + u), K(KF), col(u), BETA * S)
     lin(["jj"], ["s3f"], slot(0, 3), K(JF), up, -256.0 - BETA * (CC - DP))
-    lin(["jj"], ["s3b"], slot(1, 3), K(JF), -dn, 511 * dn - 256.0 - BETA * (CC - 1025))
-    lin(["cf"], ["m1"], col(M1), col(4), 1.0 / 16, 0.0)
-    lin(["cf"], ["n2"], col(Y0), col(4), -2.0, 0.0)
-    act(["cf"], ["ya"], col(YA), col(AA), AF.Abs, 1.0, -15.5)
-    lin(["cf"], ["yx"], col(YX), col(XX), -1.0, 0.0)
     for h, (c0, c1) in enumerate(PARTS[0]):
         V(["xt%d" % h], ["a0h%d" % h], "qz", T.aq0[:, c0:c1], T.as0[:, c0:c1], T.xt[:, 4 * c0:4 * c1])
+    V(["jr", "mg", "off"], ["floa"], "ts", T.flo[:, 0:256], T.jr[:], col(MG), col(OFF), A.subtract, A.add)
+    V([], ["s0"], "ms", T.c2[:, 0:2 * C:16], BIG)
     V(["floa", "inc"], ["flob"], "ts", T.flo[:, 256:C], T.flo[:, 0:256], col(INC), None, A.add)
-    V([], ["tabv0"], "ms", T.tab[:, CC - LK - C:CC - LK - TM], ZV)
     V(["val0a", "cf"], ["vala"], "ts", T.val[:, 0:256], T.val0[:, 0:256], col(4), None, A.add)
-    V(["val0b", "cf"], ["valb"], "ts", T.val[:, 256:C], T.val0[:, 256:C], col(4), None, A.subtract)
+    V([], ["s15"], "ms", T.c2[:, 15:2 * C:16], 0.0)
 
     def late_constants():
+        lin(["cf"], ["m1"], col(M1), col(4), 1.0 / 16, 0.0)
+        lin(["cf"], ["n2"], col(Y0), col(4), -2.0, 0.0)
+        act(["cf"], ["ya"], col(YA), col(AA), AF.Abs, 1.0, -15.5)
         lin(["cf", "m1"], ["pA"], col(PA), col(XX), 2.0, col(M1))
         lin(["cf", "m1"], ["x2"], col(X2), col(EV), 1.0, col(M1))
         act(["cf", "n2"], ["x1"], col(X1), col(0), AF.Abs, 32.0, col(Y0))
-        lin(["ya"], ["yp"], col(YP), col(YA), 1.0, -15.5)
-        lin(["ya"], ["yq"], col(YQ), col(YA), -1.0, 0.5)
-
-    def later_constants():
-        lin(["x1", "x2"], ["x3"], col(X3), col(X1), 1.0, col(X2))
-        lin(["pA"], ["pB"], col(PB), col(PA), 1.0, 96.0)
-        for i, y in enumerate((YP, YQ, YX)):
-            act(["jf", "yp", "yq", "yx"], ["wd%d" % i], T.w64[:, 96 + 16 * i:112 + 16 * i], T.jf[:, 0:16], AF.Abs, 1.0, col(y))
-        lin(["x3"], ["pC"], col(PC), col(X3), 1.0, 32.0)
-        lin(["x3"], ["pD"], col(PD), col(X3), 1.0, 48.0)
-        act(["wd0", "wd1", "wd2"], ["wa"], T.w64[:, 0:48], T.w64[:, 96:144], AF.Relu, -HOLD, HOLD)
-        for i in range(3):
-            act(["wd%d" % i], ["wb%d" % i], T.w64[:, 48 + 16 * i:63 + 16 * i], T.w64[:, 97 + 16 * i:112 + 16 * i], AF.Relu, -FREE, FREE)
-
-    def spread(name, buf, n0, i):
-        n0 = n0 << i
-        op("a", ["%s%d" % (name, i)], ["%s%d" % (name, i + 1)], "ac", buf[:, n0:2 * n0], buf[:, 0:n0], AF.Copy)
+        act(["jf"], ["jq"], T.jh[:, 0:32], T.jf[:, 0:32], AF.Abs, 1.0, -15.5)
+        lin(["pA"], ["pB"], col(PB), col(PA), 1.0, 32.0)
+        lin(["x1", "x2"], ["pC"], col(PC), col(X1), 1.0, col(X2))
+        act(["jq", "ya"], ["wd0"], T.wd[:, 0:32], T.jh[:, 0:32], AF.Abs, -1.0, col(YA))
+        act(["jpb", "cf"], ["wd1"], T.wd[:, 32:64], T.jp[:], AF.Abs, -1.0, col(QA))
+        lin(["pC"], ["pD"], col(PD), col(PC), 1.0, 16.0)
+        lin(["cf"], ["mn"], col(MN), col(4), -1.0, 0.0)
+        act(["wd0", "wd1"], ["wb"], T.wb[:, 0:63], T.wd[:, 1:64], AF.Relu, -FREE, FREE)
+        act(["wd0", "wd1"], ["wa"], T.wa[:], T.wd[:], AF.Relu, -HOLD, HOLD)
+        lin(["val0b", "mn"], ["valb"], T.val[:, 256:C], T.val0[:, 256:C], 1.0, col(MN))
+        lin(["cf"], ["qc"], col(QC), col(QB), float(PL), HOLD - FREE - ZV)
 
     def masks(c):
         r = T.rank_of(c)
@@ -277,83 +269,113 @@ def rank_program(g, core, T, topo):
     plane = lambda b: T.pw[:, b * PL:(b + 1) * PL]
     bank = lambda b, n: T.psp[:, 512 * b:512 * b + n]
     pls = lambda b: ["pw%d" % b, "pz", "pd%d" % b]
+    pall = ["pw%d" % b for b in range(4)] + ["pz"] + ["pd%d" % b for b in range(4)]
+    tabs = ["tabc"] + ["tabv%d" % i for i in range(4)]
+
+    def out_bank(h, n):
+        return ((T.pss[:, 0:n], "pss0"), (T.pss[:, 512:512 + n], "pss1"), (T.psy[:, 0:n], "psy0"))[h]
 
     def scores(t, h):
         c0, c1 = PARTS[t][h]
-        op("t", ["a%dh%d" % (t, h), "uq2", "us2"], ["pss%d" % h], "mm", T.pss[:, 512 * h:512 * h + c1 - c0], T.uq2[:], T.us2[:],
+        ps, name = out_bank(h, c1 - c0)
+        op("t", ["a%dh%d" % (t, h), "uq2", "us2"], [name], "mm", ps, T.uq2[:], T.us2[:],
            T["aq%d" % t][:, c0:c1], T["as%d" % t][:, c0:c1], True, True)
 
     def p_copy(b):
         op("a", [], ["psp%d" % b, "pw%d" % b], "ac", T.pw[:, b * PL + P0:b * PL + P0 + C], bank(b, C), AF.Copy, scale=0.0625)
         dma("s", ["pw%d" % b], ["pc%d" % b], T.pc[:, b * C:(b + 1) * C], T.pw[:, b * PL + P0:b * PL + P0 + C])
 
-    scores(0, 0)
-    scores(0, 1)
+    def spread(name, buf, i):
+        n0 = 32 << i
+        op("a", ["%s%d" % (name, i)], ["%s%d" % (name, i + 1)], "ac", buf[:, n0:2 * n0], buf[:, 0:n0], AF.Copy)
+
+    def unit(b):
+        e0 = 528 * (b % 2) + 2 - b // 2 * 2
+        V(["et%d" % (b % 2)], ["eq%d" % b], "qz", T.eq[:, 128 * b:128 * b + 128], T.es[:, 128 * b:128 * b + 128], T.et[:, e0:e0 + 512])
+
+    def partners(q, name, c0, c1):
+        src = T.tab[:].indirect(T.ow1[:, c0:c1])
+        if q == "a":
+            op("a", tabs + ["ow1"], [name], "ac", T.gp[:, 16 * c0:16 * c1], src, AF.Copy)
+        else:
+            V(tabs + ["ow1"], [name], "cp", T.gp[:, 16 * c0:16 * c1], src)
+
+    for h in range(len(PARTS[0])):
+        scores(0, h)
     for t in range(R):
         aq, asc = T["aq%d" % t], T["as%d" % t]
-        ah = ["a%dh0" % t, "a%dh1" % t]
+        ah = ["a%dh%d" % (t, h) for h in range(len(PARTS[t]))]
         mq, ms_, lq, ls = T["mq%d" % t], T["ms%d" % t], T["lq%d" % t], T["ls%d" % t]
         for b in range(4):
             op("t", ah + ["wq", "wsc"], ["psp%d" % b], "mm", bank(b, C),
                T.wq[:, 128 * b:128 * b + 128], T.wsc[:, 128 * b:128 * b + 128], aq[:], asc[:], True, True)
         for h, (c0, c1) in enumerate(PARTS[t]):
-            op("a", [], ["pss%d" % h, "sg%d" % h], "ac", T.sg[:, c0:c1], T.pss[:, 512 * h:512 * h + c1 - c0], AF.Sign, bias=TINY)
-        sg = ["sg0", "sg1", "floa", "flob"]
+            ps, name = out_bank(h, c1 - c0)
+            op("a", [], [name, "sg%d" % h], "ac", T.sg[:, c0:c1], ps, AF.Sign, bias=TINY)
         if t == 0:
             high_steps()
-            late_constants()
         else:
             p_copy(0)
-        V(sg, ["yf"], "sc", T.y2[:, 0:C], T.flo[:], T.sg[:], H0, A.max, A.add)
-        V(sg, ["yb"], "sc", T.y2[:, 2 * C - 1:C - 1:-1], T.flo[:], T.sg[:, ::-1], H0, A.max, A.subtract)
-        V(["yf"], ["tf"], "tr", T.t2[:, 0:C], T.y2[:, 0:C])
+        cm = PARTS[t][0][1]
+        sg = ["sg0", "sg1", "sg2", "floa", "flob"]
+        back = lambda: V(sg, ["yb"], "sc", T.y2[:, 2 * C - 1:C - 1:-1], T.flo[:], T.sg[:, ::-1], H0, A.max, A.subtract)
+        if t == 0:
+            V(sg, ["yf0", "yf1"], "sc", T.y2[:, 0:C], T.flo[:], T.sg[:], H0, A.max, A.add)
+            back()
+            V(["yf0", "yf1"], ["tf0", "tf1"], "tr", T.t2[:, 0:C], T.y2[:, 0:C])
+        else:
+            V(["sg0"], ["yf0"], "sc", T.y2[:, 0:cm], T.flo[:, 0:cm], T.sg[:, 0:cm], H0, A.max, A.add)
+            V(["yf0"], ["ini"], "cp", col(INI), T.y2[:, cm - 1:cm])
+            V(["yf0"], ["tf0"], "tr", T.t2[:, 0:cm], T.y2[:, 0:cm])
+            V(["sg1", "ini"], ["yf1"], "sc", T.y2[:, cm:C], T.flo[:, cm:C], T.sg[:, cm:C], col(INI), A.max, A.add)
+            back()
+            V(["yf1"], ["tf1"], "tr", T.t2[:, cm:C], T.y2[:, cm:C])
         V(["yb"], ["tb"], "tr", T.t2[:, C:2 * C], T.y2[:, C:2 * C])
+        tf = ["tf0", "tf1"]
         hf, hb = T.t2[:, 0:C:16], T.t2[:, C:2 * C:16]
-        lin(["tf"], ["d13f"], slot(0, 13), hf, -BETA, BETA * H0)
-        lin(["tf"], ["d13b"], slot(1, 13), hf, -BETA, BETA * H0)
-        lin(["tf"], ["d2b"], slot(1, 2), hf, BETA, -BETA * H0)
+        lin(tf, ["d13f"], slot(0, 13), hf, -BETA, BETA * H0)
+        lin(tf, ["d13b"], slot(1, 13), hf, -BETA, BETA * H0)
+        lin(tf, ["d2b"], slot(1, 2), hf, BETA, -BETA * H0)
         lin(["tb"], ["d1b"], slot(1, 1), hb, BETA, -BETA * H0)
         if t == 0:
-            later_constants()
-            p_copy(0)
-        else:
-            for b in range(1, 4):
-                p_copy(b)
-        V(["tf"] + cn[0], ["rf"], "sc", T.r2[:, 0:C - 1], T.t2[:, 0:C - 1], T.c2[:, 0:C - 1], float(BIG), A.min, A.add)
-        V(["tb"] + cn[1], ["rb"], "sc", T.r2[:, C:2 * C - 1], T.t2[:, C:2 * C - 1], T.c2[:, C:2 * C - 1], float(BIG), A.min, A.add)
-        for i in range(2):
-            V(["rf", "rb"], ["key%d" % i], "tt", T.key[:, 32 * i:32 * i + 32], T.r2[:, 13 + i:C:16], T.r2[:, C + 13 + i:2 * C:16], A.min)
-        if t == 0:
-            V([], ["wc"], "ms", T.w64[:, 63:96:16], FREE)
-        V(["key0", "key1"], ["kt"], "tr", T.kt[:], T.key[:, 0:64])
+            late_constants()
+        for b in range(1, 4) if t else range(1):
+            p_copy(b)
+        V(tf + cn[0], ["rf"], "sc", T.r2[:, 0:C - 1], T.t2[:, 0:C - 1], T.c2[:, 0:C - 1], BIG, A.min, A.add)
+        V(["tb"] + cn[1], ["rb"], "sc", T.r2[:, C:2 * C - 1], T.t2[:, C:2 * C - 1], T.c2[:, C:2 * C - 1], BIG, A.min, A.add)
         if t == 0:
             V(["pA", "pB", "pC", "pD"], ["prm"], "cp", T.prm[:], T.cst[:, PA:PD + 1])
-            V(["wa", "wb2", "wc"], ["wrm0"], "tt", T.wrm[:, 0:16], T.w64[:, 80:96], T.w64[:, 32:48], A.subtract)
-        V(["kt"], ["rot"], "tr", T.key[:, 64:128], T.kt[:, ::-1])
+        for i in range(2):
+            V(["rf", "rb"], ["key%d" % i], "tt", T.key[:, 64 * i:64 * i + 32], T.r2[:, 13 + i:C:16], T.r2[:, C + 13 + i:2 * C:16], A.min)
         if t == 0:
-            V(["wa", "wb0", "wb1", "wc"], ["wrp0"], "tt", T.wrp[:, 0:32], T.w64[:, 48:80], T.w64[:, 0:32], A.subtract)
-        V(["key0", "key1", "rot", "prm"], ["ow"], "ts", T.ow[:], T.key[:].indirect(T.prm[:]), -1.0 / BETA, float(CC + LK + TM), A.mult, A.min)
-        tabs = ["tabc"] + ["tabv%d" % i for i in range(4)]
+            V([], ["wb"], "ms", T.wb[:, 35:64:4], FREE)
+        for i in range(2):
+            V(["key%d" % i], ["kt%d" % i], "tr", T.kt[:, 32 * i:32 * i + 32], T.key[:, 64 * i:64 * i + 32])
         if t == 0:
-            V([], ["pd0"], "ms", T.pw[:, D0:PL:4], 0.0)
+            V([], ["wb"], "ms", T.wb[:, 15:32:16], FREE)
+        V(["kt0"], ["rot0"], "tr", T.key[:, 32:64], T.kt[:, 31::-1])
+        V(["kt1"], ["rot1"], "tr", T.key[:, 96:128], T.kt[:, 63:31:-1])
+        if t == 0:
+            V(["wa", "wb"], ["wrm0"], "tt", T.wrm[:, 0:32], T.wb[:, 32:64], T.wa[:, 32:64], A.subtract)
+        V(["key0", "rot0", "prm"], ["ow0"], "ts", T.ow[:], T.key[:, 0:64].indirect(T.prm[:, 0:2]), -1.0 / BETA, None, A.mult)
+        V(["key1", "rot1", "prm"], ["ow1"], "ts", T.ow1[:], T.key[:, 64:128].indirect(T.prm[:, 2:4]), -1.0 / BETA, float(TAB - 1), A.mult, A.min)
+        if t == 0:
+            V(["wa", "wb"], ["wrp0"], "tt", T.wrp[:, 0:32], T.wb[:, 0:32], T.wa[:, 0:32], A.subtract)
             for b in range(1, 4):
                 p_copy(b)
-                spread("wrm", T.wrm, 16, b - 1)
-                spread("wrp", T.wrp, 32, b - 1)
-            spread("wrp", T.wrp, 32, 3)
-        V(["ow", "vala", "valb"], tabs, "cp", T.tab[:].indirect(T.ow[:, 0:32]), T.val[:])
-        if t == 0:
-            V([], ["pd1"], "ms", T.pw[:, PL + D0:2 * PL:4], 0.0)
-        op("a", tabs + ["ow"], ["gpa"], "ac", T.gp[:, 0:16 * GA], T.tab[:].indirect(T.ow[:, 32:32 + GA]), AF.Copy)
-        V(tabs + ["wrm3"], ["mw"], "sc", T.mw[:], T.tab[:, CC - TM:CC + TM], T.wrm[:], FREE, A.min, A.add)
-        if t == 0:
-            V(["cf", "jc"], ["j16"], "ts", K(J16), K(JC), col(XX), None, A.add)
-        V(["mw"], ["ml"], "ts", T.ml[:], T.mw[:, 15:128:16], HOLD - FREE - ZV, None, A.add)
-        for b in (2, 3):
-            op("a", ["ml"] + pls(b), ["mt%d" % b], "ac", T.mt[:, b:512:4], plane(b).indirect(T.ml[:]), AF.Copy)
-        for b in (0, 1):
-            V(["ml"] + pls(b), ["mt%d" % b], "cp", T.mt[:, b:512:4], plane(b).indirect(T.ml[:]))
-        V(["mt%d" % b for b in range(4)], ["mq%d" % t], "qz", mq[:], ms_[:], T.mt[:])
+                if b < 3:
+                    spread("wrm", T.wrm, b - 1)
+                spread("wrp", T.wrp, b - 1)
+        V(["ow0", "vala", "valb"], tabs, "cp", T.tab[:].indirect(T.ow[:]), T.val[:])
+        partners("a", "gpa", 0, GA)
+        V(tabs + ["wrm2"], ["mw"], "sc", T.mw[:], T.tab[:, CC - TM:CC + TM], T.wrm[:], FREE, A.min, A.add)
+        partners("v", "gpc", GB, GC)
+        V(["mw", "qc"], ["ml"], "ts", T.ml[:], T.mw[:, 3:128:4], col(QC), None, A.add)
+        partners("v", "gpd", GC, GD)
+        op("a", ["ml"] + pall, ["mta"], "ac", T.mt[:, 16 * MV:512], T.pw[:].indirect(T.ml[:, MV:32]), AF.Copy)
+        V(["ml"] + pall, ["mtv"], "cp", T.mt[:, 0:16 * MV], T.pw[:].indirect(T.ml[:, 0:MV]))
+        partners("v", "gpe", GD, GE)
+        V(["mta", "mtv"], ["mq%d" % t], "qz", mq[:], ms_[:], T.mt[:])
         order("p", ["mq%d" % t], [])
         for src, dst, cast in ((mq, lq, bytes_of), (ms_, ls, lambda v: v)):
             trs = []
@@ -363,17 +385,20 @@ def rank_program(g, core, T, topo):
                                              remote_sem=T.sem["arr%d" % t], src=cast(src[:, c0:c0 + TM]), dst=cast(dst[:, c0:c0 + TM])))
                 sent[0] += len(mine[d])
             g.remote_dma_fused(trs, local_sem=T.sem.sent)
-        op("a", tabs + ["ow"], ["gpb"], "ac", T.gp[:, 16 * GA:16 * GB], T.tab[:].indirect(T.ow[:, 32 + GA:32 + GB]), AF.Copy)
-        V(tabs + ["ow"], ["gpc"], "cp", T.gp[:, 16 * GB:C], T.tab[:].indirect(T.ow[:, 32 + GB:64]))
+        if edge:
+            z0 = nb[0][1]
+            dma("s", ["mq%d" % t], ["zl%d" % t], bytes_of(lq[:, z0:z0 + TM]), bytes_of(mq[:, z0:z0 + TM]))
+            dma("s", ["mq%d" % t], ["zm%d" % t], ls[:, z0:z0 + TM], ms_[:, z0:z0 + TM])
+        partners("a", "gpb", GA, GB)
+        partners("v", "gpf", GE, 32)
         if t == 0:
+            lin(["cf", "jc"], ["j16"], K(J16), K(JC), 1.0, col(XX))
             clear_lists()
-            if edge:
-                V(["zt"], ["zq"], "qz", T.zq[:], T.zs[:], T.zt[:])
-                z0 = nb[0][1]
-                for i in range(R):
-                    dma("s", ["zq"], ["zl%d" % i], bytes_of(T["lq%d" % i][:, z0:z0 + TM]), bytes_of(T.zq[:, 0:TM]))
-                    dma("s", ["zq"], ["zm%d" % i], T["ls%d" % i][:, z0:z0 + TM], T.zs[:, 0:TM])
-        V(["gpa", "gpb", "gpc", "wrp4"], ["gw"], "sc", T.gw[:], T.gp[:], T.wrp[:], FREE, A.min, A.add)
+            V(["wrp3"], ["wrp4"], "cp", T.wrp[:, 256:C], T.wrp[:, 0:256])
+            unit(2)
+        V(["gpa", "gpb", "gpc", "gpd", "gpe", "gpf", "wrp4"], ["gw"], "sc", T.gw[:], T.gp[:], T.wrp[:], FREE, A.min, A.add)
+        if t == 0:
+            unit(0)
         V(["gw"], ["lst"], "ts", T.lst[:], T.gw[:, 15:C:16], HOLD - FREE - ZV, None, A.add)
         V(["gw"], ["l2"], "ts", K(L2), T.gw[:, 15:C:16], 2.0, 2 * (HOLD - FREE) + X0 - 2 * AV, A.mult, A.add)
         V(["lst", "pc0"] + pls(0), ["x00"], "tt", T.x0[:, P0:P0 + C], plane(0).indirect(T.lst[:]), T.pc[:, 0:C], A.add)
@@ -381,9 +406,8 @@ def rank_program(g, core, T, topo):
         V(["lst", "pc1"] + pls(1), ["x01"], "tt", T.x0[:, XL + P0:XL + P0 + C], plane(1).indirect(T.lst[:]), T.pc[:, C:2 * C], A.add)
         V(["l3"], ["lst2"], "cp", T.lst2[:], K(L3))
         if t == 0:
-            for b in (2, 0, 3, 1):
-                e0 = 528 * (b % 2) + 2 - b // 2 * 2
-                V(["et%d" % (b % 2)], ["eq%d" % b], "qz", T.eq[:, 128 * b:128 * b + 128], T.es[:, 128 * b:128 * b + 128], T.et[:, e0:e0 + 512])
+            unit(3)
+            unit(1)
         order("t", ["zl%d" % t, "zm%d" % t], [])
         wait("t", "arr%d" % t, arrive)
         for b in (2, 0, 3, 1):
@@ -392,33 +416,44 @@ def rank_program(g, core, T, topo):
         for b in (2, 3):
             op("a", [], ["psp%d" % b, "pd%d" % b], "ac", T.pw[:, b * PL + D0:(b + 1) * PL:4], bank(b, 128), AF.Copy)
         for b in (0, 1):
-            V(["mt%d" % b], ["psp%d" % b, "fx%d" % b], "tt", T.x0[:, b * XL + X0:b * XL + X0 + 8 * 127 + 1:8],
+            V(["mta", "mtv"], ["psp%d" % b, "fx%d" % b], "tt", T.x0[:, b * XL + X0:b * XL + X0 + 8 * 127 + 1:8],
               T.mt[:, 508 + b::-4], bank(b, 128), A.add)
         nq, ns = T["aq%d" % (t + 1)], T["as%d" % (t + 1)]
-        for h, (c0, c1) in enumerate(PARTS[t + 1]):
+        parts = PARTS[t + 1]
+        for h, (c0, c1) in enumerate(parts):
             for b in (0, 1):
                 op("a", ["lst2", "x0%d" % b, "fx%d" % b], ["xn%d_%d" % (h, b)], "ac", T.xn[:, 4 * c0 + b:4 * c1:4],
                    T.x0[:, b * XL:(b + 1) * XL].indirect(T.lst2[:, c0 // 16:c1 // 16]), AF.Copy)
-        for h, (c0, c1) in enumerate(PARTS[t + 1]):
-            for b in (2, 3):
-                V(["lst", "pc%d" % b] + pls(b), ["xn%d_%d" % (h, b)], "tt", T.xn[:, 4 * c0 + b:4 * c1:4],
-                  plane(b).indirect(T.lst[:, c0 // 16:c1 // 16]), T.pc[:, b * C + c0:b * C + c1], A.add)
+
+        def add(h, b):
+            c0, c1 = parts[h]
+            V(["lst", "pc%d" % b] + pls(b), ["xn%d_%d" % (h, b)], "tt", T.xn[:, 4 * c0 + b:4 * c1:4],
+              plane(b).indirect(T.lst[:, c0 // 16:c1 // 16]), T.pc[:, b * C + c0:b * C + c1], A.add)
+
+        add(0, 2)
+        for h, (c0, c1) in enumerate(parts):
+            add(h, 3)
+            if t == 0 and h == 0:
+                V(["vt"], ["vq"], "qz", T.vq[:], T.vs[:], T.vt[:])
+            elif h + 1 < len(parts):
+                add(h + 1, 2)
             names = ["a%dh%d" % (t + 1, h)]
             V(["xn%d_%d" % (h, b) for b in range(4)], names, "qz", nq[:, c0:c1], ns[:, c0:c1], T.xn[:, 4 * c0:4 * c1])
             if t < R - 1:
                 scores(t + 1, h)
-                if h == 1:
-                    V(["vt"], ["vq"], "qz", T.vq[:], T.vs[:], T.vt[:])
-            else:
-                dma("s", names, [], T.oc[:, 4 * c0:4 * c1], bytes_of(nq[:, c0:c1]))
-                op("t", names + ["vq"], ["psy%d" % h], "mm", T.psy[:, 512 * h:512 * h + c1 - c0], T.vq[:], T.vs[:], nq[:, c0:c1], ns[:, c0:c1], True, True)
                 if h == 0:
-                    op("a", [], ["psy0", "y0"], "ac", T.ysb[:, c0:c1], T.psy[:, 0:c1 - c0], AF.Copy)
-                else:
-                    V([], ["psy1", "y1"], "cp", T.ysb[:, c0:c1], T.psy[:, 512:512 + c1 - c0])
-                    for k in range(4):
-                        dma("saas"[k], ["a%dh0" % R, "a%dh1" % R], [], T.osc[4 * k:4 * k + 4, :], T["as%d" % R][32 * k:32 * k + 4, :])
-                dma("a", ["y%d" % h], [], T.y[:, c0:c1], T.ysb[:, c0:c1])
+                    add(1, 2)
+                continue
+            ps, name = out_bank(h, c1 - c0)
+            dma("s", names, [], T.oc[:, 4 * c0:4 * c1], bytes_of(nq[:, c0:c1]))
+            op("t", names + ["vq"], [name], "mm", ps, T.vq[:], T.vs[:], nq[:, c0:c1], ns[:, c0:c1], True, True)
+            if h < 2:
+                op("a", [], [name, "y%d" % h], "ac", T.ysb[:, c0:c1], ps, AF.Copy)
+            else:
+                V([], [name, "y%d" % h], "cp", T.ysb[:, c0:c1], ps)
+                for k in range(4):
+                    dma("ssas"[k], ["a%dh%d" % (R, i) for i in range(3)], [], T.osc[4 * k:4 * k + 4, :], T["as%d" % R][32 * k:32 * k + 4, :])
+            dma("a", ["y%d" % h], [], T.y[:, c0:c1], T.ysb[:, c0:c1])
     for i in range(ndma[0]):
         g.sync.wait_ge(T.sem["d%d" % i], 16)
     for q in count:

@@ -18,8 +18,9 @@ H0 = -1000.0
 BIG = 3000.0
 TINY = 2.0 ** -120
 HOLD, FREE = 1296.0, 2592.0
-PARTS = (((0, 256), (256, 384), (384, C)), ((0, 320), (320, C)), ((0, 256), (256, 384), (384, C)))
-GA, GB, GC, GD, GE = 8, 22, 24, 26, 28
+PARTS = (((0, 192), (192, 384), (384, C)), ((0, 320), (320, C)), ((0, 256), (256, 384), (384, C)))
+ADDS = ((((3, 0, 0), (2, 0, 0), (3, 1, 1)), ((2, 1, 1),)), (((3, 0, 0), (2, 0, 0), (2, 1, 1)), ((3, 1, 2), (2, 2, 2)), ()))
+GA, GB = (0, 4), (18, 22)
 MV = 16
 F4, U8 = "float8_e4m3fn_x4", "uint8"
 
@@ -35,11 +36,11 @@ SCRATCH = {
     "et": _sb(1056, "bfloat16"), "eq": _sb(512, F4), "es": _sb(512, U8), "ones": _sb(516, "bfloat16"),
     "jp": _sb(32, "float32"), "wd": _sb(64, "float32"), "wa": _sb(64, "bfloat16"), "wb": _sb(64, "bfloat16"),
     "ui": _sb(8, "int32"), "ul": _sb(8, "uint16"), "pi": _sb(16, "int32"), "cst": _sb(48, "float32"),
-    "jf": _sb(256, "float32"), "jh": _sb(256, "float32"), "jr": _sb(256, "float32"), "flo": _sb(C, "float16"),
-    "prm": _sb(4, "uint16"), "c2": _sb(2 * C, "float32"),
-    "wrp": _sb(C, "bfloat16"), "wrm": _sb(128, "bfloat16"), "val0": _sb(C, "bfloat16"), "val": _sb(C, "bfloat16"), "tab": _sb(TAB, "bfloat16"),
+    "jf": _sb(128, "float32"), "jh": _sb(128, "float32"), "jr": _sb(128, "float32"), "flo": _sb(C, "float16"),
+    "prm": _sb(2, "uint16"), "c2": _sb(2 * C, "float32"),
+    "wr": _sb(C + 128, "bfloat16"), "val": _sb(C, "bfloat16"), "tab": _sb(TAB, "bfloat16"),
     "sg": _sb(C, "bfloat16"), "y2": _sb(2 * C, "float16"), "t2": _sb(2 * C, "float16"), "r2": _sb(2 * C, "float32"),
-    "k": _sb(32 * 14, "float32"), "key": _sb(128, "float32"), "kt": _sb(64, "float32"),
+    "k": _sb(32 * 14, "float32"), "key": _sb(96, "float32"), "kt": _sb(64, "float32"),
     "ow": _sb(32, "uint16"), "ow1": _sb(32, "uint16"), "lst": _sb(32, "uint16"), "lst2": _sb(32, "uint16"), "ml": _sb(32, "uint16"),
     "mw": _sb(128, "float16"), "gp": _sb(C, "bfloat16"), "gw": _sb(C, "float16"),
     "pw": _sb(4 * PL, "bfloat16"), "pc": _sb(4 * C, "bfloat16"), "x0": _sb(2 * XL, "bfloat16"),
@@ -138,8 +139,7 @@ def rank_program(g, core, T, topo):
 
     col = lambda i: T.cst[:, i:i + 1]
     K = lambda i: T.k[:, 32 * i:32 * i + 32]
-    XX, AA, EE, EV, QA, QB, E9, PW, C1, MG, OA, OB, OC, OD, OFF, INC, Y0, M1, X1, X2, MN, PA, PB, PC, PD, INI, YA = range(5, 32)
-    QC = 42
+    XX, AA, EE, EV, QA, QB, E9, PW, C1, MG, OA, OB, OC, OFF, INC, Y0, M1, X1, X2, QC, PC, IN1, INI, YA, RA, RB = range(5, 31)
     KF, KB, JW, JF, J16, JC, L2, L3 = 0, 1, 2, 3, 4, 5, 6, 7
     KG = lambda u: K(8 + u - 5)
     slot = lambda d, pos: T.c2[:, d * C + pos:(d + 1) * C:16]
@@ -156,14 +156,13 @@ def rank_program(g, core, T, topo):
         iota(["tabc"], T.tab[:, CC - TM:CC + TM], [[0, 2 * TM]], int(ZV), 0)
 
     op("p", [], ["pi"], "io", T.pi[:, 0:2], [[12, 2]], 0, 1)
-    iota(["jf"], T.jf[:], [[1, 256]], 0, 0)
+    iota(["jf"], T.jf[:], [[1, 128]], 0, 0)
     op("p", [], ["ui"], "io", T.ui[:], [[16, 8]], 0, 0)
     iota(["jw"], K(JW), [[32, 16], [0, 2]], 0, 0)
-    iota(["val0a"], T.val0[:, 0:256], [[32, 16], [1, 16]], -256, 0)
     for u in range(5, 9):
         pat = [[0, 1 << (8 - u)], [1 << u, 2], [0, 2 << (u - 5)]]
         iota(["kg%d" % u], KG(u), pat[1:] if u == 8 else pat, 0, 0)
-    iota(["val0b"], T.val0[:, 256:C], [[32, 16], [-1, 16]], 31 - 256, 0)
+    iota(["val"], T.val[:], [[1, 32], [32, 16]], -256, 0)
     iota(["jpb"], T.jp[:], [[0, 8], [4, 4]], 0, 0)
     for name, c0, v0, there in (("tabv1", CC - LK - TM, 2 * TM - 1, rank > 0), ("tabv3", CC + LK, TM - 1, rank < n_ranks - 1)):
         iota([name], T.tab[:, c0:c0 + TM], [[-4 if there else 0, TM]], AV + 4 * v0 if there else int(ZV), 0)
@@ -174,35 +173,43 @@ def rank_program(g, core, T, topo):
         iota(["pd%d" % b], T.pw[:, b * PL + D0:(b + 1) * PL:4], [[0, 2 * TM]], 0, 0)
 
     V([], ["ones"], "ms", T.ones[:], 1.0)
+    bits = ((2, 1), (3, 2), (4, 4), (5, 8), (6, 16), (7, 15), (8, 31), (10, 14), (11, 12), (12, 3))
     V(["pi"], ["pe"], "ts", T.pi[:, 9:10], T.pi[:, 1:2], 15, None, A.bitwise_and)
-    V(["pi"], ["px"], "ts", T.pi[:, 7:8], T.pi[:, 0:1], 15, None, A.bitwise_and)
+    for u, m in bits[:5]:
+        V(["pi"], ["pb%d" % u], "ts", T.pi[:, u:u + 1], T.pi[:, 0:1], m, None, A.bitwise_and)
     V(["pe"], ["e9"], "ts", col(E9), T.pi[:, 9:10], 9.0, None, A.min)
-    bits = ((2, 1), (3, 2), (4, 4), (5, 8), (6, 16), (8, 31), (10, 14), (11, 12), (12, 3))
-    for u, m in bits:
+    for u, m in bits[5:]:
         V(["pi"], ["pb%d" % u], "ts", T.pi[:, u:u + 1], T.pi[:, 0:1], m, None, A.bitwise_and)
     V(["jf", "e9"], ["tw"], "ts", T.cst[:, 32:41], T.jf[:, 0:9], col(E9), 1.0, A.is_lt, A.add)
-    V(["pe", "px"] + ["pb%d" % u for u, _ in bits], ["cf"], "cp", T.cst[:, 0:11], T.pi[:, 2:13])
+    V(["pe"] + ["pb%d" % u for u, _ in bits], ["cf"], "cp", T.cst[:, 0:11], T.pi[:, 2:13])
+    V(["ui"], ["ul"], "cp", T.ul[:], T.ui[:])
     V(["tw"], ["pwc"], "rd", col(PW), T.cst[:, 32:41], AxisListType.X, A.mult)
-    V(["e9"], ["oa"], "ts", col(OA), col(E9), 9.0, -1256.0, A.not_equal, A.mult)
+    V(["e9"], ["oa"], "ts", col(OA), col(E9), 9.0, 1512.0, A.is_equal, A.mult)
     V(["cf"], ["ob"], "ts", col(OB), col(XX), 0.0, -3000.0, A.is_equal, A.mult)
     V(["cf"], ["oc"], "ts", col(OC), col(XX), 1.0, -1000.0, A.is_equal, A.mult)
-    V(["e9"], ["inc"], "ts", col(INC), col(E9), 9.0, 256.0, A.not_equal, A.mult)
-    V(["oa", "ob", "oc"], ["od"], "ts", col(OD), col(OA), col(OB), col(OC), A.add, A.add)
-    V(["cf", "jw"], ["jj"], "ts", K(JF), K(JW), col(AA), None, A.add)
-    V(["ui"], ["ul"], "cp", T.ul[:], T.ui[:])
+    V(["ut"], ["uq"], "qz", T.uq[:], T.us[:], T.ut[:])
+    V(["oa", "ob", "oc"], ["off"], "ts", col(OFF), col(OA), col(OB), col(OC), A.add, A.add)
+    V(["uq", "ul"], ["uq2"], "cp", T.uq2[:].bitcast(dt.uint32), T.uq[:].bitcast(dt.uint32).indirect(T.ul[:]))
     for i in range(2):
         op("p", ["ones"], ["et%d" % i], "as", T.et[:, 528 * i:528 * i + 516], T.ones[:], [[-1, 516]], A.is_equal, 0.0, 2 + i, 4)
     for name, out, n, v in (("kf", K(KF), 32, -up), ("kb", K(KB), 32, dn), ("s14f", slot(0, 14), 32, BETA * LK), ("s14b", slot(1, 14), 32, -BETA * LK),
                             ("s1f", slot(0, 1), 32, 0.0), ("s2f", slot(0, 2), 32, 0.0), ("pz", T.pw[:, 0:4 * PL:PL], 4, 0.0),
-                            ("tabv2", T.tab[:, TAB - 1:TAB], 1, ZV)):
-        lin(["jf"], [name], out, T.jf[:, 0:n], 0.0, v)
-    lin(["pwc"], ["c1"], col(C1), col(PW), -0.5, 0.5)
+                            ("tabv2", T.tab[:, TAB - 1:TAB], 1, ZV), ("s0", T.c2[:, 0:2 * C:16], 64, BIG), ("s15", T.c2[:, 15:2 * C:16], 64, 0.0)):
+        lin(["ones"], [name], out, T.ones[:, 0:n], 0.0, v)
+    act(["e9"], ["ra"], col(RA), col(E9), AF.Relu, 1.0, -7.0)
+    act(["e9"], ["rb8"], col(RB), col(E9), AF.Relu, 1.0, -8.0)
+    act(["ra"], ["in1"], col(IN1), col(RA), AF.Relu, -128.0, 128.0)
+    act(["rb8"], ["inc"], col(INC), col(RB), AF.Relu, -256.0, 256.0)
+    for u in range(5):
+        lin(["cf", "kf"], ["sf%d" % u], slot(0, 4 + u), K(KF), col(u), BETA * S)
+    lin(["pwc"], ["c1"], col(C1), col(PW), -0.5, 0.5 - 256)
     lin(["pwc"], ["mg"], col(MG), col(PW), 1.5 * 2.0 ** 23, 0.0)
+    op("a", ["uq", "ul"], ["us2"], "ac", T.us2[:], T.us[:].indirect(T.ul[:]), AF.Copy)
     lin(["jf", "c1"], ["jh", "jq"], T.jh[:], T.jf[:], 1.0, col(C1))
-    lin(["od"], ["off"], col(OFF), col(OD), 1.0, 1000.0)
     lin(["jh", "jq", "mg"], ["jr"], T.jr[:], T.jh[:], 1.0, col(MG))
 
     def high_steps():
+        lin(["jj"], ["s3f"], slot(0, 3), K(JF), up, -256.0 - BETA * (CC - DP))
         for u in range(5, 9):
             lin(["kg%d" % u], ["sf%d" % u], slot(0, 4 + u), KG(u), -up, 257.0 - BETA * (8 * S + DP) if u == 8 else BETA * S)
         for u in range(5):
@@ -214,38 +221,29 @@ def rank_program(g, core, T, topo):
 
     cn = [["s0", "s15", "s1f", "s2f", "s3f", "s14f", "d13f"] + ["sf%d" % u for u in range(9)],
           ["s0", "s15", "s3b", "s14b", "d13b", "d1b", "d2b"] + ["sb%d" % u for u in range(9)]]
-    V(["ut"], ["uq"], "qz", T.uq[:], T.us[:], T.ut[:])
-    V(["uq", "ul"], ["uq2"], "cp", T.uq2[:].bitcast(dt.uint32), T.uq[:].bitcast(dt.uint32).indirect(T.ul[:]))
-    op("a", ["uq", "ul"], ["us2"], "ac", T.us2[:], T.us[:].indirect(T.ul[:]), AF.Copy)
-    for u in range(5):
-        lin(["cf", "kf"], ["sf%d" % u], slot(0, 4 + u), K(KF), col(u), BETA * S)
-    lin(["jj"], ["s3f"], slot(0, 3), K(JF), up, -256.0 - BETA * (CC - DP))
     for h, (c0, c1) in enumerate(PARTS[0]):
         V(["xt%d" % h], ["a0h%d" % h], "qz", T.aq0[:, c0:c1], T.as0[:, c0:c1], T.xt[:, 4 * c0:4 * c1])
-    V(["jr", "mg", "off"], ["floa"], "ts", T.flo[:, 0:256], T.jr[:], col(MG), col(OFF), A.subtract, A.add)
-    V([], ["s0"], "ms", T.c2[:, 0:2 * C:16], BIG)
-    V(["floa", "inc"], ["flob"], "ts", T.flo[:, 256:C], T.flo[:, 0:256], col(INC), None, A.add)
-    V(["val0a", "cf"], ["vala"], "ts", T.val[:, 0:256], T.val0[:, 0:256], col(4), None, A.add)
-    V([], ["s15"], "ms", T.c2[:, 15:2 * C:16], 0.0)
+    V(["jr", "mg", "off"], ["flo0"], "ts", T.flo[:, 0:128], T.jr[:], col(MG), col(OFF), A.subtract, A.add)
+    V(["cf", "jw"], ["jj"], "ts", K(JF), K(JW), col(AA), None, A.add)
+    V(["flo0", "in1"], ["flo1"], "ts", T.flo[:, 128:256], T.flo[:, 0:128], col(IN1), None, A.add)
+    V(["flo0", "inc"], ["flo2"], "ts", T.flo[:, 256:384], T.flo[:, 0:128], col(INC), None, A.add)
+    V(["flo0", "in1", "inc"], ["flo3"], "ts", T.flo[:, 384:C], T.flo[:, 0:128], col(IN1), col(INC), A.add, A.add)
 
     def late_constants():
-        lin(["cf"], ["m1"], col(M1), col(4), 1.0 / 16, 0.0)
-        lin(["cf"], ["n2"], col(Y0), col(4), -2.0, 0.0)
         act(["cf"], ["ya"], col(YA), col(AA), AF.Abs, 1.0, -15.5)
-        lin(["cf", "m1"], ["pA"], col(PA), col(XX), 2.0, col(M1))
-        lin(["cf", "m1"], ["x2"], col(X2), col(EV), 1.0, col(M1))
-        act(["cf", "n2"], ["x1"], col(X1), col(0), AF.Abs, 32.0, col(Y0))
         act(["jf"], ["jq"], T.jh[:, 0:32], T.jf[:, 0:32], AF.Abs, 1.0, -15.5)
-        lin(["pA"], ["pB"], col(PB), col(PA), 1.0, 32.0)
-        lin(["x1", "x2"], ["pC"], col(PC), col(X1), 1.0, col(X2))
-        act(["jq", "ya"], ["wd0"], T.wd[:, 0:32], T.jh[:, 0:32], AF.Abs, -1.0, col(YA))
         act(["jpb", "cf"], ["wd1"], T.wd[:, 32:64], T.jp[:], AF.Abs, -1.0, col(QA))
-        lin(["pC"], ["pD"], col(PD), col(PC), 1.0, 16.0)
-        lin(["cf"], ["mn"], col(MN), col(4), -1.0, 0.0)
+        act(["jq", "ya"], ["wd0"], T.wd[:, 0:32], T.jh[:, 0:32], AF.Abs, -1.0, col(YA))
+        lin(["cf"], ["m1"], col(M1), col(4), 1.0 / 16, 0.0)
         act(["wd0", "wd1"], ["wb"], T.wb[:, 0:63], T.wd[:, 1:64], AF.Relu, -FREE, FREE)
         act(["wd0", "wd1"], ["wa"], T.wa[:], T.wd[:], AF.Relu, -HOLD, HOLD)
-        lin(["val0b", "mn"], ["valb"], T.val[:, 256:C], T.val0[:, 256:C], 1.0, col(MN))
+        lin(["cf"], ["n2"], col(Y0), col(4), -2.0, 0.0)
+        lin(["ones", "wb"], ["wc"], T.wb[:, 35:64:4], T.ones[:, 0:8], 0.0, FREE)
+        lin(["ones", "wb"], ["we"], T.wb[:, 15:32:16], T.ones[:, 0:2], 0.0, FREE)
+        lin(["cf", "m1"], ["x2"], col(X2), col(EV), 1.0, col(M1))
+        act(["cf", "n2"], ["x1"], col(X1), col(0), AF.Abs, 32.0, col(Y0))
         lin(["cf"], ["qc"], col(QC), col(QB), float(PL), HOLD - FREE - ZV)
+        lin(["x1", "x2"], ["pC"], col(PC), col(X1), 1.0, col(X2))
 
     def masks(c):
         r = T.rank_of(c)
@@ -285,9 +283,10 @@ def rank_program(g, core, T, topo):
         op("a", [], ["psp%d" % b, "pw%d" % b], "ac", T.pw[:, b * PL + P0:b * PL + P0 + C], bank(b, C), AF.Copy, scale=0.0625)
         dma("s", ["pw%d" % b], ["pc%d" % b], T.pc[:, b * C:(b + 1) * C], T.pw[:, b * PL + P0:b * PL + P0 + C])
 
-    def spread(name, buf, i):
-        n0 = 32 << i
-        op("a", ["%s%d" % (name, i)], ["%s%d" % (name, i + 1)], "ac", buf[:, n0:2 * n0], buf[:, 0:n0], AF.Copy)
+    def spread(name, i):
+        n = 32 << i
+        out, src = (T.wr[:, C - 2 * n:C - n], T.wr[:, C - n:C]) if name == "wrp" else (T.wr[:, C + n:C + 2 * n], T.wr[:, C:C + n])
+        op("a", ["%s%d" % (name, i)], ["%s%d" % (name, i + 1)], "ac", out, src, AF.Copy)
 
     def unit(b):
         e0 = 528 * (b % 2) + 2 - b // 2 * 2
@@ -314,10 +313,8 @@ def rank_program(g, core, T, topo):
             op("a", [], [name, "sg%d" % h], "ac", T.sg[:, c0:c1], ps, AF.Sign, bias=TINY)
         if t == 0:
             high_steps()
-        else:
-            p_copy(0)
         cm = PARTS[t][0][1]
-        sg = ["sg0", "sg1", "sg2", "floa", "flob"]
+        sg = ["sg0", "sg1", "sg2"] + ["flo%d" % i for i in range(4)]
         back = lambda: V(sg, ["yb"], "sc", T.y2[:, 2 * C - 1:C - 1:-1], T.flo[:], T.sg[:, ::-1], H0, A.max, A.subtract)
         if t == 0:
             V(sg, ["yf0", "yf1"], "sc", T.y2[:, 0:C], T.flo[:], T.sg[:], H0, A.max, A.add)
@@ -339,42 +336,37 @@ def rank_program(g, core, T, topo):
         lin(["tb"], ["d1b"], slot(1, 1), hb, BETA, -BETA * H0)
         if t == 0:
             late_constants()
-        for b in range(1, 4) if t else range(1):
+        for b in range(4 if t else 1):
             p_copy(b)
         V(tf + cn[0], ["rf"], "sc", T.r2[:, 0:C - 1], T.t2[:, 0:C - 1], T.c2[:, 0:C - 1], BIG, A.min, A.add)
         V(["tb"] + cn[1], ["rb"], "sc", T.r2[:, C:2 * C - 1], T.t2[:, C:2 * C - 1], T.c2[:, C:2 * C - 1], BIG, A.min, A.add)
+        least = lambda name, out, c0, step: V(["rf", "rb"], [name], "tt", out, T.r2[:, c0:C:step], T.r2[:, C + c0:2 * C:step], A.min)
         if t == 0:
-            V(["pA", "pB", "pC", "pD"], ["prm"], "cp", T.prm[:], T.cst[:, PA:PD + 1])
-        for i in range(2):
-            V(["rf", "rb"], ["key%d" % i], "tt", T.key[:, 64 * i:64 * i + 32], T.r2[:, 13 + i:C:16], T.r2[:, C + 13 + i:2 * C:16], A.min)
+            V(["wa", "wb", "wc", "we"], ["wrm0", "wrp0"], "tt", T.wr[:, C - 32:C + 32], T.wb[:], T.wa[:], A.subtract)
+        least("key0", T.key[:, 0:16], 13, 32)
+        least("key2", T.key[:, 16:32], 29, 32)
+        least("key1", T.key[:, 32:64], 14, 16)
+        V(["key0", "key2"], ["kt0"], "tr", T.kt[:, 0:32], T.key[:, 0:32])
+        V(["key1"], ["kt1"], "tr", T.kt[:, 32:64], T.key[:, 32:64])
         if t == 0:
-            V([], ["wb"], "ms", T.wb[:, 35:64:4], FREE)
-        for i in range(2):
-            V(["key%d" % i], ["kt%d" % i], "tr", T.kt[:, 32 * i:32 * i + 32], T.key[:, 64 * i:64 * i + 32])
+            V(["pC"], ["prm"], "cp", T.prm[:, 0:1], col(PC))
+        V(["kt0"], ["ow0"], "ts", T.ow[:], T.kt[:, 0:32], -1.0 / BETA, None, A.mult)
+        V(["kt1"], ["rot1"], "tr", T.key[:, 64:96], T.kt[:, 63:31:-1])
         if t == 0:
-            V([], ["wb"], "ms", T.wb[:, 15:32:16], FREE)
-        V(["kt0"], ["rot0"], "tr", T.key[:, 32:64], T.kt[:, 31::-1])
-        V(["kt1"], ["rot1"], "tr", T.key[:, 96:128], T.kt[:, 63:31:-1])
-        if t == 0:
-            V(["wa", "wb"], ["wrm0"], "tt", T.wrm[:, 0:32], T.wb[:, 32:64], T.wa[:, 32:64], A.subtract)
-        V(["key0", "rot0", "prm"], ["ow0"], "ts", T.ow[:], T.key[:, 0:64].indirect(T.prm[:, 0:2]), -1.0 / BETA, None, A.mult)
-        V(["key1", "rot1", "prm"], ["ow1"], "ts", T.ow1[:], T.key[:, 64:128].indirect(T.prm[:, 2:4]), -1.0 / BETA, float(TAB - 1), A.mult, A.min)
-        if t == 0:
-            V(["wa", "wb"], ["wrp0"], "tt", T.wrp[:, 0:32], T.wb[:, 0:32], T.wa[:, 0:32], A.subtract)
+            V(["pC"], ["prn"], "ts", T.prm[:, 1:2], col(PC), 16.0, None, A.add)
             for b in range(1, 4):
                 p_copy(b)
                 if b < 3:
-                    spread("wrm", T.wrm, b - 1)
-                spread("wrp", T.wrp, b - 1)
-        V(["ow0", "vala", "valb"], tabs, "cp", T.tab[:].indirect(T.ow[:]), T.val[:])
-        partners("a", "gpa", 0, GA)
-        V(tabs + ["wrm2"], ["mw"], "sc", T.mw[:], T.tab[:, CC - TM:CC + TM], T.wrm[:], FREE, A.min, A.add)
-        partners("v", "gpc", GB, GC)
+                    spread("wrm", b - 1)
+                    spread("wrp", b - 1)
+        V(["ow0", "val"], tabs, "cp", T.tab[:].indirect(T.ow[:]), T.val[:])
+        V(["key1", "rot1", "prm", "prn"], ["ow1"], "ts", T.ow1[:], T.key[:, 32:96].indirect(T.prm[:]), -1.0 / BETA, float(TAB - 1), A.mult, A.min)
+        if GA[t]:
+            partners("a", "gpa", 0, GA[t])
+        V(tabs + ["wrm2"], ["mw"], "sc", T.mw[:], T.tab[:, CC - TM:CC + TM], T.wr[:, C:C + 128], FREE, A.min, A.add)
         V(["mw", "qc"], ["ml"], "ts", T.ml[:], T.mw[:, 3:128:4], col(QC), None, A.add)
-        partners("v", "gpd", GC, GD)
         op("a", ["ml"] + pall, ["mta"], "ac", T.mt[:, 16 * MV:512], T.pw[:].indirect(T.ml[:, MV:32]), AF.Copy)
         V(["ml"] + pall, ["mtv"], "cp", T.mt[:, 0:16 * MV], T.pw[:].indirect(T.ml[:, 0:MV]))
-        partners("v", "gpe", GD, GE)
         V(["mta", "mtv"], ["mq%d" % t], "qz", mq[:], ms_[:], T.mt[:])
         order("p", ["mq%d" % t], [])
         for src, dst, cast in ((mq, lq, bytes_of), (ms_, ls, lambda v: v)):
@@ -389,16 +381,20 @@ def rank_program(g, core, T, topo):
             z0 = nb[0][1]
             dma("s", ["mq%d" % t], ["zl%d" % t], bytes_of(lq[:, z0:z0 + TM]), bytes_of(mq[:, z0:z0 + TM]))
             dma("s", ["mq%d" % t], ["zm%d" % t], ls[:, z0:z0 + TM], ms_[:, z0:z0 + TM])
-        partners("a", "gpb", GA, GB)
-        partners("v", "gpf", GE, 32)
+        if t == 0:
+            spread("wrp", 2)
+        partners("a", "gpb", GA[t], GB[t])
+        if t == 0:
+            spread("wrp", 3)
+        partners("v", "gpc", GB[t], 32)
         if t == 0:
             lin(["cf", "jc"], ["j16"], K(J16), K(JC), 1.0, col(XX))
             clear_lists()
-            V(["wrp3"], ["wrp4"], "cp", T.wrp[:, 256:C], T.wrp[:, 0:256])
-            unit(2)
-        V(["gpa", "gpb", "gpc", "gpd", "gpe", "gpf", "wrp4"], ["gw"], "sc", T.gw[:], T.gp[:], T.wrp[:], FREE, A.min, A.add)
-        if t == 0:
             unit(0)
+            unit(2)
+        V(["gpa", "gpb", "gpc", "wrp4"], ["gw"], "sc", T.gw[:], T.gp[:], T.wr[:, 0:C], FREE, A.min, A.add)
+        if t == 0:
+            unit(3)
         V(["gw"], ["lst"], "ts", T.lst[:], T.gw[:, 15:C:16], HOLD - FREE - ZV, None, A.add)
         V(["gw"], ["l2"], "ts", K(L2), T.gw[:, 15:C:16], 2.0, 2 * (HOLD - FREE) + X0 - 2 * AV, A.mult, A.add)
         V(["lst", "pc0"] + pls(0), ["x00"], "tt", T.x0[:, P0:P0 + C], plane(0).indirect(T.lst[:]), T.pc[:, 0:C], A.add)
@@ -406,14 +402,14 @@ def rank_program(g, core, T, topo):
         V(["lst", "pc1"] + pls(1), ["x01"], "tt", T.x0[:, XL + P0:XL + P0 + C], plane(1).indirect(T.lst[:]), T.pc[:, C:2 * C], A.add)
         V(["l3"], ["lst2"], "cp", T.lst2[:], K(L3))
         if t == 0:
-            unit(3)
             unit(1)
+            V(["vt"], ["vq"], "qz", T.vq[:], T.vs[:], T.vt[:])
         order("t", ["zl%d" % t, "zm%d" % t], [])
         wait("t", "arr%d" % t, arrive)
-        for b in (2, 0, 3, 1):
+        for b in (0, 3, 1, 2):
             op("t", ["eq%d" % b], ["psp%d" % b], "mm", bank(b, 128),
                T.eq[:, 128 * b:128 * b + 128], T.es[:, 128 * b:128 * b + 128], lq[:], ls[:], True, True)
-        for b in (2, 3):
+        for b in (3, 2):
             op("a", [], ["psp%d" % b, "pd%d" % b], "ac", T.pw[:, b * PL + D0:(b + 1) * PL:4], bank(b, 128), AF.Copy)
         for b in (0, 1):
             V(["mta", "mtv"], ["psp%d" % b, "fx%d" % b], "tt", T.x0[:, b * XL + X0:b * XL + X0 + 8 * 127 + 1:8],
@@ -425,37 +421,32 @@ def rank_program(g, core, T, topo):
                 op("a", ["lst2", "x0%d" % b, "fx%d" % b], ["xn%d_%d" % (h, b)], "ac", T.xn[:, 4 * c0 + b:4 * c1:4],
                    T.x0[:, b * XL:(b + 1) * XL].indirect(T.lst2[:, c0 // 16:c1 // 16]), AF.Copy)
 
-        def add(h, b):
-            c0, c1 = parts[h]
-            V(["lst", "pc%d" % b] + pls(b), ["xn%d_%d" % (h, b)], "tt", T.xn[:, 4 * c0 + b:4 * c1:4],
+        def add(b, h0, h1):
+            c0, c1 = parts[h0][0], parts[h1][1]
+            V(["lst", "pc%d" % b] + pls(b), ["xn%d_%d" % (h, b) for h in range(h0, h1 + 1)], "tt", T.xn[:, 4 * c0 + b:4 * c1:4],
               plane(b).indirect(T.lst[:, c0 // 16:c1 // 16]), T.pc[:, b * C + c0:b * C + c1], A.add)
 
-        add(0, 2)
         for h, (c0, c1) in enumerate(parts):
-            add(h, 3)
-            if t == 0 and h == 0:
-                V(["vt"], ["vq"], "qz", T.vq[:], T.vs[:], T.vt[:])
-            elif h + 1 < len(parts):
-                add(h + 1, 2)
+            for run in ADDS[t][h]:
+                add(*run)
             names = ["a%dh%d" % (t + 1, h)]
             V(["xn%d_%d" % (h, b) for b in range(4)], names, "qz", nq[:, c0:c1], ns[:, c0:c1], T.xn[:, 4 * c0:4 * c1])
             if t < R - 1:
                 scores(t + 1, h)
-                if h == 0:
-                    add(1, 2)
                 continue
             ps, name = out_bank(h, c1 - c0)
             dma("s", names, [], T.oc[:, 4 * c0:4 * c1], bytes_of(nq[:, c0:c1]))
             op("t", names + ["vq"], [name], "mm", ps, T.vq[:], T.vs[:], nq[:, c0:c1], ns[:, c0:c1], True, True)
-            if h < 2:
+            if h + 1 < len(parts):
                 op("a", [], [name, "y%d" % h], "ac", T.ysb[:, c0:c1], ps, AF.Copy)
             else:
                 V([], [name, "y%d" % h], "cp", T.ysb[:, c0:c1], ps)
                 for k in range(4):
-                    dma("ssas"[k], ["a%dh%d" % (R, i) for i in range(3)], [], T.osc[4 * k:4 * k + 4, :], T["as%d" % R][32 * k:32 * k + 4, :])
+                    dma("s", ["a%dh%d" % (R, i) for i in range(len(parts))], [], T.osc[4 * k:4 * k + 4, :], T["as%d" % R][32 * k:32 * k + 4, :])
             dma("a", ["y%d" % h], [], T.y[:, c0:c1], T.ysb[:, c0:c1])
-    for i in range(ndma[0]):
-        g.sync.wait_ge(T.sem["d%d" % i], 16)
     for q in count:
-        g.sync.wait_ge(T.sem[q], count[q])
+        wait("s", q, count[q])
+    for i in range(ndma[0]):
+        if not any("d%d" % i in seen[q] for q in seen):
+            wait("s", "d%d" % i, 16)
     g.wait_ge(T.sem.sent, sent[0])

from concourse.bass import DstId, RemoteDMATransfer
from concourse.mybir import dt, AluOpType, AxisListType, ActivationFunctionType

C, TM, R = 512, 64, 2
P0 = 16
ZV = -(256.0 + P0)
AV = 512
D0 = AV + 256 + P0
PL = D0 + 8 * TM
X0 = 2 * AV - 494
XL = 1552
S, DP = 3072, 1536
CC = 28928
LK = DP - 1
TAB = CC + LK + TM + 1
BETA = 2.0 ** -15
H0 = -1000.0
BIG = 3000.0
TINY = 2.0 ** -120
HOLD, FREE = 1296.0, 2592.0
PARTS = (((0, 192), (192, 384), (384, C)), ((0, 320), (320, C)), ((0, 256), (256, 384), (384, C)))
ADDS = ((((3, 0, 0), (2, 0, 0), (3, 1, 1)), ((2, 1, 1),)), (((3, 0, 0), (2, 0, 0), (2, 1, 1)), ((3, 1, 2), (2, 2, 2)), ()))
GA, GB = (0, 4), (18, 22)
MV = 16
F4, U8 = "float8_e4m3fn_x4", "uint8"


def _sb(n, t):
    return ("sbuf", [128, n], t)


SCRATCH = {
    "xt": _sb(4 * C, "bfloat16"), "ut": _sb(512, "bfloat16"), "vt": _sb(512, "bfloat16"),
    "uq": _sb(128, F4), "us": _sb(128, U8), "uq2": _sb(128, F4), "us2": _sb(128, U8),
    "vq": _sb(128, F4), "vs": _sb(128, U8), "wq": _sb(512, F4), "wsc": _sb(512, U8),
    "et": _sb(1056, "bfloat16"), "eq": _sb(512, F4), "es": _sb(512, U8), "ones": _sb(516, "bfloat16"),
    "jp": _sb(32, "float32"), "wd": _sb(64, "float32"), "wa": _sb(64, "bfloat16"), "wb": _sb(64, "bfloat16"),
    "ui": _sb(8, "int32"), "ul": _sb(8, "uint16"), "pi": _sb(16, "int32"), "cst": _sb(48, "float32"),
    "jf": _sb(128, "float32"), "jh": _sb(128, "float32"), "jr": _sb(128, "float32"), "flo": _sb(C, "float16"),
    "prm": _sb(2, "uint16"), "c2": _sb(2 * C, "float32"),
    "wr": _sb(C + 128, "bfloat16"), "val": _sb(C, "bfloat16"), "tab": _sb(TAB, "bfloat16"),
    "sg": _sb(C, "bfloat16"), "y2": _sb(2 * C, "float16"), "t2": _sb(2 * C, "float16"), "r2": _sb(2 * C, "float32"),
    "k": _sb(32 * 14, "float32"), "key": _sb(96, "float32"), "kt": _sb(64, "float32"),
    "ow": _sb(32, "uint16"), "ow1": _sb(32, "uint16"), "lst": _sb(32, "uint16"), "lst2": _sb(32, "uint16"), "ml": _sb(32, "uint16"),
    "mw": _sb(128, "float16"), "gp": _sb(C, "bfloat16"), "gw": _sb(C, "float16"),
    "pw": _sb(4 * PL, "bfloat16"), "pc": _sb(4 * C, "bfloat16"), "x0": _sb(2 * XL, "bfloat16"),
    "mt": _sb(512, "bfloat16"), "xn": _sb(4 * C, "bfloat16"), "ysb": _sb(C, "float32"),
    "pss": ("psum", [128, 1024], "float32"), "psp": ("psum", [128, 2048], "float32"), "psy": ("psum", [128, 512], "float32"),
}
for _t in range(R + 1):
    SCRATCH["aq%d" % _t] = _sb(C, F4)
    SCRATCH["as%d" % _t] = _sb(C, U8)
for _t in range(R):
    for _n in ("m", "l"):
        SCRATCH["%sq%d" % (_n, _t)] = _sb(128, F4)
        SCRATCH["%ss%d" % (_n, _t)] = _sb(128, U8)

NDMA = 36
SEMAPHORES = ["v", "a", "t", "p", "sent"] + ["arr%d" % _t for _t in range(R)] + ["d%d" % _i for _i in range(NDMA)]


def rank_program(g, core, T, topo):
    rank = T.rank_of(core)
    if rank is None:
        return
    A, AF = AluOpType, ActivationFunctionType
    n_ranks = len(T.cores)
    Q = {"v": g.vector, "a": g.scalar, "t": g.tensor, "p": g, "s": g.sync}
    count = {"v": 0, "a": 0, "t": 0, "p": 0}
    seen = {q: {} for q in Q}
    wrote, readers = {}, {}
    ndma = [0]

    def wait(q, sem, n):
        if seen[q].get(sem, 0) < n:
            Q[q].wait_ge(T.sem[sem], n)
            seen[q][sem] = n

    def order(q, r, w):
        need = {}
        for name in r:
            if name in wrote:
                s, n = wrote[name]
                need[s] = max(need.get(s, 0), n)
        for name in w:
            for s, n in readers.get(name, []) + ([wrote[name]] if name in wrote else []):
                need[s] = max(need.get(s, 0), n)
        for s, n in need.items():
            wait(q, s, n)

    def note(tok, r, w):
        for name in r:
            readers.setdefault(name, []).append(tok)
        for name in w:
            wrote[name] = tok
            readers[name] = []

    def op(q, r, w, name, *args, **kw):
        order(q, r, w)
        e = Q[q]
        calls = {
            "ts": lambda: e.tensor_scalar(*args), "tt": lambda: e.tensor_tensor(*args), "cp": lambda: e.tensor_copy(*args),
            "ms": lambda: e.memset(*args), "sc": lambda: e.tensor_tensor_scan(*args), "tr": lambda: e.transpose(*args),
            "qz": lambda: e.quantize_mx(*args), "ac": lambda: e.activation(*args, **kw), "rd": lambda: e.tensor_reduce(*args),
            "mm": lambda: e.matmul_mx(*args), "io": lambda: e.iota(*args, **kw), "as": lambda: e.affine_select(*args),
        }
        count[q] += 1
        calls[name]().then_inc(T.sem[q], 1)
        note((q, count[q]), r, w)

    def dma(q, r, w, out, in_):
        order(q, r, w)
        s = "d%d" % ndma[0]
        ndma[0] += 1
        Q[q].dma_start(out, in_).then_inc(T.sem[s], 16)
        note((s, 16), r, w)

    def V(r, w, name, *args):
        op("v", r, w, name, *args)

    def act(r, w, out, in_, f, scale, bias):
        op("a", r, w, "ac", out, in_, f, bias=bias, scale=scale)

    def lin(r, w, out, in_, scale, bias):
        act(r, w, out, in_, AF.Identity, scale, bias)

    def iota(w, *args):
        op("p", [], w, "io", *args, allow_small_or_imprecise_dtypes=True)

    def bytes_of(view):
        return view.bitcast(dt.uint8)

    nb = []
    if rank > 0:
        nb.append((T.cores[rank - 1], 0))
    if rank < n_ranks - 1:
        nb.append((T.cores[rank + 1], TM))
    edge = len(nb) < 2

    col = lambda i: T.cst[:, i:i + 1]
    K = lambda i: T.k[:, 32 * i:32 * i + 32]
    XX, AA, EE, EV, QA, QB, E9, PW, C1, MG, OA, OB, OC, OFF, INC, Y0, M1, X1, X2, QC, PC, IN1, INI, YA, RA, RB = range(5, 31)
    KF, KB, JW, JF, J16, JC, L2, L3 = 0, 1, 2, 3, 4, 5, 6, 7
    KG = lambda u: K(8 + u - 5)
    slot = lambda d, pos: T.c2[:, d * C + pos:(d + 1) * C:16]
    up, dn = 1.0 + 2 * BETA, 1.0 - 2 * BETA

    dma("s", [], ["ut"], T.ut[:], T.u[:])
    for h, (c0, c1) in enumerate(PARTS[0]):
        dma("asa"[h], [], ["xt%d" % h], T.xt[:, 4 * c0:4 * c1], T.x[:, 4 * c0:4 * c1])
    dma("s", ["xt0", "xt1", "xt2"], ["wq"], bytes_of(T.wq[:]), T.wc[:])
    dma("s", [], ["wsc"], T.wsc[:], T.ws[:])
    dma("s", [], ["vt"], T.vt[:], T.v[:])

    def clear_lists():
        iota(["tabc"], T.tab[:, CC - TM:CC + TM], [[0, 2 * TM]], int(ZV), 0)

    op("p", [], ["pi"], "io", T.pi[:, 0:2], [[12, 2]], 0, 1)
    iota(["jf"], T.jf[:], [[1, 128]], 0, 0)
    op("p", [], ["ui"], "io", T.ui[:], [[16, 8]], 0, 0)
    iota(["jw"], K(JW), [[32, 16], [0, 2]], 0, 0)
    for u in range(5, 9):
        pat = [[0, 1 << (8 - u)], [1 << u, 2], [0, 2 << (u - 5)]]
        iota(["kg%d" % u], KG(u), pat[1:] if u == 8 else pat, 0, 0)
    iota(["val"], T.val[:], [[1, 32], [32, 16]], -256, 0)
    iota(["jpb"], T.jp[:], [[0, 8], [4, 4]], 0, 0)
    for name, c0, v0, there in (("tabv1", CC - LK - TM, 2 * TM - 1, rank > 0), ("tabv3", CC + LK, TM - 1, rank < n_ranks - 1)):
        iota([name], T.tab[:, c0:c0 + TM], [[-4 if there else 0, TM]], AV + 4 * v0 if there else int(ZV), 0)
    clear_lists()
    iota(["tabv0"], T.tab[:, CC - LK - C:CC - LK - TM], [[0, C - TM]], int(ZV), 0)
    iota(["jc"], K(JC), [[16, 32]], P0, 0)
    for b in range(2):
        iota(["pd%d" % b], T.pw[:, b * PL + D0:(b + 1) * PL:4], [[0, 2 * TM]], 0, 0)

    V([], ["ones"], "ms", T.ones[:], 1.0)
    bits = ((2, 1), (3, 2), (4, 4), (5, 8), (6, 16), (7, 15), (8, 31), (10, 14), (11, 12), (12, 3))
    V(["pi"], ["pe"], "ts", T.pi[:, 9:10], T.pi[:, 1:2], 15, None, A.bitwise_and)
    for u, m in bits[:5]:
        V(["pi"], ["pb%d" % u], "ts", T.pi[:, u:u + 1], T.pi[:, 0:1], m, None, A.bitwise_and)
    V(["pe"], ["e9"], "ts", col(E9), T.pi[:, 9:10], 9.0, None, A.min)
    for u, m in bits[5:]:
        V(["pi"], ["pb%d" % u], "ts", T.pi[:, u:u + 1], T.pi[:, 0:1], m, None, A.bitwise_and)
    V(["jf", "e9"], ["tw"], "ts", T.cst[:, 32:41], T.jf[:, 0:9], col(E9), 1.0, A.is_lt, A.add)
    V(["pe"] + ["pb%d" % u for u, _ in bits], ["cf"], "cp", T.cst[:, 0:11], T.pi[:, 2:13])
    V(["ui"], ["ul"], "cp", T.ul[:], T.ui[:])
    V(["tw"], ["pwc"], "rd", col(PW), T.cst[:, 32:41], AxisListType.X, A.mult)
    V(["e9"], ["oa"], "ts", col(OA), col(E9), 9.0, 1512.0, A.is_equal, A.mult)
    V(["cf"], ["ob"], "ts", col(OB), col(XX), 0.0, -3000.0, A.is_equal, A.mult)
    V(["cf"], ["oc"], "ts", col(OC), col(XX), 1.0, -1000.0, A.is_equal, A.mult)
    V(["ut"], ["uq"], "qz", T.uq[:], T.us[:], T.ut[:])
    V(["oa", "ob", "oc"], ["off"], "ts", col(OFF), col(OA), col(OB), col(OC), A.add, A.add)
    V(["uq", "ul"], ["uq2"], "cp", T.uq2[:].bitcast(dt.uint32), T.uq[:].bitcast(dt.uint32).indirect(T.ul[:]))
    for i in range(2):
        op("p", ["ones"], ["et%d" % i], "as", T.et[:, 528 * i:528 * i + 516], T.ones[:], [[-1, 516]], A.is_equal, 0.0, 2 + i, 4)
    for name, out, n, v in (("kf", K(KF), 32, -up), ("kb", K(KB), 32, dn), ("s14f", slot(0, 14), 32, BETA * LK), ("s14b", slot(1, 14), 32, -BETA * LK),
                            ("s1f", slot(0, 1), 32, 0.0), ("s2f", slot(0, 2), 32, 0.0), ("pz", T.pw[:, 0:4 * PL:PL], 4, 0.0),
                            ("tabv2", T.tab[:, TAB - 1:TAB], 1, ZV), ("s0", T.c2[:, 0:2 * C:16], 64, BIG), ("s15", T.c2[:, 15:2 * C:16], 64, 0.0)):
        lin(["ones"], [name], out, T.ones[:, 0:n], 0.0, v)
    act(["e9"], ["ra"], col(RA), col(E9), AF.Relu, 1.0, -7.0)
    act(["e9"], ["rb8"], col(RB), col(E9), AF.Relu, 1.0, -8.0)
    act(["ra"], ["in1"], col(IN1), col(RA), AF.Relu, -128.0, 128.0)
    act(["rb8"], ["inc"], col(INC), col(RB), AF.Relu, -256.0, 256.0)
    for u in range(5):
        lin(["cf", "kf"], ["sf%d" % u], slot(0, 4 + u), K(KF), col(u), BETA * S)
    lin(["pwc"], ["c1"], col(C1), col(PW), -0.5, 0.5 - 256)
    lin(["pwc"], ["mg"], col(MG), col(PW), 1.5 * 2.0 ** 23, 0.0)
    op("a", ["uq", "ul"], ["us2"], "ac", T.us2[:], T.us[:].indirect(T.ul[:]), AF.Copy)
    lin(["jf", "c1"], ["jh", "jq"], T.jh[:], T.jf[:], 1.0, col(C1))
    lin(["jh", "jq", "mg"], ["jr"], T.jr[:], T.jh[:], 1.0, col(MG))

    def high_steps():
        lin(["jj"], ["s3f"], slot(0, 3), K(JF), up, -256.0 - BETA * (CC - DP))
        for u in range(5, 9):
            lin(["kg%d" % u], ["sf%d" % u], slot(0, 4 + u), KG(u), -up, 257.0 - BETA * (8 * S + DP) if u == 8 else BETA * S)
        for u in range(5):
            lin(["cf", "kb"], ["sb%d" % u], slot(1, 4 + u), K(KB), col(u), BETA * S - dn * (1 << u))
        for u in range(5, 9):
            lin(["kg%d" % u], ["sb%d" % u], slot(1, 4 + u), KG(u), dn,
                (257.0 - BETA * (8 * S + 1024) if u == 8 else BETA * S) - dn * (1 << u))
        lin(["jj"], ["s3b"], slot(1, 3), K(JF), -dn, 511 * dn - 256.0 - BETA * (CC - 1025))

    cn = [["s0", "s15", "s1f", "s2f", "s3f", "s14f", "d13f"] + ["sf%d" % u for u in range(9)],
          ["s0", "s15", "s3b", "s14b", "d13b", "d1b", "d2b"] + ["sb%d" % u for u in range(9)]]
    for h, (c0, c1) in enumerate(PARTS[0]):
        V(["xt%d" % h], ["a0h%d" % h], "qz", T.aq0[:, c0:c1], T.as0[:, c0:c1], T.xt[:, 4 * c0:4 * c1])
    V(["jr", "mg", "off"], ["flo0"], "ts", T.flo[:, 0:128], T.jr[:], col(MG), col(OFF), A.subtract, A.add)
    V(["cf", "jw"], ["jj"], "ts", K(JF), K(JW), col(AA), None, A.add)
    V(["flo0", "in1"], ["flo1"], "ts", T.flo[:, 128:256], T.flo[:, 0:128], col(IN1), None, A.add)
    V(["flo0", "inc"], ["flo2"], "ts", T.flo[:, 256:384], T.flo[:, 0:128], col(INC), None, A.add)
    V(["flo0", "in1", "inc"], ["flo3"], "ts", T.flo[:, 384:C], T.flo[:, 0:128], col(IN1), col(INC), A.add, A.add)

    def late_constants():
        act(["cf"], ["ya"], col(YA), col(AA), AF.Abs, 1.0, -15.5)
        act(["jf"], ["jq"], T.jh[:, 0:32], T.jf[:, 0:32], AF.Abs, 1.0, -15.5)
        act(["jpb", "cf"], ["wd1"], T.wd[:, 32:64], T.jp[:], AF.Abs, -1.0, col(QA))
        act(["jq", "ya"], ["wd0"], T.wd[:, 0:32], T.jh[:, 0:32], AF.Abs, -1.0, col(YA))
        lin(["cf"], ["m1"], col(M1), col(4), 1.0 / 16, 0.0)
        act(["wd0", "wd1"], ["wb"], T.wb[:, 0:63], T.wd[:, 1:64], AF.Relu, -FREE, FREE)
        act(["wd0", "wd1"], ["wa"], T.wa[:], T.wd[:], AF.Relu, -HOLD, HOLD)
        lin(["cf"], ["n2"], col(Y0), col(4), -2.0, 0.0)
        lin(["ones", "wb"], ["wc"], T.wb[:, 35:64:4], T.ones[:, 0:8], 0.0, FREE)
        lin(["ones", "wb"], ["we"], T.wb[:, 15:32:16], T.ones[:, 0:2], 0.0, FREE)
        lin(["cf", "m1"], ["x2"], col(X2), col(EV), 1.0, col(M1))
        act(["cf", "n2"], ["x1"], col(X1), col(0), AF.Abs, 32.0, col(Y0))
        lin(["cf"], ["qc"], col(QC), col(QB), float(PL), HOLD - FREE - ZV)
        lin(["x1", "x2"], ["pC"], col(PC), col(X1), 1.0, col(X2))

    def masks(c):
        r = T.rank_of(c)
        ds = [T.cores[i] for i in (r - 1, r + 1) if 0 <= i < n_ranks]
        used, out = set(), {}
        width = min(len(topo.engines(a, b)) for a, b in zip(T.cores, T.cores[1:]))
        for d in sorted(ds, key=lambda d: len(topo.engines(c, d))):
            free = [e for e in topo.engines(c, d) if e not in used]
            if len(ds) > 1 and not used:
                other = [x for x in ds if x != d][0]
                if not set(topo.engines(c, other)) - set(free):
                    free = free[:len(free) // 2]
            free = free[:min(width, 1 << (len(free).bit_length() - 1))]
            used.update(free)
            out[d] = free
        return out

    mine = masks(core)
    arrive = sum(2 * len(masks(d)[core]) for d, _ in nb)
    sent = [0]
    plane = lambda b: T.pw[:, b * PL:(b + 1) * PL]
    bank = lambda b, n: T.psp[:, 512 * b:512 * b + n]
    pls = lambda b: ["pw%d" % b, "pz", "pd%d" % b]
    pall = ["pw%d" % b for b in range(4)] + ["pz"] + ["pd%d" % b for b in range(4)]
    tabs = ["tabc"] + ["tabv%d" % i for i in range(4)]

    def out_bank(h, n):
        return ((T.pss[:, 0:n], "pss0"), (T.pss[:, 512:512 + n], "pss1"), (T.psy[:, 0:n], "psy0"))[h]

    def scores(t, h):
        c0, c1 = PARTS[t][h]
        ps, name = out_bank(h, c1 - c0)
        op("t", ["a%dh%d" % (t, h), "uq2", "us2"], [name], "mm", ps, T.uq2[:], T.us2[:],
           T["aq%d" % t][:, c0:c1], T["as%d" % t][:, c0:c1], True, True)

    def p_copy(b):
        op("a", [], ["psp%d" % b, "pw%d" % b], "ac", T.pw[:, b * PL + P0:b * PL + P0 + C], bank(b, C), AF.Copy, scale=0.0625)
        dma("s", ["pw%d" % b], ["pc%d" % b], T.pc[:, b * C:(b + 1) * C], T.pw[:, b * PL + P0:b * PL + P0 + C])

    def spread(name, i):
        n = 32 << i
        out, src = (T.wr[:, C - 2 * n:C - n], T.wr[:, C - n:C]) if name == "wrp" else (T.wr[:, C + n:C + 2 * n], T.wr[:, C:C + n])
        op("a", ["%s%d" % (name, i)], ["%s%d" % (name, i + 1)], "ac", out, src, AF.Copy)

    def unit(b):
        e0 = 528 * (b % 2) + 2 - b // 2 * 2
        V(["et%d" % (b % 2)], ["eq%d" % b], "qz", T.eq[:, 128 * b:128 * b + 128], T.es[:, 128 * b:128 * b + 128], T.et[:, e0:e0 + 512])

    def partners(q, name, c0, c1):
        src = T.tab[:].indirect(T.ow1[:, c0:c1])
        if q == "a":
            op("a", tabs + ["ow1"], [name], "ac", T.gp[:, 16 * c0:16 * c1], src, AF.Copy)
        else:
            V(tabs + ["ow1"], [name], "cp", T.gp[:, 16 * c0:16 * c1], src)

    for h in range(len(PARTS[0])):
        scores(0, h)
    for t in range(R):
        aq, asc = T["aq%d" % t], T["as%d" % t]
        ah = ["a%dh%d" % (t, h) for h in range(len(PARTS[t]))]
        mq, ms_, lq, ls = T["mq%d" % t], T["ms%d" % t], T["lq%d" % t], T["ls%d" % t]
        for b in range(4):
            op("t", ah + ["wq", "wsc"], ["psp%d" % b], "mm", bank(b, C),
               T.wq[:, 128 * b:128 * b + 128], T.wsc[:, 128 * b:128 * b + 128], aq[:], asc[:], True, True)
        for h, (c0, c1) in enumerate(PARTS[t]):
            ps, name = out_bank(h, c1 - c0)
            op("a", [], [name, "sg%d" % h], "ac", T.sg[:, c0:c1], ps, AF.Sign, bias=TINY)
        if t == 0:
            high_steps()
        cm = PARTS[t][0][1]
        sg = ["sg0", "sg1", "sg2"] + ["flo%d" % i for i in range(4)]
        back = lambda: V(sg, ["yb"], "sc", T.y2[:, 2 * C - 1:C - 1:-1], T.flo[:], T.sg[:, ::-1], H0, A.max, A.subtract)
        if t == 0:
            V(sg, ["yf0", "yf1"], "sc", T.y2[:, 0:C], T.flo[:], T.sg[:], H0, A.max, A.add)
            back()
            V(["yf0", "yf1"], ["tf0", "tf1"], "tr", T.t2[:, 0:C], T.y2[:, 0:C])
        else:
            V(["sg0"], ["yf0"], "sc", T.y2[:, 0:cm], T.flo[:, 0:cm], T.sg[:, 0:cm], H0, A.max, A.add)
            V(["yf0"], ["ini"], "cp", col(INI), T.y2[:, cm - 1:cm])
            V(["yf0"], ["tf0"], "tr", T.t2[:, 0:cm], T.y2[:, 0:cm])
            V(["sg1", "ini"], ["yf1"], "sc", T.y2[:, cm:C], T.flo[:, cm:C], T.sg[:, cm:C], col(INI), A.max, A.add)
            back()
            V(["yf1"], ["tf1"], "tr", T.t2[:, cm:C], T.y2[:, cm:C])
        V(["yb"], ["tb"], "tr", T.t2[:, C:2 * C], T.y2[:, C:2 * C])
        tf = ["tf0", "tf1"]
        hf, hb = T.t2[:, 0:C:16], T.t2[:, C:2 * C:16]
        lin(tf, ["d13f"], slot(0, 13), hf, -BETA, BETA * H0)
        lin(tf, ["d13b"], slot(1, 13), hf, -BETA, BETA * H0)
        lin(tf, ["d2b"], slot(1, 2), hf, BETA, -BETA * H0)
        lin(["tb"], ["d1b"], slot(1, 1), hb, BETA, -BETA * H0)
        if t == 0:
            late_constants()
        for b in range(4 if t else 1):
            p_copy(b)
        V(tf + cn[0], ["rf"], "sc", T.r2[:, 0:C - 1], T.t2[:, 0:C - 1], T.c2[:, 0:C - 1], BIG, A.min, A.add)
        V(["tb"] + cn[1], ["rb"], "sc", T.r2[:, C:2 * C - 1], T.t2[:, C:2 * C - 1], T.c2[:, C:2 * C - 1], BIG, A.min, A.add)
        least = lambda name, out, c0, step: V(["rf", "rb"], [name], "tt", out, T.r2[:, c0:C:step], T.r2[:, C + c0:2 * C:step], A.min)
        if t == 0:
            V(["wa", "wb", "wc", "we"], ["wrm0", "wrp0"], "tt", T.wr[:, C - 32:C + 32], T.wb[:], T.wa[:], A.subtract)
        least("key0", T.key[:, 0:16], 13, 32)
        least("key2", T.key[:, 16:32], 29, 32)
        least("key1", T.key[:, 32:64], 14, 16)
        V(["key0", "key2"], ["kt0"], "tr", T.kt[:, 0:32], T.key[:, 0:32])
        V(["key1"], ["kt1"], "tr", T.kt[:, 32:64], T.key[:, 32:64])
        if t == 0:
            V(["pC"], ["prm"], "cp", T.prm[:, 0:1], col(PC))
        V(["kt0"], ["ow0"], "ts", T.ow[:], T.kt[:, 0:32], -1.0 / BETA, None, A.mult)
        V(["kt1"], ["rot1"], "tr", T.key[:, 64:96], T.kt[:, 63:31:-1])
        if t == 0:
            V(["pC"], ["prn"], "ts", T.prm[:, 1:2], col(PC), 16.0, None, A.add)
            for b in range(1, 4):
                p_copy(b)
                if b < 3:
                    spread("wrm", b - 1)
                    spread("wrp", b - 1)
        V(["ow0", "val"], tabs, "cp", T.tab[:].indirect(T.ow[:]), T.val[:])
        V(["key1", "rot1", "prm", "prn"], ["ow1"], "ts", T.ow1[:], T.key[:, 32:96].indirect(T.prm[:]), -1.0 / BETA, float(TAB - 1), A.mult, A.min)
        if GA[t]:
            partners("a", "gpa", 0, GA[t])
        V(tabs + ["wrm2"], ["mw"], "sc", T.mw[:], T.tab[:, CC - TM:CC + TM], T.wr[:, C:C + 128], FREE, A.min, A.add)
        V(["mw", "qc"], ["ml"], "ts", T.ml[:], T.mw[:, 3:128:4], col(QC), None, A.add)
        op("a", ["ml"] + pall, ["mta"], "ac", T.mt[:, 16 * MV:512], T.pw[:].indirect(T.ml[:, MV:32]), AF.Copy)
        V(["ml"] + pall, ["mtv"], "cp", T.mt[:, 0:16 * MV], T.pw[:].indirect(T.ml[:, 0:MV]))
        V(["mta", "mtv"], ["mq%d" % t], "qz", mq[:], ms_[:], T.mt[:])
        order("p", ["mq%d" % t], [])
        for src, dst, cast in ((mq, lq, bytes_of), (ms_, ls, lambda v: v)):
            trs = []
            for d, c0 in nb:
                rid, pid, _ = topo.addr(d)
                trs.append(RemoteDMATransfer(dst_ids=[DstId(rid=rid, pnc=pid)], dma_engine_mask=sum(1 << e for e in mine[d]),
                                             remote_sem=T.sem["arr%d" % t], src=cast(src[:, c0:c0 + TM]), dst=cast(dst[:, c0:c0 + TM])))
                sent[0] += len(mine[d])
            g.remote_dma_fused(trs, local_sem=T.sem.sent)
        if edge:
            z0 = nb[0][1]
            dma("s", ["mq%d" % t], ["zl%d" % t], bytes_of(lq[:, z0:z0 + TM]), bytes_of(mq[:, z0:z0 + TM]))
            dma("s", ["mq%d" % t], ["zm%d" % t], ls[:, z0:z0 + TM], ms_[:, z0:z0 + TM])
        if t == 0:
            spread("wrp", 2)
        partners("a", "gpb", GA[t], GB[t])
        if t == 0:
            spread("wrp", 3)
        partners("v", "gpc", GB[t], 32)
        if t == 0:
            lin(["cf", "jc"], ["j16"], K(J16), K(JC), 1.0, col(XX))
            clear_lists()
            unit(0)
            unit(2)
        V(["gpa", "gpb", "gpc", "wrp4"], ["gw"], "sc", T.gw[:], T.gp[:], T.wr[:, 0:C], FREE, A.min, A.add)
        if t == 0:
            unit(3)
        V(["gw"], ["lst"], "ts", T.lst[:], T.gw[:, 15:C:16], HOLD - FREE - ZV, None, A.add)
        V(["gw"], ["l2"], "ts", K(L2), T.gw[:, 15:C:16], 2.0, 2 * (HOLD - FREE) + X0 - 2 * AV, A.mult, A.add)
        V(["lst", "pc0"] + pls(0), ["x00"], "tt", T.x0[:, P0:P0 + C], plane(0).indirect(T.lst[:]), T.pc[:, 0:C], A.add)
        V(["l2", "j16"], ["l3"], "tt", K(L3), K(L2), K(J16), A.max)
        V(["lst", "pc1"] + pls(1), ["x01"], "tt", T.x0[:, XL + P0:XL + P0 + C], plane(1).indirect(T.lst[:]), T.pc[:, C:2 * C], A.add)
        V(["l3"], ["lst2"], "cp", T.lst2[:], K(L3))
        if t == 0:
            unit(1)
            V(["vt"], ["vq"], "qz", T.vq[:], T.vs[:], T.vt[:])
        order("t", ["zl%d" % t, "zm%d" % t], [])
        wait("t", "arr%d" % t, arrive)
        for b in (0, 3, 1, 2):
            op("t", ["eq%d" % b], ["psp%d" % b], "mm", bank(b, 128),
               T.eq[:, 128 * b:128 * b + 128], T.es[:, 128 * b:128 * b + 128], lq[:], ls[:], True, True)
        for b in (3, 2):
            op("a", [], ["psp%d" % b, "pd%d" % b], "ac", T.pw[:, b * PL + D0:(b + 1) * PL:4], bank(b, 128), AF.Copy)
        for b in (0, 1):
            V(["mta", "mtv"], ["psp%d" % b, "fx%d" % b], "tt", T.x0[:, b * XL + X0:b * XL + X0 + 8 * 127 + 1:8],
              T.mt[:, 508 + b::-4], bank(b, 128), A.add)
        nq, ns = T["aq%d" % (t + 1)], T["as%d" % (t + 1)]
        parts = PARTS[t + 1]
        for h, (c0, c1) in enumerate(parts):
            for b in (0, 1):
                op("a", ["lst2", "x0%d" % b, "fx%d" % b], ["xn%d_%d" % (h, b)], "ac", T.xn[:, 4 * c0 + b:4 * c1:4],
                   T.x0[:, b * XL:(b + 1) * XL].indirect(T.lst2[:, c0 // 16:c1 // 16]), AF.Copy)

        def add(b, h0, h1):
            c0, c1 = parts[h0][0], parts[h1][1]
            V(["lst", "pc%d" % b] + pls(b), ["xn%d_%d" % (h, b) for h in range(h0, h1 + 1)], "tt", T.xn[:, 4 * c0 + b:4 * c1:4],
              plane(b).indirect(T.lst[:, c0 // 16:c1 // 16]), T.pc[:, b * C + c0:b * C + c1], A.add)

        for h, (c0, c1) in enumerate(parts):
            for run in ADDS[t][h]:
                add(*run)
            names = ["a%dh%d" % (t + 1, h)]
            V(["xn%d_%d" % (h, b) for b in range(4)], names, "qz", nq[:, c0:c1], ns[:, c0:c1], T.xn[:, 4 * c0:4 * c1])
            if t < R - 1:
                scores(t + 1, h)
                continue
            ps, name = out_bank(h, c1 - c0)
            dma("s", names, [], T.oc[:, 4 * c0:4 * c1], bytes_of(nq[:, c0:c1]))
            op("t", names + ["vq"], [name], "mm", ps, T.vq[:], T.vs[:], nq[:, c0:c1], ns[:, c0:c1], True, True)
            if h + 1 < len(parts):
                op("a", [], [name, "y%d" % h], "ac", T.ysb[:, c0:c1], ps, AF.Copy)
            else:
                V([], [name, "y%d" % h], "cp", T.ysb[:, c0:c1], ps)
                for k in range(4):
                    dma("s", ["a%dh%d" % (R, i) for i in range(len(parts))], [], T.osc[4 * k:4 * k + 4, :], T["as%d" % R][32 * k:32 * k + 4, :])
            dma("a", ["y%d" % h], [], T.y[:, c0:c1], T.ysb[:, c0:c1])
    for q in count:
        wait("s", q, count[q])
    for i in range(ndma[0]):
        if not any("d%d" % i in seen[q] for q in seen):
            wait("s", "d%d" % i, 16)
    g.wait_ge(T.sem.sent, sent[0])
